import numpy as np
import ml_dtypes


def mxq(x, axis, fmt="e4m3"):
    dtype, down = {"e4m3": (ml_dtypes.float8_e4m3fn, 7), "e5m2": (ml_dtypes.float8_e5m2, 14)}[fmt]
    v = np.moveaxis(np.asarray(x, np.float32).astype(ml_dtypes.bfloat16).astype(np.float64), axis, -1)
    blocks = v.reshape(v.shape[:-1] + (-1, 32))
    amax = np.abs(blocks).max(-1, keepdims=True)
    byte = np.maximum(np.where(amax > 0, np.frexp(amax)[1] - 1 + 127, 0) - down, 1)
    scale = np.exp2(byte - 127.0)
    codes = (blocks / scale).astype(np.float32).astype(dtype).astype(np.float64)
    return np.moveaxis((codes * scale).reshape(v.shape), -1, axis)


WIDE = False


def mx_kscale(k):
    if not WIDE:
        return np.ones(k)
    levels = np.array([10, -10, 5, -5, 0])
    if k % 512:
        return np.exp2(np.random.permutation(np.resize(levels, k // 32))).repeat(32)
    a = np.empty((k // 512, 16))
    for p in range(k // 512):
        a[p, :8] = np.random.permutation(np.resize(levels, 8))
        for g in range(8):
            far = levels[np.abs(levels - a[p, g]) >= 10]
            a[p, g + 8] = far[np.random.randint(len(far))]
    return np.exp2(a.ravel()).repeat(32)


BF16 = ml_dtypes.bfloat16


def bf(x):
    return np.asarray(x, np.float32).astype(BF16)


def f64(x):
    return np.asarray(x).astype(np.float64)

E4M3FN = np.array([(-1.0 if i & 128 else 1.0) * ((1.0 + (i & 7) / 8.0) * 2.0 ** (((i >> 3) & 15) - 7) if i & 120 else (i & 7) * 2.0 ** -9) for i in range(256)])


def e4m3fn_bytes(y):
    return np.clip(np.asarray(y, np.float64), -448.0, 448.0).astype(np.float32).astype(ml_dtypes.float8_e4m3fn).view(np.uint8)


def e4m3fn_values(b):
    return E4M3FN[b]


Z, V, R, B = 1024, 2048, 1536, 512

FP8_MAX = 448.0
DEPTH = 0.6


def setup_inputs():
    s = mx_kscale(V)
    t = mx_kscale(R)
    footprint = np.random.uniform(0.5, 1.5, (V, 1))
    S = np.random.standard_normal((V, R)) * footprint * DEPTH / np.sqrt(V) * s[:, None]
    S_scale = (np.abs(S).max(axis=1, keepdims=True) / FP8_MAX).astype(np.float32)
    S_bytes = e4m3fn_bytes(S / f64(S_scale))
    F = np.random.standard_normal((Z, V)) / s
    i0 = np.random.uniform(0.5, 1.5, R) * t
    D = np.random.standard_normal((R, B)) / np.sqrt(R) / t[:, None]
    return {"F": bf(F), "S_bytes": S_bytes, "S_scale": S_scale, "i0": bf(i0), "D": bf(D)}


def reference(F, S_bytes, S_scale, i0, D):
    S = e4m3fn_values(S_bytes) * np.repeat(f64(S_scale), R, axis=1)
    p = mxq(f64(F), 1, "e4m3") @ mxq(S, 0, "e4m3")
    h = f64(i0) * np.exp(-p)
    y = mxq(h, 1, "e4m3") @ mxq(f64(D), 0, "e4m3")
    return y

@@ -1,0 +1,440 @@
+from contextlib import ExitStack
+
+import concourse.mybir as mybir
+from concourse.masks import make_identity
+
+Z, V, R, B = 1024, 2048, 1536, 512
+FLOPS = 2 * Z * V * R + 2 * Z * R * B
+
+F32 = mybir.dt.float32
+BF16 = mybir.dt.bfloat16
+U32 = mybir.dt.uint32
+U8 = mybir.dt.uint8
+FP8 = mybir.dt.float8_e4m3fn
+FP8X4 = mybir.dt.float8_e4m3fn_x4
+ALU = mybir.AluOpType
+ACT = mybir.ActivationFunctionType
+
+P = 128
+PACK = 4
+KP = 512
+G = V // KP
+C = R // KP
+ZH = 512
+NH = Z // ZH
+
+
+def tile_tomography_forward_transmission_d3_kernel(tc, F, S_bytes, S_scale, i0, D, out):
+    nc = tc.nc
+    with ExitStack() as ctx:
+        keep = ctx.enter_context(tc.tile_pool(name="keep", bufs=1))
+        fraw_pool = ctx.enter_context(tc.tile_pool(name="fraw", bufs=5))
+        grp = ctx.enter_context(tc.tile_pool(name="grp", bufs=4))
+        fpool = ctx.enter_context(tc.tile_pool(name="fpool", bufs=3))
+        big = ctx.enter_context(tc.tile_pool(name="big", bufs=3))
+        sq = ctx.enter_context(tc.tile_pool(name="sq", bufs=8))
+        hp = ctx.enter_context(tc.tile_pool(name="hp", bufs=4))
+        hq = ctx.enter_context(tc.tile_pool(name="hq", bufs=1))
+        psum = ctx.enter_context(tc.psum_pool(name="psum", bufs=8))
+        ctx.enter_context(tc.manual_schedule())
+
+        scale = keep.tile([P, G, PACK], F32, name="scale")
+        i0_t = keep.tile([P, C, PACK], BF16, name="i0_t")
+        nc.scalar.dma_start(out=scale[:], in_=S_scale.rearrange("(g p t) o -> p g (t o)", p=P, t=PACK))
+        nc.scalar.dma_start(out=i0_t[:], in_=i0.rearrange("(c p t) -> p c t", p=P, t=PACK))
+        s_view = S_bytes.rearrange("(g p t) n -> g p t n", p=P, t=PACK)
+        sb_a, sb_b = [], []
+        for g in range(G):
+            a = keep.tile([P, PACK, KP], U8, name="s_bytes_a%d" % g)
+            b = keep.tile([P, PACK, 2 * KP], U8, name="s_bytes_b%d" % g)
+            sb_a.append(a)
+            sb_b.append(b)
+        f_raw = {}
+        d_raw = []
+        for c in range(C):
+            dr = keep.tile([P, PACK, B], BF16, name="d_raw%d" % c)
+            d_raw.append(dr)
+
+        def load_f(z):
+            fr = fraw_pool.tile([P, V], BF16, name="f_raw")
+            f_raw[z] = fr
+            nc.sync.dma_start(out=fr[:], in_=F[P * z : P * (z + 1), :])
+
+        d_view = D.rearrange("(c p t) b -> c p t b", p=P, t=PACK)
+
+        def load_sa(g):
+            nc.sync.dma_start(out=sb_a[g][:], in_=s_view[g][:, :, 0:KP])
+
+        def load_sb(g):
+            nc.sync.dma_start(out=sb_b[g][:], in_=s_view[g][:, :, KP:R])
+
+        def load_d(c):
+            nc.sync.dma_start(out=d_raw[c][:], in_=d_view[c])
+
+
+        i0_flat = i0_t[:].rearrange("p c t -> p (c t)")
+        ident = keep.tile([P, P], F32, name="ident")
+        make_identity(nc, ident[:])
+
+        mag = keep.tile([P, C * PACK], F32, name="mag")
+        fac = keep.tile([P, 2, C * PACK], F32, name="fac")
+        inv = keep.tile([P, C * PACK], F32, name="inv")
+        lnf = keep.tile([P, 2, C * PACK], F32, name="lnf")
+        ln_i0 = keep.tile([P, C * PACK], F32, name="ln_i0")
+        sgn = keep.tile([P, C * PACK], F32, name="sgn")
+
+        def i0_step(k):
+            if k == 0:
+                nc.vector.tensor_scalar(out=sgn[:], in0=i0_flat, scalar1=0.0, scalar2=2.0, op0=ALU.is_ge, op1=ALU.mult)
+            elif k == 1:
+                nc.vector.tensor_scalar(out=sgn[:], in0=sgn[:], scalar1=-1.0, scalar2=None, op0=ALU.add)
+            elif k == 2:
+                nc.vector.tensor_tensor(out=mag[:], in0=i0_flat, in1=sgn[:], op=ALU.mult)
+            elif k == 3:
+                nc.vector.tensor_scalar(out=mag[:], in0=mag[:], scalar1=2.0**-126, scalar2=None, op0=ALU.max)
+            elif k == 4:
+                nc.vector.tensor_scalar(out=fac[:, 0, :], in0=mag[:], scalar1=2.0**-63, scalar2=2.0**64, op0=ALU.max, op1=ALU.min)
+            elif k == 5:
+                nc.vector.reciprocal(out=inv[:], in_=fac[:, 0, :])
+            elif k == 6:
+                nc.vector.tensor_tensor(out=fac[:, 1, :], in0=mag[:], in1=inv[:], op=ALU.mult)
+
+        unit = keep.tile([P, 1], F32, name="unit")
+        ln_unit = keep.tile([P, 1], F32, name="ln_unit")
+
+        def load_ln_table():
+            nc.vector.memset(unit[:], 1.0)
+            nc.scalar.activation(out=ln_unit[:], in_=unit[:], func=ACT.Ln)
+
+        def log_i0():
+            nc.scalar.activation(out=lnf[:], in_=fac[:], func=ACT.Ln)
+
+        def add_logs():
+            nc.vector.tensor_tensor(out=ln_i0[:], in0=lnf[:, 0, :], in1=lnf[:, 1, :], op=ALU.add)
+
+        s_wide = {}
+
+        def new_wide(c):
+            wide_tile = big.tile([P, PACK, G * KP], BF16, name="big", align_bytes=64)
+            s_wide[c] = wide_tile
+        s_grp, s_codes, s_scales = {}, {}, {}
+
+        def widen(c, g, j, eng):
+            src = sb_a[g][:, j, :] if c == 0 else sb_b[g][:, j, KP * (c - 1) : KP * c]
+            dst = s_wide[c][:, j, KP * g : KP * (g + 1)]
+            if eng == "v":
+                nc.vector.tensor_scalar(out=dst, in0=src.bitcast(FP8), scalar1=scale[:, g, j : j + 1], scalar2=None, op0=ALU.mult)
+            else:
+                nc.scalar.activation(out=dst, in_=src.bitcast(FP8), func=ACT.Copy, scale=scale[:, g, j : j + 1])
+
+        def s_inter(c, t):
+            gt = grp.tile([P, 4 * KP], BF16, name="s_grp", align_bytes=64)
+            s_grp[c, t] = gt
+            src = s_wide[c][:].rearrange("p j (q i t) -> p t q j i", i=4, t=4)
+            dst = gt[:].rearrange("p (q i j) -> p q j i", i=4, j=4)
+            nc.vector.tensor_copy(out=dst, in_=src[:, t])
+
+        def s_quant(c, t):
+            co = sq.tile([P, KP], U32, name="s_codes", align_bytes=64)
+            sc = sq.tile([P, KP], U8, name="s_scales", align_bytes=64)
+            s_codes[c, t], s_scales[c, t] = co, sc
+            nc.vector.quantize_mx(out=co[:].bitcast(FP8X4), scales=sc[:], in_=s_grp[c, t][:])
+
+        f_grp = {}
+
+        def new_f_grp(q):
+            f_grp_tile = fpool.tile([P, G, ZH], F32, name="f_grp", align_bytes=64)
+            f_grp[q] = f_grp_tile
+        f_codes = [keep.tile([P, G, ZH], U32, name="f_codes%d" % h, align_bytes=64) for h in range(NH)]
+        f_scales = [keep.tile([P, G, ZH], U8, name="f_scales%d" % h, align_bytes=64) for h in range(NH)]
+
+        def f_turn(z):
+            words = f_raw[z][:].bitcast(F32)
+            q, zz = divmod(z, 2)
+            if zz == 0:
+                new_f_grp(q)
+            for gp in range(2):
+                bank = psum.tile([P, 512], F32, name="bank")
+                for k in range(2):
+                    for u in range(2):
+                        g = 2 * gp + k
+                        nc.tensor.transpose(
+                            bank[:, (2 * k + u) * P : (2 * k + u + 1) * P],
+                            words[:, 256 * g + u : 256 * (g + 1) : 2],
+                            ident[:],
+                        )
+                dst = f_grp[q][:, 2 * gp : 2 * gp + 2, 2 * P * zz : 2 * P * (zz + 1)]
+                nc.scalar.copy(
+                    out=dst.rearrange("p g (r u) -> p g r u", u=2),
+                    in_=bank[:].rearrange("p (g u r) -> p g r u", g=2, u=2),
+                )
+
+        def f_quant(q, g):
+            h, k = divmod(q, 2)
+            nc.vector.quantize_mx(
+                out=f_codes[h][:, g, 256 * k : 256 * (k + 1)].bitcast(FP8X4),
+                scales=f_scales[h][:, g, 256 * k : 256 * (k + 1)],
+                in_=f_grp[q][:, g, :].bitcast(BF16),
+            )
+
+        h_planes = {}
+        banks = {}
+
+        def project(c, t, h, half=None):
+            if (c, t, h) not in banks:
+                bank_tile = psum.tile([P, 512], F32, name="bank")
+                banks[c, t, h] = bank_tile
+            bank = banks[c, t, h]
+            zs = slice(0, ZH) if half is None else slice(256 * half, 256 * (half + 1))
+            for g in range(G):
+                cols = slice(P * g, P * (g + 1))
+                nc.tensor.matmul_mx(
+                    out=bank[:, zs],
+                    lhsT=s_codes[c, t][:, cols].bitcast(FP8X4),
+                    lhsT_scale=s_scales[c, t][:, cols],
+                    rhs=f_codes[h][:, g, zs].bitcast(FP8X4),
+                    rhs_scale=f_scales[h][:, g, zs],
+                    start=(g == 0),
+                    stop=(g == G - 1),
+                )
+
+        def attenuate(c, t, h):
+            if (c, h) not in h_planes:
+                h_planes[c, h] = hp.tile([P, PACK, ZH], BF16, name="h_plane", align_bytes=64)
+            nc.scalar.activation(
+                out=h_planes[c, h][:, t, :],
+                in_=banks[c, t, h][:],
+                func=ACT.Exp,
+                bias=ln_i0[:, PACK * c + t : PACK * c + t + 1],
+                scale=-1.0,
+            )
+
+        h_grp = {}
+        h_codes = [hq.tile([P, Z], U32, name="h_codes%d" % c, align_bytes=64) for c in range(C)]
+        h_scales = [hq.tile([P, Z], U8, name="h_scales%d" % c, align_bytes=64) for c in range(C)]
+
+        def h_inter(c, z0, w, eng):
+            gt = grp.tile([P, 4 * 256], BF16, name="h_grp", align_bytes=64)
+            h_grp[c, z0] = gt
+            h, z1 = divmod(z0, ZH)
+            src = h_planes[c, h][:, :, z1 : z1 + w].rearrange("p j (q i) -> p q j i", i=4)
+            dst = gt[:, 0 : 4 * w].rearrange("p (q i j) -> p q j i", i=4, j=4)
+            if eng == "v":
+                nc.vector.tensor_copy(out=dst, in_=src)
+            else:
+                nc.scalar.copy(out=dst, in_=src)
+
+        def h_quant(c, z0, w):
+            nc.vector.quantize_mx(
+                out=h_codes[c][:, z0 : z0 + w].bitcast(FP8X4), scales=h_scales[c][:, z0 : z0 + w], in_=h_grp[c, z0][:, 0 : 4 * w]
+            )
+
+        d_grp = []
+        d_codes = [keep.tile([P, B], U32, name="d_codes%d" % c, align_bytes=64) for c in range(C)]
+        d_scales = [keep.tile([P, B], U8, name="d_scales%d" % c, align_bytes=64) for c in range(C)]
+
+        def d_sign(c):
+            for j in range(PACK):
+                nc.vector.tensor_scalar(
+                    out=d_raw[c][:, j, :], in0=d_raw[c][:, j, :], scalar1=sgn[:, PACK * c + j : PACK * c + j + 1], scalar2=None, op0=ALU.mult
+                )
+
+        def d_inter(c, eng="v"):
+            if not d_grp:
+                d_grp_tile = big.tile([P, C, PACK * B], BF16, name="big", align_bytes=64)
+                d_grp.append(d_grp_tile)
+            dst = d_grp[0][:, c, :].rearrange("p (q i j) -> p q j i", i=4, j=4)
+            src = d_raw[c][:].rearrange("p j (q i) -> p q j i", i=4)
+            if eng == "v":
+                nc.vector.tensor_copy(out=dst, in_=src)
+            else:
+                nc.scalar.copy(out=dst, in_=src)
+
+        def d_quant(c):
+            nc.vector.quantize_mx(out=d_codes[c][:].bitcast(FP8X4), scales=d_scales[c][:], in_=d_grp[0][:, c, :])
+
+        y_banks = {}
+        y_all = []
+
+        def detect(z, cs):
+            if z not in y_banks:
+                y_banks[z] = psum.tile([P, 512], F32, name="bank")
+            for c in cs:
+                cols = slice(P * z, P * (z + 1))
+                nc.tensor.matmul_mx(
+                    out=y_banks[z][:],
+                    lhsT=h_codes[c][:, cols].bitcast(FP8X4),
+                    lhsT_scale=h_scales[c][:, cols],
+                    rhs=d_codes[c][:].bitcast(FP8X4),
+                    rhs_scale=d_scales[c][:],
+                    start=(c == 0),
+                    stop=(c == C - 1),
+                )
+
+        def store(z, eng):
+            if not y_all:
+                y_tile = big.tile([P, 8, B], F32, name="big", align_bytes=64)
+                y_all.append(y_tile)
+            yt = y_all[0][:, z, :]
+            if eng == "v":
+                nc.vector.tensor_copy(out=yt, in_=y_banks[z][:])
+            else:
+                nc.scalar.copy(out=yt, in_=y_banks[z][:])
+            nc.sync.dma_start(out=out[P * z : P * (z + 1), :], in_=yt)
+
+        load_ln_table()
+        load_sa(0)
+        load_sa(1)
+        load_sa(2)
+        load_sa(3)
+        load_f(0)
+        load_f(1)
+        load_sb(0)
+        load_f(2)
+        load_sb(1)
+        load_f(3)
+        load_sb(2)
+        load_f(4)
+        load_sb(3)
+        load_f(5)
+        new_wide(0)
+        new_wide(1)
+        step = 0
+        for g in range(G):
+            for j in range(PACK):
+                eng = "s" if (g < 2 and j >= 2) or (g == 2 and j == 3) else "v"
+                widen(0, g, j, eng)
+                if eng == "v" and step < 7:
+                    i0_step(step)
+                    step += 1
+        log_i0()
+        for z in range(5):
+            f_turn(z)
+            if z == 0:
+                for k in (6, 7):
+                    load_f(k)
+                for c in range(C):
+                    load_d(c)
+            if z < 4:
+                for j in (2, 3):
+                    widen(1, z, j, "s")
+        s_inter(0, 0)
+        s_inter(0, 1)
+        s_quant(0, 0)
+        s_inter(0, 2)
+        s_quant(0, 1)
+        add_logs()
+        for g in range(G):
+            f_quant(0, g)
+        s_inter(0, 3)
+        s_quant(0, 2)
+        for g in range(4):
+            for j in (0, 1):
+                widen(1, g, j, "v")
+        s_quant(0, 3)
+        for g in range(G):
+            f_quant(1, g)
+        for t in range(2):
+            project(0, t, 0, 0)
+        new_wide(2)
+        for g in range(1):
+            for j in (2, 3):
+                widen(2, g, j, "s")
+        for z in range(5, 8):
+            f_turn(z)
+            if True:
+                for j in (2, 3):
+                    widen(2, z - 5 + 1, j, "s")
+        for g in range(4, G):
+            for j in (0, 1):
+                widen(1, g, j, "v")
+        for t in range(2, 4):
+            project(0, t, 0, 0)
+        for t in range(4):
+            project(0, t, 0, 1)
+        s_inter(1, 0)
+        for g in range(G):
+            f_quant(2, g)
+        s_inter(1, 1)
+        s_quant(1, 0)
+        s_inter(1, 2)
+        s_quant(1, 1)
+        for g in range(G):
+            f_quant(3, g)
+        for t in range(4):
+            attenuate(0, t, 0)
+        for t in range(4):
+            project(0, t, 1, 0)
+        for t in range(4):
+            project(0, t, 1, 1)
+        for t in range(4):
+            attenuate(0, t, 1)
+        for g in range(3, G):
+            for j in (0, 1):
+                widen(2, g, j, "s")
+        for k in range(5, 13):
+            c, t = divmod(k, 4)
+            if 6 < k < 12:
+                s_inter(c, t)
+            c, t = divmod(k - 1, 4)
+            if k > 6:
+                s_quant(c, t)
+            for h in range(NH if c == 1 else 1):
+                project(c, t, h)
+            if c == 1:
+                h_inter(0, 256 * t, 256, "s")
+                for h in range(NH):
+                    attenuate(1, t, h)
+            else:
+                h_quant(0, 256 * t, 256)
+            if k == 7:
+                for cc in range(C):
+                    d_sign(cc)
+                d_inter(0)
+            if k == 7:
+                for g in range(3):
+                    for j in (0, 1):
+                        widen(2, g, j, "v")
+        for t in range(4):
+            project(2, t, 1)
+        for t in range(4):
+            attenuate(2, t, 0)
+        for k in (1, 2, 3):
+            h_inter(1, 256 * k, 256, "s")
+        for t in range(4):
+            attenuate(2, t, 1)
+        for k in (0,):
+            h_inter(1, 256 * k, 256, "v")
+        d_quant(0)
+        d_inter(1)
+        d_inter(2)
+        d_quant(1)
+        d_quant(2)
+        for k in range(2):
+            h_quant(1, 256 * k, 256)
+        for z in range(4):
+            detect(z, (0, 1))
+        h_inter(2, 0, 256, "v")
+        h_inter(2, 256, 256, "v")
+        h_quant(2, 0, 256)
+        for k in ():
+            h_inter(1, 256 * k, 256, "v")
+        h_quant(2, 256, 256)
+        for z in range(4, 8):
+            detect(z, (0,))
+        for z in range(4):
+            detect(z, (2,))
+            store(z, "s")
+        for k in range(2, 4):
+            h_quant(1, 256 * k, 256)
+        for z in range(4, 8):
+            detect(z, (1,))
+        h_inter(2, 512, 256, "v")
+        h_inter(2, 768, 128, "v")
+        h_quant(2, 512, 256)
+        h_inter(2, 896, 128, "v")
+        h_quant(2, 768, 128)
+        h_quant(2, 896, 128)
+        for z in range(4, 8):
+            detect(z, (2,))
+            store(z, "v" if z == 7 else "s")

@@ -14,6 +14,7 @@ FP8 = mybir.dt.float8_e4m3fn
 FP8X4 = mybir.dt.float8_e4m3fn_x4
 ALU = mybir.AluOpType
 ACT = mybir.ActivationFunctionType
+AXIS = mybir.AxisListType
 
 P = 128
 PACK = 4
@@ -22,216 +23,213 @@ G = V // KP
 C = R // KP
 ZH = 512
 NH = Z // ZH
+WIDE_BUFS = 7
+GRP_BUFS = 6
+CODE_BUFS = 12
+PLANE_BUFS = 5
+Y_BUFS = 6
+SI = 4
 
 
 def tile_tomography_forward_transmission_d3_kernel(tc, F, S_bytes, S_scale, i0, D, out):
     nc = tc.nc
     with ExitStack() as ctx:
         keep = ctx.enter_context(tc.tile_pool(name="keep", bufs=1))
-        fraw_pool = ctx.enter_context(tc.tile_pool(name="fraw", bufs=5))
-        grp = ctx.enter_context(tc.tile_pool(name="grp", bufs=4))
-        fpool = ctx.enter_context(tc.tile_pool(name="fpool", bufs=3))
-        big = ctx.enter_context(tc.tile_pool(name="big", bufs=3))
-        sq = ctx.enter_context(tc.tile_pool(name="sq", bufs=8))
-        hp = ctx.enter_context(tc.tile_pool(name="hp", bufs=4))
-        hq = ctx.enter_context(tc.tile_pool(name="hq", bufs=1))
+        ring = ctx.enter_context(tc.tile_pool(name="ring", bufs=1))
         psum = ctx.enter_context(tc.psum_pool(name="psum", bufs=8))
         ctx.enter_context(tc.manual_schedule())
 
         scale = keep.tile([P, G, PACK], F32, name="scale")
         i0_t = keep.tile([P, C, PACK], BF16, name="i0_t")
-        nc.scalar.dma_start(out=scale[:], in_=S_scale.rearrange("(g p t) o -> p g (t o)", p=P, t=PACK))
-        nc.scalar.dma_start(out=i0_t[:], in_=i0.rearrange("(c p t) -> p c t", p=P, t=PACK))
-        s_view = S_bytes.rearrange("(g p t) n -> g p t n", p=P, t=PACK)
-        sb_a, sb_b = [], []
-        for g in range(G):
-            a = keep.tile([P, PACK, KP], U8, name="s_bytes_a%d" % g)
-            b = keep.tile([P, PACK, 2 * KP], U8, name="s_bytes_b%d" % g)
-            sb_a.append(a)
-            sb_b.append(b)
-        f_raw = {}
-        d_raw = []
-        for c in range(C):
-            dr = keep.tile([P, PACK, B], BF16, name="d_raw%d" % c)
-            d_raw.append(dr)
+        s_view = S_bytes.rearrange("(g p j) n -> g p j n", p=P, j=PACK)
+        f_view = F.rearrange("(h z p) (g k) -> h g p z k", p=P, z=4, k=KP)
+        d_view = D.rearrange("(c p j) b -> c p j b", p=P, j=PACK)
+        s_bytes, f_raw, d_raw = {}, {}, {}
 
-        def load_f(z):
-            fr = fraw_pool.tile([P, V], BF16, name="f_raw")
-            f_raw[z] = fr
-            nc.sync.dma_start(out=fr[:], in_=F[P * z : P * (z + 1), :])
+        def load_small():
+            nc.scalar.dma_start(out=scale[:], in_=S_scale.rearrange("(g p j) o -> p g (j o)", p=P, j=PACK))
+            nc.scalar.dma_start(out=i0_t[:], in_=i0.rearrange("(c p j) -> p c j", p=P, j=PACK))
 
-        d_view = D.rearrange("(c p t) b -> c p t b", p=P, t=PACK)
+        def load_s(g, c0, c1):
+            w = KP * (c1 - c0)
+            tile = keep.tile([P, PACK, w + 32], U8, name="s_bytes_%d_%d" % (g, c0))
+            for c in range(c0, c1):
+                s_bytes[c, g] = (tile, KP * (c - c0))
+            nc.sync.dma_start(out=tile[:, :, 0:w], in_=s_view[g][:, :, KP * c0 : KP * c1])
 
-        def load_sa(g):
-            nc.sync.dma_start(out=sb_a[g][:], in_=s_view[g][:, :, 0:KP])
-
-        def load_sb(g):
-            nc.sync.dma_start(out=sb_b[g][:], in_=s_view[g][:, :, KP:R])
+        def load_f(h, g):
+            tile = ring.tile([P, 4, KP], BF16, name="f_raw", bufs=5)
+            f_raw[h, g] = tile
+            nc.sync.dma_start(out=tile[:], in_=f_view[h, g])
 
         def load_d(c):
-            nc.sync.dma_start(out=d_raw[c][:], in_=d_view[c])
+            tile = keep.tile([P, PACK, B], BF16, name="d_raw%d" % c)
+            d_raw[c] = tile
+            nc.sync.dma_start(out=tile[:], in_=d_view[c])
 
-
-        i0_flat = i0_t[:].rearrange("p c t -> p (c t)")
         ident = keep.tile([P, P], F32, name="ident")
-        make_identity(nc, ident[:])
+        ident_bf = keep.tile([P, P], BF16, name="ident_bf")
 
+        def identities():
+            make_identity(nc, ident[:])
+            nc.vector.tensor_copy(out=ident_bf[:], in_=ident[:])
+
+        i0_flat = i0_t[:].rearrange("p c j -> p (c j)")
         mag = keep.tile([P, C * PACK], F32, name="mag")
-        fac = keep.tile([P, 2, C * PACK], F32, name="fac")
-        inv = keep.tile([P, C * PACK], F32, name="inv")
-        lnf = keep.tile([P, 2, C * PACK], F32, name="lnf")
+        fac = keep.tile([P, 3, C * PACK], F32, name="fac")
+        lnf = keep.tile([P, 3, C * PACK], F32, name="lnf")
         ln_i0 = keep.tile([P, C * PACK], F32, name="ln_i0")
+        sgn2 = keep.tile([P, C * PACK], F32, name="sgn2")
         sgn = keep.tile([P, C * PACK], F32, name="sgn")
-
-        def i0_step(k):
-            if k == 0:
-                nc.vector.tensor_scalar(out=sgn[:], in0=i0_flat, scalar1=0.0, scalar2=2.0, op0=ALU.is_ge, op1=ALU.mult)
-            elif k == 1:
-                nc.vector.tensor_scalar(out=sgn[:], in0=sgn[:], scalar1=-1.0, scalar2=None, op0=ALU.add)
-            elif k == 2:
-                nc.vector.tensor_tensor(out=mag[:], in0=i0_flat, in1=sgn[:], op=ALU.mult)
-            elif k == 3:
-                nc.vector.tensor_scalar(out=mag[:], in0=mag[:], scalar1=2.0**-126, scalar2=None, op0=ALU.max)
-            elif k == 4:
-                nc.vector.tensor_scalar(out=fac[:, 0, :], in0=mag[:], scalar1=2.0**-63, scalar2=2.0**64, op0=ALU.max, op1=ALU.min)
-            elif k == 5:
-                nc.vector.reciprocal(out=inv[:], in_=fac[:, 0, :])
-            elif k == 6:
-                nc.vector.tensor_tensor(out=fac[:, 1, :], in0=mag[:], in1=inv[:], op=ALU.mult)
-
         unit = keep.tile([P, 1], F32, name="unit")
-        ln_unit = keep.tile([P, 1], F32, name="ln_unit")
+        unread = keep.tile([P, 2], F32, name="unread")
+        RANGES = ((2.0**-126, 2.0**-63, 2.0**63), (2.0**-63, 2.0**63, 1.0), (2.0**63, 2.0**126, 2.0**-63))
 
-        def load_ln_table():
+        def warm_ln():
             nc.vector.memset(unit[:], 1.0)
-            nc.scalar.activation(out=ln_unit[:], in_=unit[:], func=ACT.Ln)
+            nc.scalar.activation(out=unread[:, 0:1], in_=unit[:], func=ACT.Ln)
 
-        def log_i0():
-            nc.scalar.activation(out=lnf[:], in_=fac[:], func=ACT.Ln)
+        def warm_exp():
+            nc.scalar.activation(out=unread[:, 1:2], in_=unit[:], func=ACT.Exp)
 
-        def add_logs():
-            nc.vector.tensor_tensor(out=ln_i0[:], in0=lnf[:, 0, :], in1=lnf[:, 1, :], op=ALU.add)
+        def i0_factors():
+            nc.vector.scalar_tensor_tensor(out=mag[:], in0=i0_flat, scalar=-1.0, in1=i0_flat, op0=ALU.mult, op1=ALU.max)
+            nc.vector.tensor_scalar(out=sgn2[:], in0=i0_flat, scalar1=0.0, scalar2=2.0, op0=ALU.is_ge, op1=ALU.mult)
+            for k in range(3):
+                nc.vector.tensor_scalar(out=fac[:, k, :], in0=mag[:], scalar1=RANGES[k][0], scalar2=RANGES[k][1], op0=ALU.max, op1=ALU.min)
+            nc.vector.tensor_scalar(out=sgn[:], in0=sgn2[:], scalar1=-1.0, scalar2=None, op0=ALU.add)
 
-        s_wide = {}
+        def i0_logs():
+            for k in range(3):
+                nc.scalar.activation(out=lnf[:, k, :], in_=fac[:, k, :], func=ACT.Ln, scale=RANGES[k][2])
 
-        def new_wide(c):
-            wide_tile = big.tile([P, PACK, G * KP], BF16, name="big", align_bytes=64)
-            s_wide[c] = wide_tile
-        s_grp, s_codes, s_scales = {}, {}, {}
+        def i0_sum():
+            nc.vector.tensor_reduce(out=ln_i0[:], in_=lnf[:].rearrange("p k n -> p n k"), op=ALU.add, axis=AXIS.X)
 
-        def widen(c, g, j, eng):
-            src = sb_a[g][:, j, :] if c == 0 else sb_b[g][:, j, KP * (c - 1) : KP * c]
-            dst = s_wide[c][:, j, KP * g : KP * (g + 1)]
-            if eng == "v":
-                nc.vector.tensor_scalar(out=dst, in0=src.bitcast(FP8), scalar1=scale[:, g, j : j + 1], scalar2=None, op0=ALU.mult)
-            else:
-                nc.scalar.activation(out=dst, in_=src.bitcast(FP8), func=ACT.Copy, scale=scale[:, g, j : j + 1])
-
-        def s_inter(c, t):
-            gt = grp.tile([P, 4 * KP], BF16, name="s_grp", align_bytes=64)
-            s_grp[c, t] = gt
-            src = s_wide[c][:].rearrange("p j (q i t) -> p t q j i", i=4, t=4)
-            dst = gt[:].rearrange("p (q i j) -> p q j i", i=4, j=4)
-            nc.vector.tensor_copy(out=dst, in_=src[:, t])
-
-        def s_quant(c, t):
-            co = sq.tile([P, KP], U32, name="s_codes", align_bytes=64)
-            sc = sq.tile([P, KP], U8, name="s_scales", align_bytes=64)
-            s_codes[c, t], s_scales[c, t] = co, sc
-            nc.vector.quantize_mx(out=co[:].bitcast(FP8X4), scales=sc[:], in_=s_grp[c, t][:])
-
-        f_grp = {}
-
-        def new_f_grp(q):
-            f_grp_tile = fpool.tile([P, G, ZH], F32, name="f_grp", align_bytes=64)
-            f_grp[q] = f_grp_tile
-        f_codes = [keep.tile([P, G, ZH], U32, name="f_codes%d" % h, align_bytes=64) for h in range(NH)]
-        f_scales = [keep.tile([P, G, ZH], U8, name="f_scales%d" % h, align_bytes=64) for h in range(NH)]
-
-        def f_turn(z):
-            words = f_raw[z][:].bitcast(F32)
-            q, zz = divmod(z, 2)
-            if zz == 0:
-                new_f_grp(q)
-            for gp in range(2):
-                bank = psum.tile([P, 512], F32, name="bank")
-                for k in range(2):
-                    for u in range(2):
-                        g = 2 * gp + k
-                        nc.tensor.transpose(
-                            bank[:, (2 * k + u) * P : (2 * k + u + 1) * P],
-                            words[:, 256 * g + u : 256 * (g + 1) : 2],
-                            ident[:],
-                        )
-                dst = f_grp[q][:, 2 * gp : 2 * gp + 2, 2 * P * zz : 2 * P * (zz + 1)]
-                nc.scalar.copy(
-                    out=dst.rearrange("p g (r u) -> p g r u", u=2),
-                    in_=bank[:].rearrange("p (g u r) -> p g r u", g=2, u=2),
-                )
-
-        def f_quant(q, g):
-            h, k = divmod(q, 2)
-            nc.vector.quantize_mx(
-                out=f_codes[h][:, g, 256 * k : 256 * (k + 1)].bitcast(FP8X4),
-                scales=f_scales[h][:, g, 256 * k : 256 * (k + 1)],
-                in_=f_grp[q][:, g, :].bitcast(BF16),
-            )
-
-        h_planes = {}
-        banks = {}
-
-        def project(c, t, h, half=None):
-            if (c, t, h) not in banks:
-                bank_tile = psum.tile([P, 512], F32, name="bank")
-                banks[c, t, h] = bank_tile
-            bank = banks[c, t, h]
-            zs = slice(0, ZH) if half is None else slice(256 * half, 256 * (half + 1))
-            for g in range(G):
-                cols = slice(P * g, P * (g + 1))
-                nc.tensor.matmul_mx(
-                    out=bank[:, zs],
-                    lhsT=s_codes[c, t][:, cols].bitcast(FP8X4),
-                    lhsT_scale=s_scales[c, t][:, cols],
-                    rhs=f_codes[h][:, g, zs].bitcast(FP8X4),
-                    rhs_scale=f_scales[h][:, g, zs],
-                    start=(g == 0),
-                    stop=(g == G - 1),
-                )
-
-        def attenuate(c, t, h):
-            if (c, h) not in h_planes:
-                h_planes[c, h] = hp.tile([P, PACK, ZH], BF16, name="h_plane", align_bytes=64)
-            nc.scalar.activation(
-                out=h_planes[c, h][:, t, :],
-                in_=banks[c, t, h][:],
-                func=ACT.Exp,
-                bias=ln_i0[:, PACK * c + t : PACK * c + t + 1],
-                scale=-1.0,
-            )
-
-        h_grp = {}
-        h_codes = [hq.tile([P, Z], U32, name="h_codes%d" % c, align_bytes=64) for c in range(C)]
-        h_scales = [hq.tile([P, Z], U8, name="h_scales%d" % c, align_bytes=64) for c in range(C)]
-
-        def h_inter(c, z0, w, eng):
-            gt = grp.tile([P, 4 * 256], BF16, name="h_grp", align_bytes=64)
-            h_grp[c, z0] = gt
-            h, z1 = divmod(z0, ZH)
-            src = h_planes[c, h][:, :, z1 : z1 + w].rearrange("p j (q i) -> p q j i", i=4)
-            dst = gt[:, 0 : 4 * w].rearrange("p (q i j) -> p q j i", i=4, j=4)
+        def copy_on(eng, dst, src):
             if eng == "v":
                 nc.vector.tensor_copy(out=dst, in_=src)
             else:
                 nc.scalar.copy(out=dst, in_=src)
 
-        def h_quant(c, z0, w):
-            nc.vector.quantize_mx(
-                out=h_codes[c][:, z0 : z0 + w].bitcast(FP8X4), scales=h_scales[c][:, z0 : z0 + w], in_=h_grp[c, z0][:, 0 : 4 * w]
+        def quantize(codes, scales, src):
+            nc.vector.quantize_mx(out=codes.bitcast(FP8X4), scales=scales, in_=src)
+
+        s_wide, s_grp, s_codes, s_scales, s_banks = {}, {}, {}, {}, {}
+
+        def widen(c, g, j, eng):
+            if (c, g) not in s_wide:
+                s_wide[c, g] = ring.tile([P, PACK, KP], BF16, name="s_wide", bufs=WIDE_BUFS, align_bytes=64)
+            tile, c0 = s_bytes[c, g]
+            src = tile[:, j, c0 : c0 + KP].bitcast(FP8)
+            dst = s_wide[c, g][:, j, :]
+            if eng == "v":
+                nc.vector.tensor_scalar(out=dst, in0=src, scalar1=scale[:, g, j : j + 1], scalar2=None, op0=ALU.mult)
+            else:
+                nc.scalar.activation(out=dst, in_=src, func=ACT.Copy, scale=scale[:, g, j : j + 1])
+
+        def new_s_grp(c, g):
+            if (c, g) not in s_grp:
+                s_grp[c, g] = ring.tile([P, PACK * KP], BF16, name="grp", bufs=GRP_BUFS, align_bytes=64)
+            return s_grp[c, g]
+
+        def s_inter(c, g):
+            src = s_wide[c, g][:].rearrange("p j (q i t) -> p t q j i", i=SI, t=4)
+            dst = new_s_grp(c, g)[:].rearrange("p (t q i j) -> p t q j i", t=4, i=SI, j=4)
+            nc.vector.tensor_copy(out=dst, in_=src)
+
+        def s_weave(c, g, k):
+            b, kk = divmod(k, 2)
+            if kk == 0:
+                s_banks[c, g, b] = psum.tile([P, 2 * KP], BF16, name="bank")
+            nc.tensor.matmul(
+                out=s_banks[c, g, b][:, KP * kk : KP * (kk + 1)],
+                lhsT=ident_bf[:],
+                rhs=s_wide[c, g][:, :, P * k : P * (k + 1)].rearrange("p j n -> p n j"),
+                start=True,
+                stop=True,
             )
 
-        d_grp = []
-        d_codes = [keep.tile([P, B], U32, name="d_codes%d" % c, align_bytes=64) for c in range(C)]
-        d_scales = [keep.tile([P, B], U8, name="d_scales%d" % c, align_bytes=64) for c in range(C)]
+        def s_drain(c, g, b, eng):
+            src = s_banks[c, g, b][:].bitcast(F32).rearrange("p (m t w) -> p t m w", t=4, w=2)
+            dst = new_s_grp(c, g)[:].bitcast(F32).rearrange("p (t m w) -> p t m w", t=4, w=2)
+            copy_on(eng, dst[:, :, 64 * b : 64 * (b + 1), :], src)
+
+        def s_quant(c, g):
+            s_codes[c, g] = ring.tile([P, KP], U32, name="s_codes", bufs=CODE_BUFS, align_bytes=64)
+            s_scales[c, g] = ring.tile([P, KP], U8, name="s_scales", bufs=CODE_BUFS, align_bytes=64)
+            quantize(s_codes[c, g][:], s_scales[c, g][:], s_grp[c, g][:])
+
+        f_banks, f_grp, f_codes, f_scales = {}, {}, {}, {}
+
+        def f_turn(h, g, z):
+            b, zz = divmod(z, 2)
+            if zz == 0:
+                f_banks[h, g, b] = psum.tile([P, KP], F32, name="bank")
+            words = f_raw[h, g][:, z, :].bitcast(F32)
+            for u in range(2):
+                nc.tensor.transpose(f_banks[h, g, b][:, (2 * zz + u) * P : (2 * zz + u + 1) * P], words[:, u : 2 * P : 2], ident[:])
+
+        def f_drain(h, g, b, eng):
+            if b == 0:
+                f_grp[h, g] = ring.tile([P, PACK * ZH], BF16, name="grp", bufs=GRP_BUFS, align_bytes=64)
+            dst = f_grp[h, g][:].bitcast(F32)[:, KP * b : KP * (b + 1)]
+            copy_on(eng, dst.rearrange("p (z r u) -> p z r u", z=2, u=2), f_banks[h, g, b][:].rearrange("p (z u r) -> p z r u", z=2, u=2))
+
+        def f_quant(h, g):
+            f_codes[h, g] = keep.tile([P, ZH], U32, name="f_codes%d_%d" % (h, g), align_bytes=64)
+            f_scales[h, g] = keep.tile([P, ZH], U8, name="f_scales%d_%d" % (h, g), align_bytes=64)
+            quantize(f_codes[h, g][:], f_scales[h, g][:], f_grp[h, g][:])
+
+        p_banks, h_planes, h_grp, h_codes, h_scales = {}, {}, {}, {}, {}
+
+        def project(c, z0, w, t, g):
+            if g == 0:
+                p_banks[c, z0, t] = psum.tile([P, KP], F32, name="bank")
+            h, z1 = divmod(z0, ZH)
+            nc.tensor.matmul_mx(
+                out=p_banks[c, z0, t][:, 0:w],
+                lhsT=s_codes[c, g][:, P * t : P * (t + 1)].bitcast(FP8X4),
+                lhsT_scale=s_scales[c, g][:, P * t : P * (t + 1)],
+                rhs=f_codes[h, g][:, z1 : z1 + w].bitcast(FP8X4),
+                rhs_scale=f_scales[h, g][:, z1 : z1 + w],
+                start=(g == 0),
+                stop=(g == G - 1),
+            )
+
+        def project_g(c, z0, w, g):
+            for t in range(PACK):
+                project(c, z0, w, t, g)
+
+        def project_t(c, z0, w, t):
+            for g in range(G):
+                project(c, z0, w, t, g)
+
+        def attenuate(c, z0, w, t):
+            if t == 0:
+                h_planes[c, z0] = ring.tile([P, PACK, w], BF16, name="h_plane", bufs=PLANE_BUFS, align_bytes=64)
+            nc.scalar.activation(
+                out=h_planes[c, z0][:, t, :],
+                in_=p_banks[c, z0, t][:, 0:w],
+                func=ACT.Exp,
+                bias=ln_i0[:, PACK * c + t : PACK * c + t + 1],
+                scale=-1.0,
+            )
+
+        def h_inter(c, z0, z1, w, eng):
+            h_grp[c, z0 + z1] = ring.tile([P, PACK * w], BF16, name="grp", bufs=GRP_BUFS, align_bytes=64)
+            src = h_planes[c, z0][:, :, z1 : z1 + w].rearrange("p j (q i) -> p q j i", i=4)
+            copy_on(eng, h_grp[c, z0 + z1][:].rearrange("p (q i j) -> p q j i", i=4, j=4), src)
+
+        def h_quant(c, z, w):
+            codes = keep.tile([P, w], U32, name="h_codes%d_%d" % (c, z), align_bytes=64)
+            scales = keep.tile([P, w], U8, name="h_scales%d_%d" % (c, z), align_bytes=64)
+            for k in range(w // P):
+                h_codes[c, z // P + k] = codes[:, P * k : P * (k + 1)]
+                h_scales[c, z // P + k] = scales[:, P * k : P * (k + 1)]
+            quantize(codes[:], scales[:], h_grp[c, z][:])
+
+        d_grp, d_codes, d_scales = {}, {}, {}
 
         def d_sign(c):
             for j in range(PACK):
@@ -239,202 +237,177 @@ def tile_tomography_forward_transmission_d3_kernel(tc, F, S_bytes, S_scale, i0, 
                     out=d_raw[c][:, j, :], in0=d_raw[c][:, j, :], scalar1=sgn[:, PACK * c + j : PACK * c + j + 1], scalar2=None, op0=ALU.mult
                 )
 
-        def d_inter(c, eng="v"):
-            if not d_grp:
-                d_grp_tile = big.tile([P, C, PACK * B], BF16, name="big", align_bytes=64)
-                d_grp.append(d_grp_tile)
-            dst = d_grp[0][:, c, :].rearrange("p (q i j) -> p q j i", i=4, j=4)
-            src = d_raw[c][:].rearrange("p j (q i) -> p q j i", i=4)
-            if eng == "v":
-                nc.vector.tensor_copy(out=dst, in_=src)
-            else:
-                nc.scalar.copy(out=dst, in_=src)
+        def d_inter(c, eng):
+            d_grp[c] = ring.tile([P, PACK * B], BF16, name="grp", bufs=GRP_BUFS, align_bytes=64)
+            copy_on(eng, d_grp[c][:].rearrange("p (q i j) -> p q j i", i=4, j=4), d_raw[c][:].rearrange("p j (q i) -> p q j i", i=4))
 
         def d_quant(c):
-            nc.vector.quantize_mx(out=d_codes[c][:].bitcast(FP8X4), scales=d_scales[c][:], in_=d_grp[0][:, c, :])
+            d_codes[c] = keep.tile([P, B], U32, name="d_codes%d" % c, align_bytes=64)
+            d_scales[c] = keep.tile([P, B], U8, name="d_scales%d" % c, align_bytes=64)
+            quantize(d_codes[c][:], d_scales[c][:], d_grp[c][:])
 
         y_banks = {}
-        y_all = []
 
-        def detect(z, cs):
-            if z not in y_banks:
-                y_banks[z] = psum.tile([P, 512], F32, name="bank")
-            for c in cs:
-                cols = slice(P * z, P * (z + 1))
-                nc.tensor.matmul_mx(
-                    out=y_banks[z][:],
-                    lhsT=h_codes[c][:, cols].bitcast(FP8X4),
-                    lhsT_scale=h_scales[c][:, cols],
-                    rhs=d_codes[c][:].bitcast(FP8X4),
-                    rhs_scale=d_scales[c][:],
-                    start=(c == 0),
-                    stop=(c == C - 1),
-                )
+        def detect(z, c, first, last):
+            if first:
+                y_banks[z] = psum.tile([P, B], F32, name="bank")
+            nc.tensor.matmul_mx(
+                out=y_banks[z][:],
+                lhsT=h_codes[c, z].bitcast(FP8X4),
+                lhsT_scale=h_scales[c, z],
+                rhs=d_codes[c][:].bitcast(FP8X4),
+                rhs_scale=d_scales[c][:],
+                start=first,
+                stop=last,
+            )
 
         def store(z, eng):
-            if not y_all:
-                y_tile = big.tile([P, 8, B], F32, name="big", align_bytes=64)
-                y_all.append(y_tile)
-            yt = y_all[0][:, z, :]
-            if eng == "v":
-                nc.vector.tensor_copy(out=yt, in_=y_banks[z][:])
-            else:
-                nc.scalar.copy(out=yt, in_=y_banks[z][:])
-            nc.sync.dma_start(out=out[P * z : P * (z + 1), :], in_=yt)
+            y_tile = ring.tile([P, B], F32, name="y_tile", bufs=Y_BUFS)
+            copy_on(eng, y_tile[:], y_banks[z][:])
+            nc.sync.dma_start(out=out[P * z : P * (z + 1), :], in_=y_tile[:])
 
-        load_ln_table()
-        load_sa(0)
-        load_sa(1)
-        load_sa(2)
-        load_sa(3)
-        load_f(0)
-        load_f(1)
-        load_sb(0)
-        load_f(2)
-        load_sb(1)
-        load_f(3)
-        load_sb(2)
-        load_f(4)
-        load_sb(3)
-        load_f(5)
-        new_wide(0)
-        new_wide(1)
-        step = 0
-        for g in range(G):
+        def widen_rows(c, g, engs):
             for j in range(PACK):
-                eng = "s" if (g < 2 and j >= 2) or (g == 2 and j == 3) else "v"
-                widen(0, g, j, eng)
-                if eng == "v" and step < 7:
-                    i0_step(step)
-                    step += 1
-        log_i0()
-        for z in range(5):
-            f_turn(z)
-            if z == 0:
-                for k in (6, 7):
-                    load_f(k)
-                for c in range(C):
-                    load_d(c)
-            if z < 4:
-                for j in (2, 3):
-                    widen(1, z, j, "s")
-        s_inter(0, 0)
-        s_inter(0, 1)
-        s_quant(0, 0)
-        s_inter(0, 2)
-        s_quant(0, 1)
-        add_logs()
-        for g in range(G):
-            f_quant(0, g)
-        s_inter(0, 3)
-        s_quant(0, 2)
-        for g in range(4):
-            for j in (0, 1):
-                widen(1, g, j, "v")
-        s_quant(0, 3)
-        for g in range(G):
-            f_quant(1, g)
-        for t in range(2):
-            project(0, t, 0, 0)
-        new_wide(2)
-        for g in range(1):
-            for j in (2, 3):
-                widen(2, g, j, "s")
-        for z in range(5, 8):
-            f_turn(z)
-            if True:
-                for j in (2, 3):
-                    widen(2, z - 5 + 1, j, "s")
-        for g in range(4, G):
-            for j in (0, 1):
-                widen(1, g, j, "v")
-        for t in range(2, 4):
-            project(0, t, 0, 0)
-        for t in range(4):
-            project(0, t, 0, 1)
+                if engs[j] != "-":
+                    widen(c, g, j, engs[j])
+
+        def turn(h, g, weave):
+            for k in range(4):
+                f_turn(h, g, k)
+                if weave:
+                    s_weave(0, g, k)
+                if k % 2 == 1:
+                    f_drain(h, g, k // 2, "s")
+                    if weave:
+                        s_drain(0, g, k // 2, "s")
+
+        load_small()
+        load_s(0, 0, 1)
+        load_s(0, 1, C)
+        load_f(0, 0)
+        load_s(1, 0, 1)
+        load_f(0, 1)
+        for g in range(2, G):
+            load_s(g, 0, 1)
+            load_s(g - 1, 1, C)
+            load_f(0, g)
+        load_f(1, 0)
+        load_s(G - 1, 1, C)
+        for g in range(1, G):
+            load_f(1, g)
+        for c in range(C):
+            load_d(c)
+        warm_ln()
+        identities()
+        i0_factors()
+        i0_logs()
+        warm_exp()
+        widen_rows(0, 0, "vvvv")
+        i0_sum()
+        widen_rows(1, 0, "vvvv")
+        widen_rows(2, 0, "vvss")
+        for k in range(4):
+            s_weave(0, 0, k)
+            if k % 2 == 1:
+                s_drain(0, 0, k // 2, "s")
+        turn(0, 0, False)
+        widen_rows(0, 1, "vvvv")
         s_inter(1, 0)
-        for g in range(G):
-            f_quant(2, g)
-        s_inter(1, 1)
+        s_quant(0, 0)
+        f_quant(0, 0)
+        turn(0, 1, True)
+        project_g(0, 0, ZH, 0)
+        widen_rows(0, 2, "vvvv")
         s_quant(1, 0)
-        s_inter(1, 2)
+        f_quant(0, 1)
+        s_quant(0, 1)
+        widen_rows(1, 1, "vvss")
+        turn(0, 2, True)
+        project_g(0, 0, ZH, 1)
+        widen_rows(0, 3, "vvvv")
+        s_inter(1, 1)
+        f_quant(0, 2)
+        s_quant(0, 2)
+        widen_rows(1, 2, "vvss")
+        turn(0, 3, True)
+        project_g(0, 0, ZH, 2)
         s_quant(1, 1)
-        for g in range(G):
-            f_quant(3, g)
-        for t in range(4):
-            attenuate(0, t, 0)
-        for t in range(4):
-            project(0, t, 1, 0)
-        for t in range(4):
-            project(0, t, 1, 1)
-        for t in range(4):
-            attenuate(0, t, 1)
-        for g in range(3, G):
-            for j in (0, 1):
-                widen(2, g, j, "s")
-        for k in range(5, 13):
-            c, t = divmod(k, 4)
-            if 6 < k < 12:
-                s_inter(c, t)
-            c, t = divmod(k - 1, 4)
-            if k > 6:
-                s_quant(c, t)
-            for h in range(NH if c == 1 else 1):
-                project(c, t, h)
-            if c == 1:
-                h_inter(0, 256 * t, 256, "s")
-                for h in range(NH):
-                    attenuate(1, t, h)
-            else:
-                h_quant(0, 256 * t, 256)
-            if k == 7:
-                for cc in range(C):
-                    d_sign(cc)
-                d_inter(0)
-            if k == 7:
-                for g in range(3):
-                    for j in (0, 1):
-                        widen(2, g, j, "v")
-        for t in range(4):
-            project(2, t, 1)
-        for t in range(4):
-            attenuate(2, t, 0)
-        for k in (1, 2, 3):
-            h_inter(1, 256 * k, 256, "s")
-        for t in range(4):
-            attenuate(2, t, 1)
-        for k in (0,):
-            h_inter(1, 256 * k, 256, "v")
+        s_inter(1, 2)
+        f_quant(0, 3)
+        s_quant(0, 3)
+        widen_rows(1, 3, "vvss")
+        turn(1, 0, False)
+        turn(1, 1, False)
+        project_g(0, 0, ZH, 3)
+        f_quant(1, 0)
+        s_inter(1, 3)
+        f_quant(1, 1)
+        s_quant(1, 2)
+        widen_rows(2, 1, "vv--")
+        s_inter(2, 0)
+        attenuate(0, 0, ZH, 0)
+        attenuate(0, 0, ZH, 1)
+        turn(1, 2, False)
+        attenuate(0, 0, ZH, 2)
+        attenuate(0, 0, ZH, 3)
+        project_g(0, ZH, ZH, 0)
+        turn(1, 3, False)
+        project_g(0, ZH, ZH, 1)
+        f_quant(1, 2)
+        s_quant(1, 3)
+        f_quant(1, 3)
+        s_quant(2, 0)
+        project_g(0, ZH, ZH, 2)
+        project_g(0, ZH, ZH, 3)
+        widen_rows(2, 1, "--ss")
+        widen_rows(2, 2, "vvss")
+        d_sign(0)
+        s_inter(2, 1)
+        d_inter(0, "v")
+        s_quant(2, 1)
+        s_inter(2, 2)
         d_quant(0)
-        d_inter(1)
-        d_inter(2)
+        for g in range(G):
+            project_g(1, 0, ZH, g)
+            attenuate(0, ZH, ZH, g)
+        widen_rows(2, 3, "vsss")
+        d_sign(1)
+        s_quant(2, 2)
+        s_inter(2, 3)
+        d_sign(2)
+        s_quant(2, 3)
+        d_inter(1, "v")
+        d_inter(2, "v")
         d_quant(1)
+        for t in range(PACK):
+            attenuate(1, 0, ZH, t)
+        h_inter(0, 0, 0, ZH, "s")
+        for t in range(PACK):
+            project_t(1, ZH, ZH, t)
+            attenuate(1, ZH, ZH, t)
+        h_inter(0, ZH, 0, ZH, "v")
         d_quant(2)
-        for k in range(2):
-            h_quant(1, 256 * k, 256)
-        for z in range(4):
-            detect(z, (0, 1))
-        h_inter(2, 0, 256, "v")
-        h_inter(2, 256, 256, "v")
+        h_quant(0, 0, ZH)
+        h_quant(0, ZH, ZH)
+        for t in range(PACK):
+            project_t(2, 0, ZH, t)
+            attenuate(2, 0, ZH, t)
+        h_inter(1, 0, 0, ZH, "s")
+        h_inter(2, 0, 0, 256, "v")
+        h_inter(2, 0, 256, 256, "v")
         h_quant(2, 0, 256)
-        for k in ():
-            h_inter(1, 256 * k, 256, "v")
         h_quant(2, 256, 256)
-        for z in range(4, 8):
-            detect(z, (0,))
-        for z in range(4):
-            detect(z, (2,))
-            store(z, "s")
-        for k in range(2, 4):
-            h_quant(1, 256 * k, 256)
-        for z in range(4, 8):
-            detect(z, (1,))
-        h_inter(2, 512, 256, "v")
-        h_inter(2, 768, 128, "v")
-        h_quant(2, 512, 256)
-        h_inter(2, 896, 128, "v")
-        h_quant(2, 768, 128)
-        h_quant(2, 896, 128)
-        for z in range(4, 8):
-            detect(z, (2,))
-            store(z, "v" if z == 7 else "s")
+        h_quant(1, 0, ZH)
+        h_inter(1, ZH, 0, ZH, "v")
+        for t in range(PACK):
+            project_t(2, ZH, ZH, t)
+            attenuate(2, ZH, ZH, t)
+        h_inter(2, ZH, 0, 256, "v")
+        h_quant(1, ZH, ZH)
+        h_inter(2, ZH, 256, 256, "v")
+        h_quant(2, ZH, 256)
+        h_quant(2, ZH + 256, 256)
+        for z in range(8):
+            for c in range(C):
+                detect(z, c, c == 0, c == C - 1)
+            store(z, "s" if z < 7 else "v")

@@ -47,8 +47,8 @@ def tile_tomography_forward_transmission_d3_kernel(tc, F, S_bytes, S_scale, i0, 
         s_bytes, f_raw, d_raw = {}, {}, {}
 
         def load_small():
-            nc.scalar.dma_start(out=scale[:], in_=S_scale.rearrange("(g p j) o -> p g (j o)", p=P, j=PACK))
-            nc.scalar.dma_start(out=i0_t[:], in_=i0.rearrange("(c p j) -> p c j", p=P, j=PACK))
+            nc.sync.dma_start(out=scale[:], in_=S_scale.rearrange("(g p j) o -> p g (j o)", p=P, j=PACK))
+            nc.sync.dma_start(out=i0_t[:], in_=i0.rearrange("(c p j) -> p c j", p=P, j=PACK))
 
         def load_s(g, c0, c1):
             w = KP * (c1 - c0)
@@ -68,11 +68,9 @@ def tile_tomography_forward_transmission_d3_kernel(tc, F, S_bytes, S_scale, i0, 
             nc.sync.dma_start(out=tile[:], in_=d_view[c])
 
         ident = keep.tile([P, P], F32, name="ident")
-        ident_bf = keep.tile([P, P], BF16, name="ident_bf")
 
         def identities():
             make_identity(nc, ident[:])
-            nc.vector.tensor_copy(out=ident_bf[:], in_=ident[:])
 
         i0_flat = i0_t[:].rearrange("p c j -> p (c j)")
         mag = keep.tile([P, C * PACK], F32, name="mag")
@@ -137,23 +135,6 @@ def tile_tomography_forward_transmission_d3_kernel(tc, F, S_bytes, S_scale, i0, 
             src = s_wide[c, g][:].rearrange("p j (q i t) -> p t q j i", i=SI, t=4)
             dst = new_s_grp(c, g)[:].rearrange("p (t q i j) -> p t q j i", t=4, i=SI, j=4)
             nc.vector.tensor_copy(out=dst, in_=src)
-
-        def s_weave(c, g, k):
-            b, kk = divmod(k, 2)
-            if kk == 0:
-                s_banks[c, g, b] = psum.tile([P, 2 * KP], BF16, name="bank")
-            nc.tensor.matmul(
-                out=s_banks[c, g, b][:, KP * kk : KP * (kk + 1)],
-                lhsT=ident_bf[:],
-                rhs=s_wide[c, g][:, :, P * k : P * (k + 1)].rearrange("p j n -> p n j"),
-                start=True,
-                stop=True,
-            )
-
-        def s_drain(c, g, b, eng):
-            src = s_banks[c, g, b][:].bitcast(F32).rearrange("p (m t w) -> p t m w", t=4, w=2)
-            dst = new_s_grp(c, g)[:].bitcast(F32).rearrange("p (t m w) -> p t m w", t=4, w=2)
-            copy_on(eng, dst[:, :, 64 * b : 64 * (b + 1), :], src)
 
         def s_quant(c, g):
             s_codes[c, g] = ring.tile([P, KP], U32, name="s_codes", bufs=CODE_BUFS, align_bytes=64)
@@ -271,29 +252,23 @@ def tile_tomography_forward_transmission_d3_kernel(tc, F, S_bytes, S_scale, i0, 
                 if engs[j] != "-":
                     widen(c, g, j, engs[j])
 
-        def turn(h, g, weave):
+        def turn(h, g):
             for k in range(4):
                 f_turn(h, g, k)
-                if weave:
-                    s_weave(0, g, k)
-                if k % 2 == 1:
-                    f_drain(h, g, k // 2, "s")
-                    if weave:
-                        s_drain(0, g, k // 2, "s")
+
+        def drain(h, g):
+            for b in range(2):
+                f_drain(h, g, b, "s")
 
         load_small()
-        load_s(0, 0, 1)
-        load_s(0, 1, C)
-        load_f(0, 0)
-        load_s(1, 0, 1)
-        load_f(0, 1)
-        for g in range(2, G):
+        for g in range(G):
             load_s(g, 0, 1)
-            load_s(g - 1, 1, C)
+            if g == G - 1:
+                load_s(0, 1, C)
             load_f(0, g)
         load_f(1, 0)
-        load_s(G - 1, 1, C)
         for g in range(1, G):
+            load_s(g, 1, C)
             load_f(1, g)
         for c in range(C):
             load_d(c)
@@ -304,110 +279,128 @@ def tile_tomography_forward_transmission_d3_kernel(tc, F, S_bytes, S_scale, i0, 
         warm_exp()
         widen_rows(0, 0, "vvvv")
         i0_sum()
-        widen_rows(1, 0, "vvvv")
-        widen_rows(2, 0, "vvss")
-        for k in range(4):
-            s_weave(0, 0, k)
-            if k % 2 == 1:
-                s_drain(0, 0, k // 2, "s")
-        turn(0, 0, False)
-        widen_rows(0, 1, "vvvv")
-        s_inter(1, 0)
+        s_inter(0, 0)
+        widen_rows(0, 1, "vvss")
+        turn(0, 0)
+        drain(0, 0)
         s_quant(0, 0)
+        s_inter(0, 1)
+        widen_rows(0, 2, "--ss")
+        turn(0, 1)
+        drain(0, 1)
         f_quant(0, 0)
-        turn(0, 1, True)
         project_g(0, 0, ZH, 0)
-        widen_rows(0, 2, "vvvv")
-        s_quant(1, 0)
-        f_quant(0, 1)
+        widen_rows(0, 2, "vv--")
         s_quant(0, 1)
-        widen_rows(1, 1, "vvss")
-        turn(0, 2, True)
+        f_quant(0, 1)
+        s_inter(0, 2)
+        widen_rows(0, 3, "ssss")
+        turn(0, 2)
+        drain(0, 2)
         project_g(0, 0, ZH, 1)
-        widen_rows(0, 3, "vvvv")
-        s_inter(1, 1)
-        f_quant(0, 2)
         s_quant(0, 2)
-        widen_rows(1, 2, "vvss")
-        turn(0, 3, True)
+        s_inter(0, 3)
+        f_quant(0, 2)
+        widen_rows(1, 0, "vvss")
+        turn(0, 3)
+        drain(0, 3)
         project_g(0, 0, ZH, 2)
-        s_quant(1, 1)
-        s_inter(1, 2)
-        f_quant(0, 3)
         s_quant(0, 3)
-        widen_rows(1, 3, "vvss")
-        turn(1, 0, False)
-        turn(1, 1, False)
+        s_inter(1, 0)
+        f_quant(0, 3)
+        widen_rows(1, 1, "vvss")
+        turn(1, 0)
+        drain(1, 0)
         project_g(0, 0, ZH, 3)
+        s_quant(1, 0)
         f_quant(1, 0)
-        s_inter(1, 3)
-        f_quant(1, 1)
-        s_quant(1, 2)
-        widen_rows(2, 1, "vv--")
-        s_inter(2, 0)
+        s_inter(1, 1)
+        widen_rows(1, 2, "vvss")
+        turn(1, 1)
         attenuate(0, 0, ZH, 0)
         attenuate(0, 0, ZH, 1)
-        turn(1, 2, False)
+        drain(1, 1)
+        project_g(0, ZH, ZH, 0)
+        s_quant(1, 1)
+        f_quant(1, 1)
+        s_inter(1, 2)
+        turn(1, 2)
         attenuate(0, 0, ZH, 2)
         attenuate(0, 0, ZH, 3)
-        project_g(0, ZH, ZH, 0)
-        turn(1, 3, False)
+        drain(1, 2)
         project_g(0, ZH, ZH, 1)
+        widen_rows(1, 3, "vvvv")
         f_quant(1, 2)
-        s_quant(1, 3)
-        f_quant(1, 3)
-        s_quant(2, 0)
+        s_quant(1, 2)
+        turn(1, 3)
+        drain(1, 3)
         project_g(0, ZH, ZH, 2)
+        widen_rows(2, 0, "vvss")
+        f_quant(1, 3)
+        s_inter(1, 3)
         project_g(0, ZH, ZH, 3)
-        widen_rows(2, 1, "--ss")
-        widen_rows(2, 2, "vvss")
-        d_sign(0)
-        s_inter(2, 1)
-        d_inter(0, "v")
-        s_quant(2, 1)
-        s_inter(2, 2)
-        d_quant(0)
+        widen_rows(2, 1, "vsss")
+        s_inter(2, 0)
+        s_quant(1, 3)
+        widen_rows(2, 2, "vsss")
         for g in range(G):
             project_g(1, 0, ZH, g)
             attenuate(0, ZH, ZH, g)
+        s_inter(2, 1)
+        s_quant(2, 0)
         widen_rows(2, 3, "vsss")
-        d_sign(1)
+        s_inter(2, 2)
+        s_quant(2, 1)
+        d_sign(0)
         s_quant(2, 2)
         s_inter(2, 3)
-        d_sign(2)
+        d_inter(0, "v")
         s_quant(2, 3)
+        d_sign(1)
+        d_quant(0)
         d_inter(1, "v")
-        d_inter(2, "v")
+        d_sign(2)
         d_quant(1)
+        d_inter(2, "v")
         for t in range(PACK):
             attenuate(1, 0, ZH, t)
         h_inter(0, 0, 0, ZH, "s")
         for t in range(PACK):
             project_t(1, ZH, ZH, t)
             attenuate(1, ZH, ZH, t)
-        h_inter(0, ZH, 0, ZH, "v")
-        d_quant(2)
-        h_quant(0, 0, ZH)
-        h_quant(0, ZH, ZH)
+        for g in range(G):
+            project_g(2, 0, ZH, g)
         for t in range(PACK):
-            project_t(2, 0, ZH, t)
             attenuate(2, 0, ZH, t)
         h_inter(1, 0, 0, ZH, "s")
-        h_inter(2, 0, 0, 256, "v")
-        h_inter(2, 0, 256, 256, "v")
-        h_quant(2, 0, 256)
-        h_quant(2, 256, 256)
+        h_quant(0, 0, ZH)
+        d_quant(2)
+        h_inter(2, 0, 0, ZH, "v")
+        h_inter(0, ZH, 0, 256, "v")
+        h_quant(2, 0, ZH)
         h_quant(1, 0, ZH)
-        h_inter(1, ZH, 0, ZH, "v")
         for t in range(PACK):
             project_t(2, ZH, ZH, t)
             attenuate(2, ZH, ZH, t)
+        h_inter(2, ZH, 256, 256, "s")
+        for c in (0, 2, 1):
+            for z in range(4):
+                detect(z, c, c == 0, c == 1)
+                if c == 1:
+                    store(z, "s")
+        h_inter(1, ZH, 0, 256, "v")
+        h_quant(0, ZH, 256)
         h_inter(2, ZH, 0, 256, "v")
-        h_quant(1, ZH, ZH)
-        h_inter(2, ZH, 256, 256, "v")
+        h_quant(1, ZH, 256)
+        h_inter(0, ZH, 256, 256, "v")
         h_quant(2, ZH, 256)
+        h_inter(1, ZH, 256, 256, "v")
+        h_quant(0, ZH + 256, 256)
         h_quant(2, ZH + 256, 256)
-        for z in range(8):
-            for c in range(C):
-                detect(z, c, c == 0, c == C - 1)
-            store(z, "s" if z < 7 else "v")
+        h_quant(1, ZH + 256, 256)
+        for z0, order in ((4, (0, 1, 2)), (6, (0, 2, 1))):
+            for c in order:
+                for z in (z0, z0 + 1):
+                    detect(z, c, c == order[0], c == order[2])
+                    if c == order[2]:
+                        store(z, "v" if z == 7 else "s")

@@ -27,7 +27,7 @@ WIDE_BUFS = 7
 GRP_BUFS = 6
 CODE_BUFS = 12
 PLANE_BUFS = 5
-Y_BUFS = 6
+Y_BUFS = 8
 SI = 4
 
 
@@ -43,24 +43,40 @@ def tile_tomography_forward_transmission_d3_kernel(tc, F, S_bytes, S_scale, i0, 
         i0_t = keep.tile([P, C, PACK], BF16, name="i0_t")
         s_view = S_bytes.rearrange("(g p j) n -> g p j n", p=P, j=PACK)
         f_view = F.rearrange("(h z p) (g k) -> h g p z k", p=P, z=4, k=KP)
+        f_pairs = F.rearrange("(h z p) (g k) -> h g p z k", p=P, z=4, k=2 * KP)
         d_view = D.rearrange("(c p j) b -> c p j b", p=P, j=PACK)
         s_bytes, f_raw, d_raw = {}, {}, {}
 
-        def load_small():
+        def load_scale():
             nc.sync.dma_start(out=scale[:], in_=S_scale.rearrange("(g p j) o -> p g (j o)", p=P, j=PACK))
+
+        def load_i0():
             nc.sync.dma_start(out=i0_t[:], in_=i0.rearrange("(c p j) -> p c j", p=P, j=PACK))
+
+        def load_s_rows(j0):
+            tile = keep.tile([P, 2, KP + 32], U8, name="s_first_%d" % j0)
+            for j in (j0, j0 + 1):
+                s_bytes[0, 0, j] = tile[:, j - j0, 0:KP]
+            nc.sync.dma_start(out=tile[:, :, 0:KP], in_=s_view[0][:, j0 : j0 + 2, 0:KP])
 
         def load_s(g, c0, c1):
             w = KP * (c1 - c0)
             tile = keep.tile([P, PACK, w + 32], U8, name="s_bytes_%d_%d" % (g, c0))
             for c in range(c0, c1):
-                s_bytes[c, g] = (tile, KP * (c - c0))
+                for j in range(PACK):
+                    s_bytes[c, g, j] = tile[:, j, KP * (c - c0) : KP * (c - c0 + 1)]
             nc.sync.dma_start(out=tile[:, :, 0:w], in_=s_view[g][:, :, KP * c0 : KP * c1])
 
         def load_f(h, g):
-            tile = ring.tile([P, 4, KP], BF16, name="f_raw", bufs=5)
+            tile = ring.tile([P, 4, KP], BF16, name="f_raw", bufs=3)
             f_raw[h, g] = tile
             nc.sync.dma_start(out=tile[:], in_=f_view[h, g])
+
+        def load_f_pair(h, g0):
+            tile = ring.tile([P, 4, 2 * KP], BF16, name="f_pair", bufs=2)
+            for g in (g0, g0 + 1):
+                f_raw[h, g] = tile[:, :, KP * (g - g0) : KP * (g - g0 + 1)]
+            nc.sync.dma_start(out=tile[:], in_=f_pairs[h, g0 // 2])
 
         def load_d(c):
             tile = keep.tile([P, PACK, B], BF16, name="d_raw%d" % c)
@@ -85,10 +101,10 @@ def tile_tomography_forward_transmission_d3_kernel(tc, F, S_bytes, S_scale, i0, 
 
         def warm_ln():
             nc.vector.memset(unit[:], 1.0)
-            nc.scalar.activation(out=unread[:, 0:1], in_=unit[:], func=ACT.Ln)
+            nc.scalar.activation(out=unread[:, 0:1], in_=unit[:, 0:1], func=ACT.Ln)
 
         def warm_exp():
-            nc.scalar.activation(out=unread[:, 1:2], in_=unit[:], func=ACT.Exp)
+            nc.scalar.activation(out=unread[:, 1:2], in_=unit[:, 0:1], func=ACT.Exp)
 
         def i0_factors():
             nc.vector.scalar_tensor_tensor(out=mag[:], in0=i0_flat, scalar=-1.0, in1=i0_flat, op0=ALU.mult, op1=ALU.max)
@@ -118,13 +134,24 @@ def tile_tomography_forward_transmission_d3_kernel(tc, F, S_bytes, S_scale, i0, 
         def widen(c, g, j, eng):
             if (c, g) not in s_wide:
                 s_wide[c, g] = ring.tile([P, PACK, KP], BF16, name="s_wide", bufs=WIDE_BUFS, align_bytes=64)
-            tile, c0 = s_bytes[c, g]
-            src = tile[:, j, c0 : c0 + KP].bitcast(FP8)
+            src = s_bytes[c, g, j].bitcast(FP8)
             dst = s_wide[c, g][:, j, :]
             if eng == "v":
                 nc.vector.tensor_scalar(out=dst, in0=src, scalar1=scale[:, g, j : j + 1], scalar2=None, op0=ALU.mult)
             else:
                 nc.scalar.activation(out=dst, in_=src, func=ACT.Copy, scale=scale[:, g, j : j + 1])
+
+        def widen_pairs(c, g):
+            s_wide[c, g] = ring.tile([P, 2, 2 * KP], BF16, name="s_wide", bufs=WIDE_BUFS, align_bytes=64)
+            for j in range(PACK):
+                src = s_bytes[c, g, j].bitcast(FP8)
+                dst = s_wide[c, g][:, j // 2, :].rearrange("p (t m e) -> p m t e", t=4, e=2)[:, :, :, j % 2]
+                nc.vector.tensor_scalar(out=dst, in0=src, scalar1=scale[:, g, j : j + 1], scalar2=None, op0=ALU.mult)
+
+        def join_pairs(c, g, eng):
+            src = s_wide[c, g][:].bitcast(F32).rearrange("p u n -> p n u")
+            dst = new_s_grp(c, g)[:].bitcast(F32).rearrange("p (n u) -> p n u", u=2)
+            copy_on(eng, dst, src)
 
         def new_s_grp(c, g):
             if (c, g) not in s_grp:
@@ -229,23 +256,23 @@ def tile_tomography_forward_transmission_d3_kernel(tc, F, S_bytes, S_scale, i0, 
 
         y_banks = {}
 
-        def detect(z, c, first, last):
+        def detect(z, c, first, last, b0=0, w=B):
             if first:
-                y_banks[z] = psum.tile([P, B], F32, name="bank")
+                y_banks[z, b0] = psum.tile([P, B], F32, name="bank")
             nc.tensor.matmul_mx(
-                out=y_banks[z][:],
+                out=y_banks[z, b0][:, 0:w],
                 lhsT=h_codes[c, z].bitcast(FP8X4),
                 lhsT_scale=h_scales[c, z],
-                rhs=d_codes[c][:].bitcast(FP8X4),
-                rhs_scale=d_scales[c][:],
+                rhs=d_codes[c][:, b0 : b0 + w].bitcast(FP8X4),
+                rhs_scale=d_scales[c][:, b0 : b0 + w],
                 start=first,
                 stop=last,
             )
 
-        def store(z, eng):
-            y_tile = ring.tile([P, B], F32, name="y_tile", bufs=Y_BUFS)
-            copy_on(eng, y_tile[:], y_banks[z][:])
-            nc.sync.dma_start(out=out[P * z : P * (z + 1), :], in_=y_tile[:])
+        def store(z, eng, b0=0, w=B, queue=nc.sync):
+            y_tile = ring.tile([P, w], F32, name="y_tile", bufs=Y_BUFS)
+            copy_on(eng, y_tile[:], y_banks[z, b0][:, 0:w])
+            queue.dma_start(out=out[P * z : P * (z + 1), b0 : b0 + w], in_=y_tile[:])
 
         def widen_rows(c, g, engs):
             for j in range(PACK):
@@ -260,16 +287,28 @@ def tile_tomography_forward_transmission_d3_kernel(tc, F, S_bytes, S_scale, i0, 
             for b in range(2):
                 f_drain(h, g, b, "s")
 
-        load_small()
+        def turn_between(h, g, c, z0, gp):
+            for b in range(2):
+                f_turn(h, g, 2 * b)
+                f_turn(h, g, 2 * b + 1)
+                f_drain(h, g, b, "s")
+                project(c, z0, ZH, 2 * b, gp)
+                project(c, z0, ZH, 2 * b + 1, gp)
+
+        load_scale()
+        load_i0()
+        load_s_rows(0)
+        load_s_rows(2)
         for g in range(G):
-            load_s(g, 0, 1)
-            if g == G - 1:
-                load_s(0, 1, C)
+            if g > 0:
+                load_s(g, 0, 1)
             load_f(0, g)
-        load_f(1, 0)
-        for g in range(1, G):
-            load_s(g, 1, C)
-            load_f(1, g)
+        load_s(0, 1, C)
+        load_f_pair(1, 0)
+        load_s(1, 1, C)
+        load_f_pair(1, 2)
+        load_s(2, 1, C)
+        load_s(3, 1, C)
         for c in range(C):
             load_d(c)
         warm_ln()
@@ -285,79 +324,75 @@ def tile_tomography_forward_transmission_d3_kernel(tc, F, S_bytes, S_scale, i0, 
         drain(0, 0)
         s_quant(0, 0)
         s_inter(0, 1)
-        widen_rows(0, 2, "--ss")
+        widen_rows(0, 2, "vvss")
         turn(0, 1)
         drain(0, 1)
-        f_quant(0, 0)
-        project_g(0, 0, ZH, 0)
-        widen_rows(0, 2, "vv--")
         s_quant(0, 1)
-        f_quant(0, 1)
+        f_quant(0, 0)
         s_inter(0, 2)
-        widen_rows(0, 3, "ssss")
         turn(0, 2)
         drain(0, 2)
-        project_g(0, 0, ZH, 1)
+        widen_rows(0, 3, "vsss")
+        f_quant(0, 1)
         s_quant(0, 2)
-        s_inter(0, 3)
-        f_quant(0, 2)
-        widen_rows(1, 0, "vvss")
         turn(0, 3)
         drain(0, 3)
-        project_g(0, 0, ZH, 2)
-        s_quant(0, 3)
-        s_inter(1, 0)
+        project_g(0, 0, ZH, 0)
+        f_quant(0, 2)
+        s_inter(0, 3)
+        widen_rows(1, 0, "vsss")
         f_quant(0, 3)
-        widen_rows(1, 1, "vvss")
+        s_quant(0, 3)
         turn(1, 0)
         drain(1, 0)
-        project_g(0, 0, ZH, 3)
+        project_g(0, 0, ZH, 1)
+        s_inter(1, 0)
+        widen_rows(1, 1, "vvss")
+        turn(1, 1)
+        drain(1, 1)
+        project_g(0, 0, ZH, 2)
         s_quant(1, 0)
         f_quant(1, 0)
         s_inter(1, 1)
         widen_rows(1, 2, "vvss")
-        turn(1, 1)
-        attenuate(0, 0, ZH, 0)
-        attenuate(0, 0, ZH, 1)
-        drain(1, 1)
-        project_g(0, ZH, ZH, 0)
-        s_quant(1, 1)
-        f_quant(1, 1)
-        s_inter(1, 2)
         turn(1, 2)
-        attenuate(0, 0, ZH, 2)
-        attenuate(0, 0, ZH, 3)
         drain(1, 2)
-        project_g(0, ZH, ZH, 1)
-        widen_rows(1, 3, "vvvv")
-        f_quant(1, 2)
-        s_quant(1, 2)
+        project_g(0, 0, ZH, 3)
+        f_quant(1, 1)
+        s_quant(1, 1)
+        s_inter(1, 2)
+        widen_rows(1, 3, "vvss")
         turn(1, 3)
         drain(1, 3)
-        project_g(0, ZH, ZH, 2)
-        widen_rows(2, 0, "vvss")
+        for t in range(PACK):
+            attenuate(0, 0, ZH, t)
+        f_quant(1, 2)
+        s_quant(1, 2)
         f_quant(1, 3)
         s_inter(1, 3)
-        project_g(0, ZH, ZH, 3)
-        widen_rows(2, 1, "vsss")
-        s_inter(2, 0)
+        for g in range(G):
+            project_g(0, ZH, ZH, g)
+        widen_rows(2, 0, "vvss")
         s_quant(1, 3)
+        d_sign(0)
+        s_inter(2, 0)
+        widen_rows(2, 1, "vvss")
+        for t in range(PACK):
+            attenuate(0, ZH, ZH, t)
+        s_quant(2, 0)
+        s_inter(2, 1)
         widen_rows(2, 2, "vsss")
+        d_inter(0, "v")
         for g in range(G):
             project_g(1, 0, ZH, g)
-            attenuate(0, ZH, ZH, g)
-        s_inter(2, 1)
-        s_quant(2, 0)
         widen_rows(2, 3, "vsss")
-        s_inter(2, 2)
         s_quant(2, 1)
-        d_sign(0)
+        s_inter(2, 2)
+        d_quant(0)
         s_quant(2, 2)
         s_inter(2, 3)
-        d_inter(0, "v")
-        s_quant(2, 3)
         d_sign(1)
-        d_quant(0)
+        s_quant(2, 3)
         d_inter(1, "v")
         d_sign(2)
         d_quant(1)
@@ -372,35 +407,44 @@ def tile_tomography_forward_transmission_d3_kernel(tc, F, S_bytes, S_scale, i0, 
             project_g(2, 0, ZH, g)
         for t in range(PACK):
             attenuate(2, 0, ZH, t)
-        h_inter(1, 0, 0, ZH, "s")
-        h_quant(0, 0, ZH)
+        h_inter(0, ZH, 0, ZH, "s")
+        h_inter(1, 0, 0, ZH, "v")
         d_quant(2)
-        h_inter(2, 0, 0, ZH, "v")
-        h_inter(0, ZH, 0, 256, "v")
-        h_quant(2, 0, ZH)
+        h_quant(0, 0, ZH)
+        h_inter(2, 0, 0, 256, "v")
         h_quant(1, 0, ZH)
+        h_quant(2, 0, 256)
+        h_inter(2, 0, 256, 256, "v")
+        h_inter(1, ZH, 0, 256, "v")
+        h_quant(2, 256, 256)
+        h_quant(0, ZH, ZH)
         for t in range(PACK):
             project_t(2, ZH, ZH, t)
             attenuate(2, ZH, ZH, t)
-        h_inter(2, ZH, 256, 256, "s")
-        for c in (0, 2, 1):
+        for c in range(C):
             for z in range(4):
-                detect(z, c, c == 0, c == 1)
-                if c == 1:
+                detect(z, c, c == 0, c == C - 1)
+                if c == C - 1:
                     store(z, "s")
-        h_inter(1, ZH, 0, 256, "v")
-        h_quant(0, ZH, 256)
         h_inter(2, ZH, 0, 256, "v")
         h_quant(1, ZH, 256)
-        h_inter(0, ZH, 256, 256, "v")
         h_quant(2, ZH, 256)
         h_inter(1, ZH, 256, 256, "v")
-        h_quant(0, ZH + 256, 256)
-        h_quant(2, ZH + 256, 256)
+        h_inter(2, ZH, 256, 128, "v")
+        for c in range(C):
+            for z in (4, 5):
+                detect(z, c, c == 0, c == C - 1)
+                if c == C - 1:
+                    store(z, "s")
+        h_inter(2, ZH, 384, 128, "v")
         h_quant(1, ZH + 256, 256)
-        for z0, order in ((4, (0, 1, 2)), (6, (0, 2, 1))):
-            for c in order:
-                for z in (z0, z0 + 1):
-                    detect(z, c, c == order[0], c == order[2])
-                    if c == order[2]:
-                        store(z, "v" if z == 7 else "s")
+        h_quant(2, ZH + 256, 128)
+        h_quant(2, ZH + 384, 128)
+        for c in range(C - 1):
+            for z in (6, 7):
+                for b0 in (0, 256):
+                    detect(z, c, c == 0, False, b0, 256)
+        for z in (6, 7):
+            for b0 in (0, 256):
+                detect(z, C - 1, False, True, b0, 256)
+                store(z, "v" if b0 == 0 else "s", b0, 256)

@@ -205,10 +205,6 @@ def tile_tomography_forward_transmission_d3_kernel(tc, F, S_bytes, S_scale, i0, 
                 stop=(g == G - 1),
             )
 
-        def project_g(c, z0, w, g):
-            for t in range(PACK):
-                project(c, z0, w, t, g)
-
         def project_t(c, z0, w, t):
             for g in range(G):
                 project(c, z0, w, t, g)
@@ -287,13 +283,10 @@ def tile_tomography_forward_transmission_d3_kernel(tc, F, S_bytes, S_scale, i0, 
             for b in range(2):
                 f_drain(h, g, b, "s")
 
-        def turn_between(h, g, c, z0, gp):
-            for b in range(2):
-                f_turn(h, g, 2 * b)
-                f_turn(h, g, 2 * b + 1)
-                f_drain(h, g, b, "s")
-                project(c, z0, ZH, 2 * b, gp)
-                project(c, z0, ZH, 2 * b + 1, gp)
+        def project_pairs(c, z0, ts, g0):
+            for t in ts:
+                project(c, z0, ZH, t, g0)
+                project(c, z0, ZH, t, g0 + 1)
 
         load_scale()
         load_i0()
@@ -337,27 +330,28 @@ def tile_tomography_forward_transmission_d3_kernel(tc, F, S_bytes, S_scale, i0, 
         s_quant(0, 2)
         turn(0, 3)
         drain(0, 3)
-        project_g(0, 0, ZH, 0)
+        project_pairs(0, 0, (0, 1), 0)
         f_quant(0, 2)
         s_inter(0, 3)
         widen_rows(1, 0, "vsss")
         f_quant(0, 3)
         s_quant(0, 3)
+        widen_rows(2, 0, "--s-")
         turn(1, 0)
         drain(1, 0)
-        project_g(0, 0, ZH, 1)
+        project_pairs(0, 0, (2, 3), 0)
         s_inter(1, 0)
         widen_rows(1, 1, "vvss")
         turn(1, 1)
         drain(1, 1)
-        project_g(0, 0, ZH, 2)
+        project_pairs(0, 0, (0, 1), 2)
         s_quant(1, 0)
         f_quant(1, 0)
         s_inter(1, 1)
         widen_rows(1, 2, "vvss")
         turn(1, 2)
         drain(1, 2)
-        project_g(0, 0, ZH, 3)
+        project_pairs(0, 0, (2, 3), 2)
         f_quant(1, 1)
         s_quant(1, 1)
         s_inter(1, 2)
@@ -370,30 +364,32 @@ def tile_tomography_forward_transmission_d3_kernel(tc, F, S_bytes, S_scale, i0, 
         s_quant(1, 2)
         f_quant(1, 3)
         s_inter(1, 3)
-        for g in range(G):
-            project_g(0, ZH, ZH, g)
-        widen_rows(2, 0, "vvss")
+        for g0 in (0, 2):
+            project_pairs(0, ZH, range(PACK), g0)
+        widen_rows(2, 0, "vv-s")
         s_quant(1, 3)
-        d_sign(0)
         s_inter(2, 0)
         widen_rows(2, 1, "vvss")
-        for t in range(PACK):
-            attenuate(0, ZH, ZH, t)
+        attenuate(0, ZH, ZH, 0)
+        attenuate(0, ZH, ZH, 1)
         s_quant(2, 0)
         s_inter(2, 1)
         widen_rows(2, 2, "vsss")
-        d_inter(0, "v")
-        for g in range(G):
-            project_g(1, 0, ZH, g)
+        attenuate(0, ZH, ZH, 2)
+        attenuate(0, ZH, ZH, 3)
+        for t in range(PACK):
+            project_t(1, 0, ZH, t)
         widen_rows(2, 3, "vsss")
         s_quant(2, 1)
         s_inter(2, 2)
-        d_quant(0)
+        d_sign(0)
         s_quant(2, 2)
         s_inter(2, 3)
         d_sign(1)
         s_quant(2, 3)
+        d_inter(0, "v")
         d_inter(1, "v")
+        d_quant(0)
         d_sign(2)
         d_quant(1)
         d_inter(2, "v")
@@ -403,15 +399,14 @@ def tile_tomography_forward_transmission_d3_kernel(tc, F, S_bytes, S_scale, i0, 
         for t in range(PACK):
             project_t(1, ZH, ZH, t)
             attenuate(1, ZH, ZH, t)
-        for g in range(G):
-            project_g(2, 0, ZH, g)
         for t in range(PACK):
+            project_t(2, 0, ZH, t)
             attenuate(2, 0, ZH, t)
         h_inter(0, ZH, 0, ZH, "s")
         h_inter(1, 0, 0, ZH, "v")
         d_quant(2)
-        h_quant(0, 0, ZH)
         h_inter(2, 0, 0, 256, "v")
+        h_quant(0, 0, ZH)
         h_quant(1, 0, ZH)
         h_quant(2, 0, 256)
         h_inter(2, 0, 256, 256, "v")
@@ -421,28 +416,26 @@ def tile_tomography_forward_transmission_d3_kernel(tc, F, S_bytes, S_scale, i0, 
         for t in range(PACK):
             project_t(2, ZH, ZH, t)
             attenuate(2, ZH, ZH, t)
-        for c in range(C):
-            for z in range(4):
+        for z in range(4):
+            for c in range(C):
                 detect(z, c, c == 0, c == C - 1)
-                if c == C - 1:
-                    store(z, "s")
+            store(z, "s")
         h_inter(2, ZH, 0, 256, "v")
         h_quant(1, ZH, 256)
         h_quant(2, ZH, 256)
         h_inter(1, ZH, 256, 256, "v")
         h_inter(2, ZH, 256, 128, "v")
-        for c in range(C):
-            for z in (4, 5):
+        for z in (4, 5):
+            for c in range(C):
                 detect(z, c, c == 0, c == C - 1)
-                if c == C - 1:
-                    store(z, "s")
+            store(z, "s")
         h_inter(2, ZH, 384, 128, "v")
         h_quant(1, ZH + 256, 256)
         h_quant(2, ZH + 256, 128)
         h_quant(2, ZH + 384, 128)
-        for c in range(C - 1):
-            for z in (6, 7):
-                for b0 in (0, 256):
+        for z in (6, 7):
+            for b0 in (0, 256):
+                for c in range(C - 1):
                     detect(z, c, c == 0, False, b0, 256)
         for z in (6, 7):
             for b0 in (0, 256):

@@ -18,17 +18,24 @@ AXIS = mybir.AxisListType
 
 P = 128
 PACK = 4
-KP = 512
+KP = P * PACK
 G = V // KP
 C = R // KP
-ZH = 512
-NH = Z // ZH
+ZH = Z // 2
+ZQ = ZH // 2
+TILES = ZH // P
+BH = B // 2
+RUN = 4
+F32_MAX = (2.0 - 2.0**-23) * 2.0**127
+
+F_RAW_BUFS = 3
+F_PAIR_BUFS = 2
 WIDE_BUFS = 7
-GRP_BUFS = 6
-CODE_BUFS = 12
+GROUPED_BUFS = 6
 PLANE_BUFS = 5
 Y_BUFS = 8
-SI = 4
+
+LN_RANGES = ((2.0**-126, 2.0**-63, 2.0**63), (2.0**-63, 2.0**64, 1.0), (2.0**64, F32_MAX, 2.0**-64))
 
 
 def tile_tomography_forward_transmission_d3_kernel(tc, F, S_bytes, S_scale, i0, D, out):
@@ -42,41 +49,34 @@ def tile_tomography_forward_transmission_d3_kernel(tc, F, S_bytes, S_scale, i0, 
         scale = keep.tile([P, G, PACK], F32, name="scale")
         i0_t = keep.tile([P, C, PACK], BF16, name="i0_t")
         s_view = S_bytes.rearrange("(g p j) n -> g p j n", p=P, j=PACK)
-        f_view = F.rearrange("(h z p) (g k) -> h g p z k", p=P, z=4, k=KP)
-        f_pairs = F.rearrange("(h z p) (g k) -> h g p z k", p=P, z=4, k=2 * KP)
+        f_view = F.rearrange("(h z p) (g k) -> h g p z k", p=P, z=TILES, k=KP)
+        f_pair_view = F.rearrange("(h z p) (g k) -> h g p z k", p=P, z=TILES, k=2 * KP)
         d_view = D.rearrange("(c p j) b -> c p j b", p=P, j=PACK)
         s_bytes, f_raw, d_raw = {}, {}, {}
 
-        def load_scale():
-            nc.sync.dma_start(out=scale[:], in_=S_scale.rearrange("(g p j) o -> p g (j o)", p=P, j=PACK))
-
-        def load_i0():
-            nc.sync.dma_start(out=i0_t[:], in_=i0.rearrange("(c p j) -> p c j", p=P, j=PACK))
-
-        def load_s_rows(j0):
-            tile = keep.tile([P, 2, KP + 32], U8, name="s_first_%d" % j0)
+        def load_s_first(j0):
+            tile = keep.tile([P, 2, KP], U8, name="s_first_%d" % j0)
             for j in (j0, j0 + 1):
-                s_bytes[0, 0, j] = tile[:, j - j0, 0:KP]
-            nc.sync.dma_start(out=tile[:, :, 0:KP], in_=s_view[0][:, j0 : j0 + 2, 0:KP])
+                s_bytes[0, 0, j] = tile[:, j - j0, :]
+            nc.sync.dma_start(out=tile[:], in_=s_view[0][:, j0 : j0 + 2, 0:KP])
 
         def load_s(g, c0, c1):
-            w = KP * (c1 - c0)
-            tile = keep.tile([P, PACK, w + 32], U8, name="s_bytes_%d_%d" % (g, c0))
+            tile = keep.tile([P, PACK, KP * (c1 - c0)], U8, name="s_bytes_%d_%d" % (g, c0))
             for c in range(c0, c1):
                 for j in range(PACK):
                     s_bytes[c, g, j] = tile[:, j, KP * (c - c0) : KP * (c - c0 + 1)]
-            nc.sync.dma_start(out=tile[:, :, 0:w], in_=s_view[g][:, :, KP * c0 : KP * c1])
+            nc.sync.dma_start(out=tile[:], in_=s_view[g][:, :, KP * c0 : KP * c1])
 
         def load_f(h, g):
-            tile = ring.tile([P, 4, KP], BF16, name="f_raw", bufs=3)
+            tile = ring.tile([P, TILES, KP], BF16, name="f_raw", bufs=F_RAW_BUFS)
             f_raw[h, g] = tile
             nc.sync.dma_start(out=tile[:], in_=f_view[h, g])
 
         def load_f_pair(h, g0):
-            tile = ring.tile([P, 4, 2 * KP], BF16, name="f_pair", bufs=2)
+            tile = ring.tile([P, TILES, 2 * KP], BF16, name="f_pair", bufs=F_PAIR_BUFS)
             for g in (g0, g0 + 1):
                 f_raw[h, g] = tile[:, :, KP * (g - g0) : KP * (g - g0 + 1)]
-            nc.sync.dma_start(out=tile[:], in_=f_pairs[h, g0 // 2])
+            nc.sync.dma_start(out=tile[:], in_=f_pair_view[h, g0 // 2])
 
         def load_d(c):
             tile = keep.tile([P, PACK, B], BF16, name="d_raw%d" % c)
@@ -85,155 +85,136 @@ def tile_tomography_forward_transmission_d3_kernel(tc, F, S_bytes, S_scale, i0, 
 
         ident = keep.tile([P, P], F32, name="ident")
 
-        def identities():
-            make_identity(nc, ident[:])
-
         i0_flat = i0_t[:].rearrange("p c j -> p (c j)")
         mag = keep.tile([P, C * PACK], F32, name="mag")
-        fac = keep.tile([P, 3, C * PACK], F32, name="fac")
-        lnf = keep.tile([P, 3, C * PACK], F32, name="lnf")
+        factors = keep.tile([P, len(LN_RANGES), C * PACK], F32, name="factors")
+        logs = keep.tile([P, len(LN_RANGES), C * PACK], F32, name="logs")
         ln_i0 = keep.tile([P, C * PACK], F32, name="ln_i0")
-        sgn2 = keep.tile([P, C * PACK], F32, name="sgn2")
+        sgn_plus_1 = keep.tile([P, C * PACK], F32, name="sgn_plus_1")
         sgn = keep.tile([P, C * PACK], F32, name="sgn")
-        unit = keep.tile([P, 1], F32, name="unit")
+        one = keep.tile([P, 1], F32, name="one")
         unread = keep.tile([P, 2], F32, name="unread")
-        RANGES = ((2.0**-126, 2.0**-63, 2.0**63), (2.0**-63, 2.0**63, 1.0), (2.0**63, 2.0**126, 2.0**-63))
-
-        def warm_ln():
-            nc.vector.memset(unit[:], 1.0)
-            nc.scalar.activation(out=unread[:, 0:1], in_=unit[:, 0:1], func=ACT.Ln)
-
-        def warm_exp():
-            nc.scalar.activation(out=unread[:, 1:2], in_=unit[:, 0:1], func=ACT.Exp)
 
         def i0_factors():
             nc.vector.scalar_tensor_tensor(out=mag[:], in0=i0_flat, scalar=-1.0, in1=i0_flat, op0=ALU.mult, op1=ALU.max)
-            nc.vector.tensor_scalar(out=sgn2[:], in0=i0_flat, scalar1=0.0, scalar2=2.0, op0=ALU.is_ge, op1=ALU.mult)
-            for k in range(3):
-                nc.vector.tensor_scalar(out=fac[:, k, :], in0=mag[:], scalar1=RANGES[k][0], scalar2=RANGES[k][1], op0=ALU.max, op1=ALU.min)
-            nc.vector.tensor_scalar(out=sgn[:], in0=sgn2[:], scalar1=-1.0, scalar2=None, op0=ALU.add)
+            nc.vector.tensor_scalar(out=sgn_plus_1[:], in0=i0_flat, scalar1=0.0, scalar2=2.0, op0=ALU.is_ge, op1=ALU.mult)
+            for k, (low, high, shift) in enumerate(LN_RANGES):
+                nc.vector.tensor_scalar(out=factors[:, k, :], in0=mag[:], scalar1=low, scalar2=high, op0=ALU.max, op1=ALU.min)
+            nc.vector.tensor_scalar(out=sgn[:], in0=sgn_plus_1[:], scalar1=-1.0, scalar2=None, op0=ALU.add)
 
         def i0_logs():
-            for k in range(3):
-                nc.scalar.activation(out=lnf[:, k, :], in_=fac[:, k, :], func=ACT.Ln, scale=RANGES[k][2])
+            for k, (low, high, shift) in enumerate(LN_RANGES):
+                nc.scalar.activation(out=logs[:, k, :], in_=factors[:, k, :], func=ACT.Ln, scale=shift)
 
         def i0_sum():
-            nc.vector.tensor_reduce(out=ln_i0[:], in_=lnf[:].rearrange("p k n -> p n k"), op=ALU.add, axis=AXIS.X)
+            nc.vector.tensor_reduce(out=ln_i0[:], in_=logs[:].rearrange("p k n -> p n k"), op=ALU.add, axis=AXIS.X)
 
-        def copy_on(eng, dst, src):
-            if eng == "v":
+        def copy_on(engine, dst, src):
+            if engine == "v":
                 nc.vector.tensor_copy(out=dst, in_=src)
             else:
                 nc.scalar.copy(out=dst, in_=src)
 
-        def quantize(codes, scales, src):
-            nc.vector.quantize_mx(out=codes.bitcast(FP8X4), scales=scales, in_=src)
+        def new_grouped(columns):
+            return ring.tile([P, PACK * columns], BF16, name="grouped", bufs=GROUPED_BUFS, align_bytes=64)
 
-        s_wide, s_grp, s_codes, s_scales, s_banks = {}, {}, {}, {}, {}
+        def interleave(engine, grouped, rows):
+            dst = grouped[:].rearrange("p (q i j) -> p q j i", i=RUN, j=PACK)
+            copy_on(engine, dst, rows.rearrange("p j (q i) -> p q j i", i=RUN))
 
-        def widen(c, g, j, eng):
+        def quantize(codes, scales, grouped):
+            nc.vector.quantize_mx(out=codes[:].bitcast(FP8X4), scales=scales[:], in_=grouped[:])
+
+        s_wide, s_grouped, s_codes, s_scales = {}, {}, {}, {}
+
+        def widen(c, g, engines):
             if (c, g) not in s_wide:
                 s_wide[c, g] = ring.tile([P, PACK, KP], BF16, name="s_wide", bufs=WIDE_BUFS, align_bytes=64)
-            src = s_bytes[c, g, j].bitcast(FP8)
-            dst = s_wide[c, g][:, j, :]
-            if eng == "v":
-                nc.vector.tensor_scalar(out=dst, in0=src, scalar1=scale[:, g, j : j + 1], scalar2=None, op0=ALU.mult)
-            else:
-                nc.scalar.activation(out=dst, in_=src, func=ACT.Copy, scale=scale[:, g, j : j + 1])
-
-        def widen_pairs(c, g):
-            s_wide[c, g] = ring.tile([P, 2, 2 * KP], BF16, name="s_wide", bufs=WIDE_BUFS, align_bytes=64)
             for j in range(PACK):
                 src = s_bytes[c, g, j].bitcast(FP8)
-                dst = s_wide[c, g][:, j // 2, :].rearrange("p (t m e) -> p m t e", t=4, e=2)[:, :, :, j % 2]
-                nc.vector.tensor_scalar(out=dst, in0=src, scalar1=scale[:, g, j : j + 1], scalar2=None, op0=ALU.mult)
+                dst = s_wide[c, g][:, j, :]
+                if engines[j] == "v":
+                    nc.vector.tensor_scalar(out=dst, in0=src, scalar1=scale[:, g, j : j + 1], scalar2=None, op0=ALU.mult)
+                elif engines[j] == "s":
+                    nc.scalar.activation(out=dst, in_=src, func=ACT.Copy, scale=scale[:, g, j : j + 1])
 
-        def join_pairs(c, g, eng):
-            src = s_wide[c, g][:].bitcast(F32).rearrange("p u n -> p n u")
-            dst = new_s_grp(c, g)[:].bitcast(F32).rearrange("p (n u) -> p n u", u=2)
-            copy_on(eng, dst, src)
-
-        def new_s_grp(c, g):
-            if (c, g) not in s_grp:
-                s_grp[c, g] = ring.tile([P, PACK * KP], BF16, name="grp", bufs=GRP_BUFS, align_bytes=64)
-            return s_grp[c, g]
-
-        def s_inter(c, g):
-            src = s_wide[c, g][:].rearrange("p j (q i t) -> p t q j i", i=SI, t=4)
-            dst = new_s_grp(c, g)[:].rearrange("p (t q i j) -> p t q j i", t=4, i=SI, j=4)
+        def s_interleave(c, g):
+            s_grouped[c, g] = new_grouped(KP)
+            src = s_wide[c, g][:].rearrange("p j (q i t) -> p t q j i", i=RUN, t=PACK)
+            dst = s_grouped[c, g][:].rearrange("p (t q i j) -> p t q j i", t=PACK, i=RUN, j=PACK)
             nc.vector.tensor_copy(out=dst, in_=src)
 
         def s_quant(c, g):
-            s_codes[c, g] = ring.tile([P, KP], U32, name="s_codes", bufs=CODE_BUFS, align_bytes=64)
-            s_scales[c, g] = ring.tile([P, KP], U8, name="s_scales", bufs=CODE_BUFS, align_bytes=64)
-            quantize(s_codes[c, g][:], s_scales[c, g][:], s_grp[c, g][:])
+            s_codes[c, g] = ring.tile([P, KP], U32, name="s_codes", bufs=C * G, align_bytes=64)
+            s_scales[c, g] = ring.tile([P, KP], U8, name="s_scales", bufs=C * G, align_bytes=64)
+            quantize(s_codes[c, g], s_scales[c, g], s_grouped[c, g])
 
-        f_banks, f_grp, f_codes, f_scales = {}, {}, {}, {}
+        f_grouped, f_codes, f_scales = {}, {}, {}
 
-        def f_turn(h, g, z):
-            b, zz = divmod(z, 2)
-            if zz == 0:
-                f_banks[h, g, b] = psum.tile([P, KP], F32, name="bank")
-            words = f_raw[h, g][:, z, :].bitcast(F32)
-            for u in range(2):
-                nc.tensor.transpose(f_banks[h, g, b][:, (2 * zz + u) * P : (2 * zz + u + 1) * P], words[:, u : 2 * P : 2], ident[:])
-
-        def f_drain(h, g, b, eng):
-            if b == 0:
-                f_grp[h, g] = ring.tile([P, PACK * ZH], BF16, name="grp", bufs=GRP_BUFS, align_bytes=64)
-            dst = f_grp[h, g][:].bitcast(F32)[:, KP * b : KP * (b + 1)]
-            copy_on(eng, dst.rearrange("p (z r u) -> p z r u", z=2, u=2), f_banks[h, g, b][:].rearrange("p (z u r) -> p z r u", z=2, u=2))
+        def turn(h, g):
+            banks = []
+            for z in range(TILES):
+                if z % 2 == 0:
+                    banks.append(psum.tile([P, KP], F32, name="bank"))
+                words = f_raw[h, g][:, z, :].bitcast(F32)
+                for u in range(2):
+                    column = (2 * (z % 2) + u) * P
+                    nc.tensor.transpose(banks[-1][:, column : column + P], words[:, u : 2 * P : 2], ident[:])
+            f_grouped[h, g] = new_grouped(ZH)
+            for b, bank in enumerate(banks):
+                dst = f_grouped[h, g][:].bitcast(F32)[:, KP * b : KP * (b + 1)]
+                nc.scalar.copy(
+                    out=dst.rearrange("p (z r u) -> p z r u", z=2, u=2), in_=bank[:].rearrange("p (z u r) -> p z r u", z=2, u=2)
+                )
 
         def f_quant(h, g):
             f_codes[h, g] = keep.tile([P, ZH], U32, name="f_codes%d_%d" % (h, g), align_bytes=64)
             f_scales[h, g] = keep.tile([P, ZH], U8, name="f_scales%d_%d" % (h, g), align_bytes=64)
-            quantize(f_codes[h, g][:], f_scales[h, g][:], f_grp[h, g][:])
+            quantize(f_codes[h, g], f_scales[h, g], f_grouped[h, g])
 
-        p_banks, h_planes, h_grp, h_codes, h_scales = {}, {}, {}, {}, {}
+        p_banks, h_rows, h_grouped, h_codes, h_scales = {}, {}, {}, {}, {}
 
-        def project(c, z0, w, t, g):
-            if g == 0:
-                p_banks[c, z0, t] = psum.tile([P, KP], F32, name="bank")
+        def project(c, h, slices, passes):
+            for t in slices:
+                for g in passes:
+                    if g == 0:
+                        p_banks[c, h, t] = psum.tile([P, ZH], F32, name="bank")
+                    nc.tensor.matmul_mx(
+                        out=p_banks[c, h, t][:],
+                        lhsT=s_codes[c, g][:, P * t : P * (t + 1)].bitcast(FP8X4),
+                        lhsT_scale=s_scales[c, g][:, P * t : P * (t + 1)],
+                        rhs=f_codes[h, g][:].bitcast(FP8X4),
+                        rhs_scale=f_scales[h, g][:],
+                        start=(g == 0),
+                        stop=(g == G - 1),
+                    )
+
+        def attenuate(c, h, slices):
+            for t in slices:
+                if t == 0:
+                    h_rows[c, h] = ring.tile([P, PACK, ZH], BF16, name="h_rows", bufs=PLANE_BUFS, align_bytes=64)
+                nc.scalar.activation(
+                    out=h_rows[c, h][:, t, :],
+                    in_=p_banks[c, h, t][:],
+                    func=ACT.Exp,
+                    bias=ln_i0[:, PACK * c + t : PACK * c + t + 1],
+                    scale=-1.0,
+                )
+
+        def h_interleave(c, z0, w, engine):
             h, z1 = divmod(z0, ZH)
-            nc.tensor.matmul_mx(
-                out=p_banks[c, z0, t][:, 0:w],
-                lhsT=s_codes[c, g][:, P * t : P * (t + 1)].bitcast(FP8X4),
-                lhsT_scale=s_scales[c, g][:, P * t : P * (t + 1)],
-                rhs=f_codes[h, g][:, z1 : z1 + w].bitcast(FP8X4),
-                rhs_scale=f_scales[h, g][:, z1 : z1 + w],
-                start=(g == 0),
-                stop=(g == G - 1),
-            )
+            h_grouped[c, z0] = new_grouped(w)
+            interleave(engine, h_grouped[c, z0], h_rows[c, h][:, :, z1 : z1 + w])
 
-        def project_t(c, z0, w, t):
-            for g in range(G):
-                project(c, z0, w, t, g)
-
-        def attenuate(c, z0, w, t):
-            if t == 0:
-                h_planes[c, z0] = ring.tile([P, PACK, w], BF16, name="h_plane", bufs=PLANE_BUFS, align_bytes=64)
-            nc.scalar.activation(
-                out=h_planes[c, z0][:, t, :],
-                in_=p_banks[c, z0, t][:, 0:w],
-                func=ACT.Exp,
-                bias=ln_i0[:, PACK * c + t : PACK * c + t + 1],
-                scale=-1.0,
-            )
-
-        def h_inter(c, z0, z1, w, eng):
-            h_grp[c, z0 + z1] = ring.tile([P, PACK * w], BF16, name="grp", bufs=GRP_BUFS, align_bytes=64)
-            src = h_planes[c, z0][:, :, z1 : z1 + w].rearrange("p j (q i) -> p q j i", i=4)
-            copy_on(eng, h_grp[c, z0 + z1][:].rearrange("p (q i j) -> p q j i", i=4, j=4), src)
-
-        def h_quant(c, z, w):
-            codes = keep.tile([P, w], U32, name="h_codes%d_%d" % (c, z), align_bytes=64)
-            scales = keep.tile([P, w], U8, name="h_scales%d_%d" % (c, z), align_bytes=64)
+        def h_quant(c, z0, w):
+            codes = keep.tile([P, w], U32, name="h_codes%d_%d" % (c, z0), align_bytes=64)
+            scales = keep.tile([P, w], U8, name="h_scales%d_%d" % (c, z0), align_bytes=64)
             for k in range(w // P):
-                h_codes[c, z // P + k] = codes[:, P * k : P * (k + 1)]
-                h_scales[c, z // P + k] = scales[:, P * k : P * (k + 1)]
-            quantize(codes[:], scales[:], h_grp[c, z][:])
+                h_codes[c, z0 // P + k] = codes[:, P * k : P * (k + 1)]
+                h_scales[c, z0 // P + k] = scales[:, P * k : P * (k + 1)]
+            quantize(codes, scales, h_grouped[c, z0])
 
-        d_grp, d_codes, d_scales = {}, {}, {}
+        d_grouped, d_codes, d_scales = {}, {}, {}
 
         def d_sign(c):
             for j in range(PACK):
@@ -241,203 +222,177 @@ def tile_tomography_forward_transmission_d3_kernel(tc, F, S_bytes, S_scale, i0, 
                     out=d_raw[c][:, j, :], in0=d_raw[c][:, j, :], scalar1=sgn[:, PACK * c + j : PACK * c + j + 1], scalar2=None, op0=ALU.mult
                 )
 
-        def d_inter(c, eng):
-            d_grp[c] = ring.tile([P, PACK * B], BF16, name="grp", bufs=GRP_BUFS, align_bytes=64)
-            copy_on(eng, d_grp[c][:].rearrange("p (q i j) -> p q j i", i=4, j=4), d_raw[c][:].rearrange("p j (q i) -> p q j i", i=4))
+        def d_interleave(c):
+            d_grouped[c] = new_grouped(B)
+            interleave("v", d_grouped[c], d_raw[c][:])
 
         def d_quant(c):
             d_codes[c] = keep.tile([P, B], U32, name="d_codes%d" % c, align_bytes=64)
             d_scales[c] = keep.tile([P, B], U8, name="d_scales%d" % c, align_bytes=64)
-            quantize(d_codes[c][:], d_scales[c][:], d_grp[c][:])
+            quantize(d_codes[c], d_scales[c], d_grouped[c])
 
         y_banks = {}
 
-        def detect(z, c, first, last, b0=0, w=B):
-            if first:
-                y_banks[z, b0] = psum.tile([P, B], F32, name="bank")
-            nc.tensor.matmul_mx(
-                out=y_banks[z, b0][:, 0:w],
-                lhsT=h_codes[c, z].bitcast(FP8X4),
-                lhsT_scale=h_scales[c, z],
-                rhs=d_codes[c][:, b0 : b0 + w].bitcast(FP8X4),
-                rhs_scale=d_scales[c][:, b0 : b0 + w],
-                start=first,
-                stop=last,
-            )
+        def detect(z, groups, b0, w):
+            for c in groups:
+                if c == 0:
+                    y_banks[z, b0] = psum.tile([P, B], F32, name="bank")
+                nc.tensor.matmul_mx(
+                    out=y_banks[z, b0][:, 0:w],
+                    lhsT=h_codes[c, z].bitcast(FP8X4),
+                    lhsT_scale=h_scales[c, z],
+                    rhs=d_codes[c][:, b0 : b0 + w].bitcast(FP8X4),
+                    rhs_scale=d_scales[c][:, b0 : b0 + w],
+                    start=(c == 0),
+                    stop=(c == C - 1),
+                )
 
-        def store(z, eng, b0=0, w=B, queue=nc.sync):
+        def store(z, b0, w, engine):
             y_tile = ring.tile([P, w], F32, name="y_tile", bufs=Y_BUFS)
-            copy_on(eng, y_tile[:], y_banks[z, b0][:, 0:w])
-            queue.dma_start(out=out[P * z : P * (z + 1), b0 : b0 + w], in_=y_tile[:])
+            copy_on(engine, y_tile[:], y_banks[z, b0][:, 0:w])
+            nc.sync.dma_start(out=out[P * z : P * (z + 1), b0 : b0 + w], in_=y_tile[:])
 
-        def widen_rows(c, g, engs):
-            for j in range(PACK):
-                if engs[j] != "-":
-                    widen(c, g, j, engs[j])
-
-        def turn(h, g):
-            for k in range(4):
-                f_turn(h, g, k)
-
-        def drain(h, g):
-            for b in range(2):
-                f_drain(h, g, b, "s")
-
-        def project_pairs(c, z0, ts, g0):
-            for t in ts:
-                project(c, z0, ZH, t, g0)
-                project(c, z0, ZH, t, g0 + 1)
-
-        load_scale()
-        load_i0()
-        load_s_rows(0)
-        load_s_rows(2)
-        for g in range(G):
-            if g > 0:
-                load_s(g, 0, 1)
+        nc.sync.dma_start(out=scale[:], in_=S_scale.rearrange("(g p j) o -> p g (j o)", p=P, j=PACK))
+        nc.sync.dma_start(out=i0_t[:], in_=i0.rearrange("(c p j) -> p c j", p=P, j=PACK))
+        load_s_first(0)
+        load_s_first(2)
+        load_f(0, 0)
+        for g in range(1, G):
+            load_s(g, 0, 1)
             load_f(0, g)
-        load_s(0, 1, C)
-        load_f_pair(1, 0)
-        load_s(1, 1, C)
-        load_f_pair(1, 2)
-        load_s(2, 1, C)
-        load_s(3, 1, C)
+        for g in range(G):
+            load_s(g, 1, C)
+            if g < G // 2:
+                load_f_pair(1, 2 * g)
         for c in range(C):
             load_d(c)
-        warm_ln()
-        identities()
+
+        nc.vector.memset(one[:], 1.0)
+        nc.scalar.activation(out=unread[:, 0:1], in_=one[:], func=ACT.Ln)
+        make_identity(nc, ident[:])
         i0_factors()
         i0_logs()
-        warm_exp()
-        widen_rows(0, 0, "vvvv")
+        nc.scalar.activation(out=unread[:, 1:2], in_=one[:], func=ACT.Exp)
+
+        widen(0, 0, "vvvv")
         i0_sum()
-        s_inter(0, 0)
-        widen_rows(0, 1, "vvss")
+        s_interleave(0, 0)
+        widen(0, 1, "vvss")
         turn(0, 0)
-        drain(0, 0)
         s_quant(0, 0)
-        s_inter(0, 1)
-        widen_rows(0, 2, "vvss")
+        s_interleave(0, 1)
+        widen(0, 2, "vvss")
         turn(0, 1)
-        drain(0, 1)
         s_quant(0, 1)
         f_quant(0, 0)
-        s_inter(0, 2)
+        s_interleave(0, 2)
         turn(0, 2)
-        drain(0, 2)
-        widen_rows(0, 3, "vsss")
+        widen(0, 3, "vsss")
         f_quant(0, 1)
         s_quant(0, 2)
+
         turn(0, 3)
-        drain(0, 3)
-        project_pairs(0, 0, (0, 1), 0)
+        project(0, 0, (0, 1), (0, 1))
         f_quant(0, 2)
-        s_inter(0, 3)
-        widen_rows(1, 0, "vsss")
+        s_interleave(0, 3)
+        widen(1, 0, "vsss")
         f_quant(0, 3)
         s_quant(0, 3)
-        widen_rows(2, 0, "--s-")
+        widen(2, 0, "--s-")
         turn(1, 0)
-        drain(1, 0)
-        project_pairs(0, 0, (2, 3), 0)
-        s_inter(1, 0)
-        widen_rows(1, 1, "vvss")
+        project(0, 0, (2, 3), (0, 1))
+        s_interleave(1, 0)
+        widen(1, 1, "vvss")
         turn(1, 1)
-        drain(1, 1)
-        project_pairs(0, 0, (0, 1), 2)
+        project(0, 0, (0, 1), (2, 3))
         s_quant(1, 0)
         f_quant(1, 0)
-        s_inter(1, 1)
-        widen_rows(1, 2, "vvss")
+        s_interleave(1, 1)
+        widen(1, 2, "vvss")
         turn(1, 2)
-        drain(1, 2)
-        project_pairs(0, 0, (2, 3), 2)
+        project(0, 0, (2, 3), (2, 3))
         f_quant(1, 1)
         s_quant(1, 1)
-        s_inter(1, 2)
-        widen_rows(1, 3, "vvss")
+        s_interleave(1, 2)
+        widen(1, 3, "vvss")
         turn(1, 3)
-        drain(1, 3)
-        for t in range(PACK):
-            attenuate(0, 0, ZH, t)
+        attenuate(0, 0, range(PACK))
         f_quant(1, 2)
         s_quant(1, 2)
         f_quant(1, 3)
-        s_inter(1, 3)
-        for g0 in (0, 2):
-            project_pairs(0, ZH, range(PACK), g0)
-        widen_rows(2, 0, "vv-s")
+        s_interleave(1, 3)
+
+        project(0, 1, range(PACK), (0, 1))
+        project(0, 1, range(PACK), (2, 3))
+        widen(2, 0, "vv-s")
         s_quant(1, 3)
-        s_inter(2, 0)
-        widen_rows(2, 1, "vvss")
-        attenuate(0, ZH, ZH, 0)
-        attenuate(0, ZH, ZH, 1)
+        s_interleave(2, 0)
+        widen(2, 1, "vvss")
+        attenuate(0, 1, (0, 1))
         s_quant(2, 0)
-        s_inter(2, 1)
-        widen_rows(2, 2, "vsss")
-        attenuate(0, ZH, ZH, 2)
-        attenuate(0, ZH, ZH, 3)
-        for t in range(PACK):
-            project_t(1, 0, ZH, t)
-        widen_rows(2, 3, "vsss")
+        s_interleave(2, 1)
+        widen(2, 2, "vsss")
+        attenuate(0, 1, (2, 3))
+
+        project(1, 0, range(PACK), range(G))
+        widen(2, 3, "vsss")
         s_quant(2, 1)
-        s_inter(2, 2)
+        s_interleave(2, 2)
         d_sign(0)
         s_quant(2, 2)
-        s_inter(2, 3)
+        s_interleave(2, 3)
         d_sign(1)
         s_quant(2, 3)
-        d_inter(0, "v")
-        d_inter(1, "v")
+        d_interleave(0)
+        d_interleave(1)
         d_quant(0)
         d_sign(2)
         d_quant(1)
-        d_inter(2, "v")
+        d_interleave(2)
+        attenuate(1, 0, range(PACK))
+        h_interleave(0, 0, ZH, "s")
         for t in range(PACK):
-            attenuate(1, 0, ZH, t)
-        h_inter(0, 0, 0, ZH, "s")
+            project(1, 1, (t,), range(G))
+            attenuate(1, 1, (t,))
+
         for t in range(PACK):
-            project_t(1, ZH, ZH, t)
-            attenuate(1, ZH, ZH, t)
-        for t in range(PACK):
-            project_t(2, 0, ZH, t)
-            attenuate(2, 0, ZH, t)
-        h_inter(0, ZH, 0, ZH, "s")
-        h_inter(1, 0, 0, ZH, "v")
+            project(2, 0, (t,), range(G))
+            attenuate(2, 0, (t,))
+        h_interleave(0, ZH, ZH, "s")
+        h_interleave(1, 0, ZH, "v")
         d_quant(2)
-        h_inter(2, 0, 0, 256, "v")
+        h_interleave(2, 0, ZQ, "v")
         h_quant(0, 0, ZH)
         h_quant(1, 0, ZH)
-        h_quant(2, 0, 256)
-        h_inter(2, 0, 256, 256, "v")
-        h_inter(1, ZH, 0, 256, "v")
-        h_quant(2, 256, 256)
+        h_quant(2, 0, ZQ)
+        h_interleave(2, ZQ, ZQ, "v")
+        h_interleave(1, ZH, ZQ, "v")
+        h_quant(2, ZQ, ZQ)
         h_quant(0, ZH, ZH)
         for t in range(PACK):
-            project_t(2, ZH, ZH, t)
-            attenuate(2, ZH, ZH, t)
-        for z in range(4):
-            for c in range(C):
-                detect(z, c, c == 0, c == C - 1)
-            store(z, "s")
-        h_inter(2, ZH, 0, 256, "v")
-        h_quant(1, ZH, 256)
-        h_quant(2, ZH, 256)
-        h_inter(1, ZH, 256, 256, "v")
-        h_inter(2, ZH, 256, 128, "v")
-        for z in (4, 5):
-            for c in range(C):
-                detect(z, c, c == 0, c == C - 1)
-            store(z, "s")
-        h_inter(2, ZH, 384, 128, "v")
-        h_quant(1, ZH + 256, 256)
-        h_quant(2, ZH + 256, 128)
-        h_quant(2, ZH + 384, 128)
-        for z in (6, 7):
-            for b0 in (0, 256):
-                for c in range(C - 1):
-                    detect(z, c, c == 0, False, b0, 256)
-        for z in (6, 7):
-            for b0 in (0, 256):
-                detect(z, C - 1, False, True, b0, 256)
-                store(z, "v" if b0 == 0 else "s", b0, 256)
+            project(2, 1, (t,), range(G))
+            attenuate(2, 1, (t,))
+
+        for z in range(TILES):
+            detect(z, range(C), 0, B)
+            store(z, 0, B, "s")
+        h_interleave(2, ZH, ZQ, "v")
+        h_quant(1, ZH, ZQ)
+        h_quant(2, ZH, ZQ)
+        h_interleave(1, ZH + ZQ, ZQ, "v")
+        h_interleave(2, ZH + ZQ, P, "v")
+        for z in (TILES, TILES + 1):
+            detect(z, range(C), 0, B)
+            store(z, 0, B, "s")
+        h_interleave(2, Z - P, P, "v")
+        h_quant(1, ZH + ZQ, ZQ)
+        h_quant(2, ZH + ZQ, P)
+        h_quant(2, Z - P, P)
+        last_tiles = (TILES + 2, TILES + 3)
+        for z in last_tiles:
+            for b0 in (0, BH):
+                detect(z, range(C - 1), b0, BH)
+        for z in last_tiles:
+            for b0, engine in ((0, "v"), (BH, "s")):
+                detect(z, (C - 1,), b0, BH)
+                store(z, b0, BH, engine)

@@ -43,10 +43,12 @@ def tile_tomography_forward_transmission_d3_kernel(tc, F, S_bytes, S_scale, i0, 
     with ExitStack() as ctx:
         keep = ctx.enter_context(tc.tile_pool(name="keep", bufs=1))
         ring = ctx.enter_context(tc.tile_pool(name="ring", bufs=1))
-        psum = ctx.enter_context(tc.psum_pool(name="psum", bufs=8))
+        psum = ctx.enter_context(tc.psum_pool(name="psum", bufs=1))
         ctx.enter_context(tc.manual_schedule())
 
-        scale = keep.tile([P, G, PACK], F32, name="scale")
+        scale_first = keep.tile([P, 1, PACK], F32, name="scale_first")
+        scale_rest = keep.tile([P, G - 1, PACK], F32, name="scale_rest")
+        scale_view = S_scale.rearrange("(g p j) o -> p g (j o)", p=P, j=PACK)
         i0_t = keep.tile([P, C, PACK], BF16, name="i0_t")
         s_view = S_bytes.rearrange("(g p j) n -> g p j n", p=P, j=PACK)
         f_view = F.rearrange("(h z p) (g k) -> h g p z k", p=P, z=TILES, k=KP)
@@ -84,6 +86,9 @@ def tile_tomography_forward_transmission_d3_kernel(tc, F, S_bytes, S_scale, i0, 
             nc.sync.dma_start(out=tile[:], in_=d_view[c])
 
         ident = keep.tile([P, P], F32, name="ident")
+
+        def new_bank(n):
+            return psum.tile([P, KP], F32, name="bank%d" % n)
 
         i0_flat = i0_t[:].rearrange("p c j -> p (c j)")
         mag = keep.tile([P, C * PACK], F32, name="mag")
@@ -133,10 +138,11 @@ def tile_tomography_forward_transmission_d3_kernel(tc, F, S_bytes, S_scale, i0, 
             for j in range(PACK):
                 src = s_bytes[c, g, j].bitcast(FP8)
                 dst = s_wide[c, g][:, j, :]
+                scale = scale_first[:, 0, j : j + 1] if g == 0 else scale_rest[:, g - 1, j : j + 1]
                 if engines[j] == "v":
-                    nc.vector.tensor_scalar(out=dst, in0=src, scalar1=scale[:, g, j : j + 1], scalar2=None, op0=ALU.mult)
+                    nc.vector.tensor_scalar(out=dst, in0=src, scalar1=scale, scalar2=None, op0=ALU.mult)
                 elif engines[j] == "s":
-                    nc.scalar.activation(out=dst, in_=src, func=ACT.Copy, scale=scale[:, g, j : j + 1])
+                    nc.scalar.activation(out=dst, in_=src, func=ACT.Copy, scale=scale)
 
         def s_interleave(c, g):
             s_grouped[c, g] = new_grouped(KP)
@@ -151,17 +157,22 @@ def tile_tomography_forward_transmission_d3_kernel(tc, F, S_bytes, S_scale, i0, 
 
         f_grouped, f_codes, f_scales = {}, {}, {}
 
+        f_banks = {}
+
         def turn(h, g):
             banks = []
+            f_banks[h, g] = banks
             for z in range(TILES):
                 if z % 2 == 0:
-                    banks.append(psum.tile([P, KP], F32, name="bank"))
+                    banks.append(new_bank(PACK + 2 * (g % 2) + z // 2))
                 words = f_raw[h, g][:, z, :].bitcast(F32)
                 for u in range(2):
                     column = (2 * (z % 2) + u) * P
                     nc.tensor.transpose(banks[-1][:, column : column + P], words[:, u : 2 * P : 2], ident[:])
+
+        def f_copy(h, g):
             f_grouped[h, g] = new_grouped(ZH)
-            for b, bank in enumerate(banks):
+            for b, bank in enumerate(f_banks[h, g]):
                 dst = f_grouped[h, g][:].bitcast(F32)[:, KP * b : KP * (b + 1)]
                 nc.scalar.copy(
                     out=dst.rearrange("p (z r u) -> p z r u", z=2, u=2), in_=bank[:].rearrange("p (z u r) -> p z r u", z=2, u=2)
@@ -174,11 +185,18 @@ def tile_tomography_forward_transmission_d3_kernel(tc, F, S_bytes, S_scale, i0, 
 
         p_banks, h_rows, h_grouped, h_codes, h_scales = {}, {}, {}, {}, {}
 
+        def p_bank(c, h, t):
+            if (c, h) == (0, 1):
+                return (0, 1, 4, 5)[t]
+            if (c, h) == (1, 0):
+                return (2, 3, 6, 7)[t]
+            return (0, 1, 4, 5)[t] if h == 1 else (2, 3, 6, 7)[t] if c > 0 else t
+
         def project(c, h, slices, passes):
             for t in slices:
                 for g in passes:
                     if g == 0:
-                        p_banks[c, h, t] = psum.tile([P, ZH], F32, name="bank")
+                        p_banks[c, h, t] = new_bank(p_bank(c, h, t))
                     nc.tensor.matmul_mx(
                         out=p_banks[c, h, t][:],
                         lhsT=s_codes[c, g][:, P * t : P * (t + 1)].bitcast(FP8X4),
@@ -191,7 +209,7 @@ def tile_tomography_forward_transmission_d3_kernel(tc, F, S_bytes, S_scale, i0, 
 
         def attenuate(c, h, slices):
             for t in slices:
-                if t == 0:
+                if (c, h) not in h_rows:
                     h_rows[c, h] = ring.tile([P, PACK, ZH], BF16, name="h_rows", bufs=PLANE_BUFS, align_bytes=64)
                 nc.scalar.activation(
                     out=h_rows[c, h][:, t, :],
@@ -233,10 +251,10 @@ def tile_tomography_forward_transmission_d3_kernel(tc, F, S_bytes, S_scale, i0, 
 
         y_banks = {}
 
-        def detect(z, groups, b0, w):
+        def detect(z, groups, b0, w, bank):
             for c in groups:
                 if c == 0:
-                    y_banks[z, b0] = psum.tile([P, B], F32, name="bank")
+                    y_banks[z, b0] = new_bank(bank)
                 nc.tensor.matmul_mx(
                     out=y_banks[z, b0][:, 0:w],
                     lhsT=h_codes[c, z].bitcast(FP8X4),
@@ -252,11 +270,12 @@ def tile_tomography_forward_transmission_d3_kernel(tc, F, S_bytes, S_scale, i0, 
             copy_on(engine, y_tile[:], y_banks[z, b0][:, 0:w])
             nc.sync.dma_start(out=out[P * z : P * (z + 1), b0 : b0 + w], in_=y_tile[:])
 
-        nc.sync.dma_start(out=scale[:], in_=S_scale.rearrange("(g p j) o -> p g (j o)", p=P, j=PACK))
         nc.sync.dma_start(out=i0_t[:], in_=i0.rearrange("(c p j) -> p c j", p=P, j=PACK))
+        nc.sync.dma_start(out=scale_first[:], in_=scale_view[:, 0:1, :])
         load_s_first(0)
         load_s_first(2)
         load_f(0, 0)
+        nc.sync.dma_start(out=scale_rest[:], in_=scale_view[:, 1:G, :])
         for g in range(1, G):
             load_s(g, 0, 1)
             load_f(0, g)
@@ -271,128 +290,133 @@ def tile_tomography_forward_transmission_d3_kernel(tc, F, S_bytes, S_scale, i0, 
         nc.scalar.activation(out=unread[:, 0:1], in_=one[:], func=ACT.Ln)
         make_identity(nc, ident[:])
         i0_factors()
+        widen(0, 0, "vsvv")
         i0_logs()
         nc.scalar.activation(out=unread[:, 1:2], in_=one[:], func=ACT.Exp)
-
-        widen(0, 0, "vvvv")
         i0_sum()
         s_interleave(0, 0)
-        widen(0, 1, "vvss")
         turn(0, 0)
+        f_copy(0, 0)
         s_quant(0, 0)
-        s_interleave(0, 1)
-        widen(0, 2, "vvss")
-        turn(0, 1)
-        s_quant(0, 1)
+        widen(0, 1, "vvvs")
         f_quant(0, 0)
+        s_interleave(0, 1)
+        turn(0, 1)
+        project(0, 0, (0, 1), (0,))
+        widen(0, 2, "vvss")
+        f_copy(0, 1)
+        s_quant(0, 1)
         s_interleave(0, 2)
-        turn(0, 2)
-        widen(0, 3, "vsss")
         f_quant(0, 1)
+        turn(0, 2)
+        project(0, 0, (2, 3), (0,))
+        f_copy(0, 2)
+        widen(0, 3, "vsss")
         s_quant(0, 2)
-
-        turn(0, 3)
-        project(0, 0, (0, 1), (0, 1))
         f_quant(0, 2)
+        turn(0, 3)
+        f_copy(0, 3)
+        project(0, 0, range(PACK), (1, 2))
         s_interleave(0, 3)
         widen(1, 0, "vsss")
         f_quant(0, 3)
         s_quant(0, 3)
         widen(2, 0, "--s-")
         turn(1, 0)
-        project(0, 0, (2, 3), (0, 1))
+        f_copy(1, 0)
+        project(0, 0, (0, 1), (3,))
         s_interleave(1, 0)
         widen(1, 1, "vvss")
         turn(1, 1)
-        project(0, 0, (0, 1), (2, 3))
+        f_copy(1, 1)
+        project(0, 0, (2, 3), (3,))
         s_quant(1, 0)
         f_quant(1, 0)
         s_interleave(1, 1)
-        widen(1, 2, "vvss")
-        turn(1, 2)
-        project(0, 0, (2, 3), (2, 3))
         f_quant(1, 1)
+        turn(1, 2)
+        attenuate(0, 0, (0, 1))
+        f_copy(1, 2)
+        project(0, 1, (0, 1), (0, 1))
+        widen(1, 2, "vvvs")
         s_quant(1, 1)
-        s_interleave(1, 2)
-        widen(1, 3, "vvss")
-        turn(1, 3)
-        attenuate(0, 0, range(PACK))
         f_quant(1, 2)
-        s_quant(1, 2)
+        turn(1, 3)
+        f_copy(1, 3)
+        attenuate(0, 0, (2, 3))
+        s_interleave(1, 2)
+        widen(1, 3, "vvvs")
         f_quant(1, 3)
+        s_quant(1, 2)
+        project(0, 1, (0, 1), (2,))
+        project(0, 1, (2, 3), (0, 1, 2))
+        project(0, 1, range(PACK), (3,))
+        project(1, 0, range(PACK), (0, 1, 2))
         s_interleave(1, 3)
-
-        project(0, 1, range(PACK), (0, 1))
-        project(0, 1, range(PACK), (2, 3))
         widen(2, 0, "vv-s")
         s_quant(1, 3)
-        s_interleave(2, 0)
+        project(1, 0, range(PACK), (3,))
         widen(2, 1, "vvss")
         attenuate(0, 1, (0, 1))
+        s_interleave(2, 0)
+        attenuate(0, 1, (2, 3))
+        widen(2, 2, "vsss")
         s_quant(2, 0)
         s_interleave(2, 1)
-        widen(2, 2, "vsss")
-        attenuate(0, 1, (2, 3))
-
-        project(1, 0, range(PACK), range(G))
         widen(2, 3, "vsss")
         s_quant(2, 1)
         s_interleave(2, 2)
-        d_sign(0)
-        s_quant(2, 2)
         s_interleave(2, 3)
-        d_sign(1)
+        s_quant(2, 2)
         s_quant(2, 3)
+        for c in range(C):
+            d_sign(c)
         d_interleave(0)
         d_interleave(1)
         d_quant(0)
-        d_sign(2)
-        d_quant(1)
         d_interleave(2)
+        d_quant(1)
         attenuate(1, 0, range(PACK))
         h_interleave(0, 0, ZH, "s")
         for t in range(PACK):
             project(1, 1, (t,), range(G))
             attenuate(1, 1, (t,))
-
         for t in range(PACK):
             project(2, 0, (t,), range(G))
             attenuate(2, 0, (t,))
-        h_interleave(0, ZH, ZH, "s")
-        h_interleave(1, 0, ZH, "v")
+        h_interleave(1, 0, ZH, "s")
+        h_quant(0, 0, ZH)
         d_quant(2)
         h_interleave(2, 0, ZQ, "v")
-        h_quant(0, 0, ZH)
         h_quant(1, 0, ZH)
         h_quant(2, 0, ZQ)
         h_interleave(2, ZQ, ZQ, "v")
-        h_interleave(1, ZH, ZQ, "v")
+        h_interleave(0, ZH, ZQ, "v")
         h_quant(2, ZQ, ZQ)
-        h_quant(0, ZH, ZH)
         for t in range(PACK):
             project(2, 1, (t,), range(G))
             attenuate(2, 1, (t,))
-
-        for z in range(TILES):
-            detect(z, range(C), 0, B)
-            store(z, 0, B, "s")
+        h_interleave(1, ZH, ZQ, "v")
+        h_quant(0, ZH, ZQ)
         h_interleave(2, ZH, ZQ, "v")
         h_quant(1, ZH, ZQ)
         h_quant(2, ZH, ZQ)
-        h_interleave(1, ZH + ZQ, ZQ, "v")
-        h_interleave(2, ZH + ZQ, P, "v")
-        for z in (TILES, TILES + 1):
-            detect(z, range(C), 0, B)
+        for z in range(TILES):
+            detect(z, range(C), 0, B, (2, 3, 6, 7)[z])
             store(z, 0, B, "s")
-        h_interleave(2, Z - P, P, "v")
-        h_quant(1, ZH + ZQ, ZQ)
-        h_quant(2, ZH + ZQ, P)
-        h_quant(2, Z - P, P)
-        last_tiles = (TILES + 2, TILES + 3)
-        for z in last_tiles:
-            for b0 in (0, BH):
-                detect(z, range(C - 1), b0, BH)
-        for z in last_tiles:
-            for b0, engine in ((0, "v"), (BH, "s")):
-                detect(z, (C - 1,), b0, BH)
-                store(z, b0, BH, engine)
+            if z % 2 == 1:
+                h_interleave(0, ZH + ZQ + P * (z // 2), P, "s")
+        last = 2 * TILES - 1
+        for z in (last - 1, last):
+            h_interleave(1, P * z, P, "v")
+            h_interleave(2, P * z, P, "v")
+            for c in range(C):
+                h_quant(c, P * z, P)
+        for z in range(TILES, last):
+            detect(z, range(C), 0, B, (0, 1, 4)[z - TILES])
+            store(z, 0, B, "s")
+        for b0, bank in ((0, 5), (BH, 2)):
+            detect(last, range(C - 1), b0, BH, bank)
+        for b0, engine in ((0, "v"), (BH, "s")):
+            detect(last, (C - 1,), b0, BH, None)
+            store(last, b0, BH, engine)

@@ -49,11 +49,12 @@ def tile_tomography_forward_transmission_d3_kernel(tc, F, S_bytes, S_scale, i0, 
         scale_first = keep.tile([P, 1, PACK], F32, name="scale_first")
         scale_rest = keep.tile([P, G - 1, PACK], F32, name="scale_rest")
         scale_view = S_scale.rearrange("(g p j) o -> p g (j o)", p=P, j=PACK)
-        i0_t = keep.tile([P, C, PACK], BF16, name="i0_t")
+        i0_t = keep.tile([P, C, PACK * PACK], BF16, name="i0_t")
         s_view = S_bytes.rearrange("(g p j) n -> g p j n", p=P, j=PACK)
         f_view = F.rearrange("(h z p) (g k) -> h g p z k", p=P, z=TILES, k=KP)
         f_pair_view = F.rearrange("(h z p) (g k) -> h g p z k", p=P, z=TILES, k=2 * KP)
-        d_view = D.rearrange("(c p j) b -> c p j b", p=P, j=PACK)
+        d_view = D.rearrange("(c a t e) b -> c e a t b", t=PACK, e=PACK, c=C)
+        i0_view = i0.rearrange("(c a r) -> a c r", c=C, r=PACK * PACK)
         s_bytes, f_raw, d_raw = {}, {}, {}
 
         def load_s_first(j0):
@@ -83,14 +84,20 @@ def tile_tomography_forward_transmission_d3_kernel(tc, F, S_bytes, S_scale, i0, 
         def load_d(c):
             tile = keep.tile([P, PACK, B], BF16, name="d_raw%d" % c)
             d_raw[c] = tile
-            nc.sync.dma_start(out=tile[:], in_=d_view[c])
+            for e in range(PACK):
+                nc.sync.dma_start(out=tile[e:P:PACK], in_=d_view[c, e])
+
+        def load_i0():
+            span = PACK * (PACK - 1) + 1
+            for e in range(PACK):
+                nc.sync.dma_start(out=i0_t[e:P:PACK, :, 0:span], in_=i0_view[:, :, e : e + span])
 
         ident = keep.tile([P, P], F32, name="ident")
 
         def new_bank(n):
             return psum.tile([P, KP], F32, name="bank%d" % n)
 
-        i0_flat = i0_t[:].rearrange("p c j -> p (c j)")
+        i0_flat = i0_t[:].rearrange("p c r -> p (c r)")[:, 0 : C * PACK * PACK : PACK]
         mag = keep.tile([P, C * PACK], F32, name="mag")
         factors = keep.tile([P, len(LN_RANGES), C * PACK], F32, name="factors")
         logs = keep.tile([P, len(LN_RANGES), C * PACK], F32, name="logs")
@@ -146,7 +153,7 @@ def tile_tomography_forward_transmission_d3_kernel(tc, F, S_bytes, S_scale, i0, 
 
         def s_interleave(c, g):
             s_grouped[c, g] = new_grouped(KP)
-            src = s_wide[c, g][:].rearrange("p j (q i t) -> p t q j i", i=RUN, t=PACK)
+            src = s_wide[c, g][:].rearrange("p j (q t i) -> p t q j i", i=RUN, t=PACK)
             dst = s_grouped[c, g][:].rearrange("p (t q i j) -> p t q j i", t=PACK, i=RUN, j=PACK)
             nc.vector.tensor_copy(out=dst, in_=src)
 
@@ -185,18 +192,11 @@ def tile_tomography_forward_transmission_d3_kernel(tc, F, S_bytes, S_scale, i0, 
 
         p_banks, h_rows, h_grouped, h_codes, h_scales = {}, {}, {}, {}, {}
 
-        def p_bank(c, h, t):
-            if (c, h) == (0, 1):
-                return (0, 1, 4, 5)[t]
-            if (c, h) == (1, 0):
-                return (2, 3, 6, 7)[t]
-            return (0, 1, 4, 5)[t] if h == 1 else (2, 3, 6, 7)[t] if c > 0 else t
-
         def project(c, h, slices, passes):
             for t in slices:
                 for g in passes:
                     if g == 0:
-                        p_banks[c, h, t] = new_bank(p_bank(c, h, t))
+                        p_banks[c, h, t] = new_bank(t if (c, h) == (0, 0) else PACK * (1 - h) + t)
                     nc.tensor.matmul_mx(
                         out=p_banks[c, h, t][:],
                         lhsT=s_codes[c, g][:, P * t : P * (t + 1)].bitcast(FP8X4),
@@ -270,9 +270,9 @@ def tile_tomography_forward_transmission_d3_kernel(tc, F, S_bytes, S_scale, i0, 
             copy_on(engine, y_tile[:], y_banks[z, b0][:, 0:w])
             nc.sync.dma_start(out=out[P * z : P * (z + 1), b0 : b0 + w], in_=y_tile[:])
 
-        nc.sync.dma_start(out=i0_t[:], in_=i0.rearrange("(c p j) -> p c j", p=P, j=PACK))
         nc.sync.dma_start(out=scale_first[:], in_=scale_view[:, 0:1, :])
         load_s_first(0)
+        load_i0()
         load_s_first(2)
         load_f(0, 0)
         nc.sync.dma_start(out=scale_rest[:], in_=scale_view[:, 1:G, :])
@@ -289,8 +289,9 @@ def tile_tomography_forward_transmission_d3_kernel(tc, F, S_bytes, S_scale, i0, 
         nc.vector.memset(one[:], 1.0)
         nc.scalar.activation(out=unread[:, 0:1], in_=one[:], func=ACT.Ln)
         make_identity(nc, ident[:])
+        widen(0, 0, "vs--")
         i0_factors()
-        widen(0, 0, "vsvv")
+        widen(0, 0, "--vv")
         i0_logs()
         nc.scalar.activation(out=unread[:, 1:2], in_=one[:], func=ACT.Exp)
         i0_sum()
@@ -316,7 +317,8 @@ def tile_tomography_forward_transmission_d3_kernel(tc, F, S_bytes, S_scale, i0, 
         f_quant(0, 2)
         turn(0, 3)
         f_copy(0, 3)
-        project(0, 0, range(PACK), (1, 2))
+        project(0, 0, range(PACK), (1,))
+        project(0, 0, range(PACK), (2,))
         s_interleave(0, 3)
         widen(1, 0, "vsss")
         f_quant(0, 3)
@@ -325,45 +327,45 @@ def tile_tomography_forward_transmission_d3_kernel(tc, F, S_bytes, S_scale, i0, 
         turn(1, 0)
         f_copy(1, 0)
         project(0, 0, (0, 1), (3,))
+        attenuate(0, 0, (0, 1))
         s_interleave(1, 0)
-        widen(1, 1, "vvss")
+        widen(1, 1, "vvvv")
         turn(1, 1)
         f_copy(1, 1)
         project(0, 0, (2, 3), (3,))
+        attenuate(0, 0, (2, 3))
         s_quant(1, 0)
         f_quant(1, 0)
         s_interleave(1, 1)
         f_quant(1, 1)
         turn(1, 2)
-        attenuate(0, 0, (0, 1))
         f_copy(1, 2)
-        project(0, 1, (0, 1), (0, 1))
-        widen(1, 2, "vvvs")
-        s_quant(1, 1)
-        f_quant(1, 2)
+        project(0, 1, (0, 1), (0,))
         turn(1, 3)
         f_copy(1, 3)
-        attenuate(0, 0, (2, 3))
-        s_interleave(1, 2)
-        widen(1, 3, "vvvs")
+        widen(1, 2, "vvvv")
+        f_quant(1, 2)
+        s_quant(1, 1)
         f_quant(1, 3)
+        project(0, 1, (0, 1), (1,))
+        project(0, 1, (2, 3), (0, 1))
+        project(0, 1, range(PACK), (2, 3))
+        s_interleave(1, 2)
+        widen(1, 3, "vsss")
+        widen(2, 0, "vs-s")
         s_quant(1, 2)
-        project(0, 1, (0, 1), (2,))
-        project(0, 1, (2, 3), (0, 1, 2))
-        project(0, 1, range(PACK), (3,))
-        project(1, 0, range(PACK), (0, 1, 2))
         s_interleave(1, 3)
-        widen(2, 0, "vv-s")
-        s_quant(1, 3)
-        project(1, 0, range(PACK), (3,))
+        attenuate(0, 1, range(PACK))
         widen(2, 1, "vvss")
-        attenuate(0, 1, (0, 1))
+        s_quant(1, 3)
+        project(1, 0, range(PACK), (0, 1))
+        project(1, 0, range(PACK), (2, 3))
         s_interleave(2, 0)
-        attenuate(0, 1, (2, 3))
-        widen(2, 2, "vsss")
+        widen(2, 2, "vvss")
         s_quant(2, 0)
         s_interleave(2, 1)
         widen(2, 3, "vsss")
+        attenuate(1, 0, range(PACK))
         s_quant(2, 1)
         s_interleave(2, 2)
         s_interleave(2, 3)
@@ -376,7 +378,6 @@ def tile_tomography_forward_transmission_d3_kernel(tc, F, S_bytes, S_scale, i0, 
         d_quant(0)
         d_interleave(2)
         d_quant(1)
-        attenuate(1, 0, range(PACK))
         h_interleave(0, 0, ZH, "s")
         for t in range(PACK):
             project(1, 1, (t,), range(G))
@@ -402,7 +403,9 @@ def tile_tomography_forward_transmission_d3_kernel(tc, F, S_bytes, S_scale, i0, 
         h_quant(1, ZH, ZQ)
         h_quant(2, ZH, ZQ)
         for z in range(TILES):
-            detect(z, range(C), 0, B, (2, 3, 6, 7)[z])
+            detect(z, (0,), 0, B, PACK + z)
+        for z in range(TILES):
+            detect(z, (1, 2), 0, B, None)
             store(z, 0, B, "s")
             if z % 2 == 1:
                 h_interleave(0, ZH + ZQ + P * (z // 2), P, "s")
@@ -412,10 +415,14 @@ def tile_tomography_forward_transmission_d3_kernel(tc, F, S_bytes, S_scale, i0, 
             h_interleave(2, P * z, P, "v")
             for c in range(C):
                 h_quant(c, P * z, P)
-        for z in range(TILES, last):
-            detect(z, range(C), 0, B, (0, 1, 4)[z - TILES])
+        for z in (TILES, TILES + 1):
+            detect(z, (0, 1), 0, B, z - TILES)
+        for z in (TILES, TILES + 1):
+            detect(z, (2,), 0, B, None)
             store(z, 0, B, "s")
-        for b0, bank in ((0, 5), (BH, 2)):
+        detect(last - 1, range(C), 0, B, 2)
+        store(last - 1, 0, B, "s")
+        for b0, bank in ((0, 3), (BH, PACK)):
             detect(last, range(C - 1), b0, BH, bank)
         for b0, engine in ((0, "v"), (BH, "s")):
             detect(last, (C - 1,), b0, BH, None)

@@ -102,17 +102,17 @@ def tile_tomography_forward_transmission_d3_kernel(tc, F, S_bytes, S_scale, i0, 
         factors = keep.tile([P, len(LN_RANGES), C * PACK], F32, name="factors")
         logs = keep.tile([P, len(LN_RANGES), C * PACK], F32, name="logs")
         ln_i0 = keep.tile([P, C * PACK], F32, name="ln_i0")
-        sgn_plus_1 = keep.tile([P, C * PACK], F32, name="sgn_plus_1")
         sgn = keep.tile([P, C * PACK], F32, name="sgn")
         one = keep.tile([P, 1], F32, name="one")
         unread = keep.tile([P, 2], F32, name="unread")
 
+        def i0_parts():
+            nc.scalar.activation(out=mag[:], in_=i0_flat, func=ACT.Abs)
+            nc.scalar.activation(out=sgn[:], in_=i0_flat, func=ACT.Sign)
+
         def i0_factors():
-            nc.vector.scalar_tensor_tensor(out=mag[:], in0=i0_flat, scalar=-1.0, in1=i0_flat, op0=ALU.mult, op1=ALU.max)
-            nc.vector.tensor_scalar(out=sgn_plus_1[:], in0=i0_flat, scalar1=0.0, scalar2=2.0, op0=ALU.is_ge, op1=ALU.mult)
             for k, (low, high, shift) in enumerate(LN_RANGES):
                 nc.vector.tensor_scalar(out=factors[:, k, :], in0=mag[:], scalar1=low, scalar2=high, op0=ALU.max, op1=ALU.min)
-            nc.vector.tensor_scalar(out=sgn[:], in0=sgn_plus_1[:], scalar1=-1.0, scalar2=None, op0=ALU.add)
 
         def i0_logs():
             for k, (low, high, shift) in enumerate(LN_RANGES):
@@ -289,22 +289,23 @@ def tile_tomography_forward_transmission_d3_kernel(tc, F, S_bytes, S_scale, i0, 
         nc.vector.memset(one[:], 1.0)
         nc.scalar.activation(out=unread[:, 0:1], in_=one[:], func=ACT.Ln)
         make_identity(nc, ident[:])
-        widen(0, 0, "vs--")
+        widen(0, 0, "vsv-")
+        i0_parts()
+        widen(0, 0, "---s")
         i0_factors()
-        widen(0, 0, "--vv")
         i0_logs()
         nc.scalar.activation(out=unread[:, 1:2], in_=one[:], func=ACT.Exp)
-        i0_sum()
         s_interleave(0, 0)
         turn(0, 0)
         f_copy(0, 0)
-        s_quant(0, 0)
         widen(0, 1, "vvvs")
+        s_quant(0, 0)
+        i0_sum()
         f_quant(0, 0)
         s_interleave(0, 1)
         turn(0, 1)
         project(0, 0, (0, 1), (0,))
-        widen(0, 2, "vvss")
+        widen(0, 2, "vsss")
         f_copy(0, 1)
         s_quant(0, 1)
         s_interleave(0, 2)
@@ -343,7 +344,7 @@ def tile_tomography_forward_transmission_d3_kernel(tc, F, S_bytes, S_scale, i0, 
         project(0, 1, (0, 1), (0,))
         turn(1, 3)
         f_copy(1, 3)
-        widen(1, 2, "vvvv")
+        widen(1, 2, "vvvs")
         f_quant(1, 2)
         s_quant(1, 1)
         f_quant(1, 3)
@@ -356,12 +357,12 @@ def tile_tomography_forward_transmission_d3_kernel(tc, F, S_bytes, S_scale, i0, 
         s_quant(1, 2)
         s_interleave(1, 3)
         attenuate(0, 1, range(PACK))
-        widen(2, 1, "vvss")
+        widen(2, 1, "vsss")
         s_quant(1, 3)
         project(1, 0, range(PACK), (0, 1))
         project(1, 0, range(PACK), (2, 3))
         s_interleave(2, 0)
-        widen(2, 2, "vvss")
+        widen(2, 2, "vsss")
         s_quant(2, 0)
         s_interleave(2, 1)
         widen(2, 3, "vsss")
@@ -385,45 +386,44 @@ def tile_tomography_forward_transmission_d3_kernel(tc, F, S_bytes, S_scale, i0, 
         for t in range(PACK):
             project(2, 0, (t,), range(G))
             attenuate(2, 0, (t,))
-        h_interleave(1, 0, ZH, "s")
+        h_interleave(0, ZH, ZQ, "s")
         h_quant(0, 0, ZH)
+        h_interleave(1, 0, ZH, "v")
         d_quant(2)
+        h_quant(0, ZH, ZQ)
         h_interleave(2, 0, ZQ, "v")
         h_quant(1, 0, ZH)
         h_quant(2, 0, ZQ)
-        h_interleave(2, ZQ, ZQ, "v")
-        h_interleave(0, ZH, ZQ, "v")
-        h_quant(2, ZQ, ZQ)
         for t in range(PACK):
             project(2, 1, (t,), range(G))
             attenuate(2, 1, (t,))
+        h_interleave(0, ZH + ZQ, ZQ, "s")
+        h_interleave(2, ZQ, ZQ, "v")
         h_interleave(1, ZH, ZQ, "v")
-        h_quant(0, ZH, ZQ)
+        h_quant(2, ZQ, ZQ)
+        h_quant(0, ZH + ZQ, ZQ)
         h_interleave(2, ZH, ZQ, "v")
         h_quant(1, ZH, ZQ)
         h_quant(2, ZH, ZQ)
-        for z in range(TILES):
-            detect(z, (0,), 0, B, PACK + z)
-        for z in range(TILES):
-            detect(z, (1, 2), 0, B, None)
-            store(z, 0, B, "s")
-            if z % 2 == 1:
-                h_interleave(0, ZH + ZQ + P * (z // 2), P, "s")
         last = 2 * TILES - 1
         for z in (last - 1, last):
-            h_interleave(1, P * z, P, "v")
-            h_interleave(2, P * z, P, "v")
-            for c in range(C):
+            for c in (1, 2):
+                h_interleave(c, P * z, P, "v")
+            for c in (1, 2):
                 h_quant(c, P * z, P)
-        for z in (TILES, TILES + 1):
-            detect(z, (0, 1), 0, B, z - TILES)
-        for z in (TILES, TILES + 1):
-            detect(z, (2,), 0, B, None)
+        for z in range(TILES + 2):
+            detect(z, (0,), 0, B, (PACK + z) % 8)
+        for z in range(TILES + 2):
+            detect(z, (1, 2), 0, B, None)
             store(z, 0, B, "s")
-        detect(last - 1, range(C), 0, B, 2)
+            if z == TILES - 1:
+                detect(last - 1, (0,), 0, B, 2)
+                for b0, bank in ((0, 3), (BH, PACK)):
+                    detect(last, (0,), b0, BH, bank)
+        detect(last - 1, (1, 2), 0, B, None)
         store(last - 1, 0, B, "s")
-        for b0, bank in ((0, 3), (BH, PACK)):
-            detect(last, range(C - 1), b0, BH, bank)
+        for c in (1, 2):
+            for b0 in (0, BH):
+                detect(last, (c,), b0, BH, None)
         for b0, engine in ((0, "v"), (BH, "s")):
-            detect(last, (C - 1,), b0, BH, None)
             store(last, b0, BH, engine)

@@ -1,3 +1,4 @@
+import math
 from contextlib import ExitStack
 
 import concourse.mybir as mybir
@@ -14,7 +15,6 @@ FP8 = mybir.dt.float8_e4m3fn
 FP8X4 = mybir.dt.float8_e4m3fn_x4
 ALU = mybir.AluOpType
 ACT = mybir.ActivationFunctionType
-AXIS = mybir.AxisListType
 
 P = 128
 PACK = 4
@@ -26,16 +26,18 @@ ZQ = ZH // 2
 TILES = ZH // P
 BH = B // 2
 RUN = 4
-F32_MAX = (2.0 - 2.0**-23) * 2.0**127
 
 F_RAW_BUFS = 3
 F_PAIR_BUFS = 2
-WIDE_BUFS = 7
+WIDE_BUFS = 6
+WIDE_PAIR_BUFS = 1
 GROUPED_BUFS = 6
-PLANE_BUFS = 5
-Y_BUFS = 8
+Y_BUFS = 6
 
-LN_RANGES = ((2.0**-126, 2.0**-63, 2.0**63), (2.0**-63, 2.0**64, 1.0), (2.0**64, F32_MAX, 2.0**-64))
+GUESS_SHIFT = 0.043
+GUESS_SLOPE = math.log(2.0) / 2.0**23
+GUESS_START = (GUESS_SHIFT - 127.0) * math.log(2.0)
+LOG_TERMS = 5
 
 
 def tile_tomography_forward_transmission_d3_kernel(tc, F, S_bytes, S_scale, i0, D, out):
@@ -50,12 +52,17 @@ def tile_tomography_forward_transmission_d3_kernel(tc, F, S_bytes, S_scale, i0, 
         scale_rest = keep.tile([P, G - 1, PACK], F32, name="scale_rest")
         scale_view = S_scale.rearrange("(g p j) o -> p g (j o)", p=P, j=PACK)
         i0_t = keep.tile([P, C, PACK * PACK], BF16, name="i0_t")
+        i0_view = i0.rearrange("(c a r) -> a c r", c=C, r=PACK * PACK)
         s_view = S_bytes.rearrange("(g p j) n -> g p j n", p=P, j=PACK)
         f_view = F.rearrange("(h z p) (g k) -> h g p z k", p=P, z=TILES, k=KP)
         f_pair_view = F.rearrange("(h z p) (g k) -> h g p z k", p=P, z=TILES, k=2 * KP)
-        d_view = D.rearrange("(c a t e) b -> c e a t b", t=PACK, e=PACK, c=C)
-        i0_view = i0.rearrange("(c a r) -> a c r", c=C, r=PACK * PACK)
+        d_view = D.rearrange("(c a j e) b -> c e a j b", c=C, j=PACK, e=PACK)
         s_bytes, f_raw, d_raw = {}, {}, {}
+
+        def load_i0():
+            span = PACK * (PACK - 1) + 1
+            for e in range(PACK):
+                nc.sync.dma_start(out=i0_t[e:P:PACK, :, 0:span], in_=i0_view[:, :, e : e + span])
 
         def load_s_first(j0):
             tile = keep.tile([P, 2, KP], U8, name="s_first_%d" % j0)
@@ -81,16 +88,12 @@ def tile_tomography_forward_transmission_d3_kernel(tc, F, S_bytes, S_scale, i0, 
                 f_raw[h, g] = tile[:, :, KP * (g - g0) : KP * (g - g0 + 1)]
             nc.sync.dma_start(out=tile[:], in_=f_pair_view[h, g0 // 2])
 
-        def load_d(c):
-            tile = keep.tile([P, PACK, B], BF16, name="d_raw%d" % c)
-            d_raw[c] = tile
-            for e in range(PACK):
-                nc.sync.dma_start(out=tile[e:P:PACK], in_=d_view[c, e])
-
-        def load_i0():
-            span = PACK * (PACK - 1) + 1
-            for e in range(PACK):
-                nc.sync.dma_start(out=i0_t[e:P:PACK, :, 0:span], in_=i0_view[:, :, e : e + span])
+        def load_d(c0, c1):
+            tile = keep.tile([P, PACK, (c1 - c0) * B], BF16, name="d_raw%d" % c0)
+            d_raw[c0] = tile
+            for c in range(c0, c1):
+                for e in range(PACK):
+                    nc.sync.dma_start(out=tile[e:P:PACK, :, B * (c - c0) : B * (c - c0 + 1)], in_=d_view[c, e])
 
         ident = keep.tile([P, P], F32, name="ident")
 
@@ -98,28 +101,55 @@ def tile_tomography_forward_transmission_d3_kernel(tc, F, S_bytes, S_scale, i0, 
             return psum.tile([P, KP], F32, name="bank%d" % n)
 
         i0_flat = i0_t[:].rearrange("p c r -> p (c r)")[:, 0 : C * PACK * PACK : PACK]
-        mag = keep.tile([P, C * PACK], F32, name="mag")
-        factors = keep.tile([P, len(LN_RANGES), C * PACK], F32, name="factors")
-        logs = keep.tile([P, len(LN_RANGES), C * PACK], F32, name="logs")
-        ln_i0 = keep.tile([P, C * PACK], F32, name="ln_i0")
-        sgn = keep.tile([P, C * PACK], F32, name="sgn")
-        one = keep.tile([P, 1], F32, name="one")
-        unread = keep.tile([P, 2], F32, name="unread")
+        mag, sgn, guess, half_inv, root, ratio, d, ln_i0 = [
+            keep.tile([P, C * PACK], F32, name=name)[:] for name in ("mag", "sgn", "guess", "half_inv", "root", "ratio", "d", "ln_i0")
+        ]
+        series = [keep.tile([P, C * PACK], F32, name="series%d" % k)[:] for k in range(LOG_TERMS)]
 
-        def i0_parts():
-            nc.scalar.activation(out=mag[:], in_=i0_flat, func=ACT.Abs)
-            nc.scalar.activation(out=sgn[:], in_=i0_flat, func=ACT.Sign)
+        def series_step(k):
+            n = LOG_TERMS - k
+            nc.vector.scalar_tensor_tensor(out=series[k], in0=series[k - 1], scalar=(-1.0) ** (n + 1) / n, in1=d, op0=ALU.add, op1=ALU.mult)
 
-        def i0_factors():
-            for k, (low, high, shift) in enumerate(LN_RANGES):
-                nc.vector.tensor_scalar(out=factors[:, k, :], in0=mag[:], scalar1=low, scalar2=high, op0=ALU.max, op1=ALU.min)
+        ln_steps = [
+            lambda: nc.scalar.activation(out=mag, in_=i0_flat, func=ACT.Abs),
+            lambda: nc.scalar.activation(out=guess, in_=mag.bitcast(U32), func=ACT.Identity, scale=GUESS_SLOPE, bias=GUESS_START),
+            lambda: nc.scalar.activation(out=half_inv, in_=guess, func=ACT.Exp, scale=-0.5),
+            lambda: nc.vector.tensor_tensor(out=root, in0=mag, in1=half_inv, op=ALU.mult),
+            lambda: nc.vector.tensor_tensor(out=ratio, in0=root, in1=half_inv, op=ALU.mult),
+            lambda: nc.vector.tensor_scalar(out=d, in0=ratio, scalar1=-1.0, scalar2=None, op0=ALU.add),
+            lambda: nc.vector.tensor_scalar(out=series[0], in0=d, scalar1=(-1.0) ** (LOG_TERMS + 1) / LOG_TERMS, scalar2=None, op0=ALU.mult),
+            lambda: series_step(1),
+            lambda: series_step(2),
+            lambda: series_step(3),
+            lambda: series_step(4),
+            lambda: nc.vector.tensor_tensor(out=ln_i0, in0=series[LOG_TERMS - 1], in1=guess, op=ALU.add),
+        ]
 
-        def i0_logs():
-            for k, (low, high, shift) in enumerate(LN_RANGES):
-                nc.scalar.activation(out=logs[:, k, :], in_=factors[:, k, :], func=ACT.Ln, scale=shift)
+        def ln_step():
+            ln_steps.pop(0)()
 
-        def i0_sum():
-            nc.vector.tensor_reduce(out=ln_i0[:], in_=logs[:].rearrange("p k n -> p n k"), op=ALU.add, axis=AXIS.X)
+        grouped, batches, codes, scales = {}, {}, {}, {}
+
+        def new_batch(*parts):
+            tile = ring.tile([P, PACK * sum(w for key, w in parts)], BF16, name="grouped", bufs=GROUPED_BUFS, align_bytes=64)
+            start = 0
+            for key, w in parts:
+                grouped[key] = tile[:, PACK * start : PACK * (start + w)]
+                start = start + w
+            batches[parts[0][0]] = (tile, parts)
+
+        def quantize(first_key):
+            tile, parts = batches[first_key]
+            width = sum(w for key, w in parts)
+            name = "_".join(str(x) for x in first_key)
+            code_tile = keep.tile([P, width], U32, name="codes_" + name, align_bytes=64)
+            scale_tile = keep.tile([P, width], U8, name="scales_" + name, align_bytes=64)
+            nc.vector.quantize_mx(out=code_tile[:].bitcast(FP8X4), scales=scale_tile[:], in_=tile[:])
+            start = 0
+            for key, w in parts:
+                codes[key] = code_tile[:, start : start + w]
+                scales[key] = scale_tile[:, start : start + w]
+                start = start + w
 
         def copy_on(engine, dst, src):
             if engine == "v":
@@ -127,21 +157,21 @@ def tile_tomography_forward_transmission_d3_kernel(tc, F, S_bytes, S_scale, i0, 
             else:
                 nc.scalar.copy(out=dst, in_=src)
 
-        def new_grouped(columns):
-            return ring.tile([P, PACK * columns], BF16, name="grouped", bufs=GROUPED_BUFS, align_bytes=64)
+        def interleave(engine, dst, rows):
+            copy_on(engine, dst.rearrange("p (q i j) -> p q j i", i=RUN, j=PACK), rows.rearrange("p j (q i) -> p q j i", i=RUN))
 
-        def interleave(engine, grouped, rows):
-            dst = grouped[:].rearrange("p (q i j) -> p q j i", i=RUN, j=PACK)
-            copy_on(engine, dst, rows.rearrange("p j (q i) -> p q j i", i=RUN))
+        s_wide, s_place = {}, {}
 
-        def quantize(codes, scales, grouped):
-            nc.vector.quantize_mx(out=codes[:].bitcast(FP8X4), scales=scales[:], in_=grouped[:])
-
-        s_wide, s_grouped, s_codes, s_scales = {}, {}, {}, {}
+        def new_wide(c, passes):
+            n = len(passes)
+            bufs = WIDE_BUFS if n == 1 else WIDE_PAIR_BUFS
+            tile = ring.tile([P, PACK, n * KP], BF16, name="s_wide%d" % n, bufs=bufs, align_bytes=64)
+            for u, g in enumerate(passes):
+                s_wide[c, g] = tile[:, :, KP * u : KP * (u + 1)]
+                s_place[c, g] = (passes[0], n, u)
+            s_wide["all", c, passes[0]] = tile
 
         def widen(c, g, engines):
-            if (c, g) not in s_wide:
-                s_wide[c, g] = ring.tile([P, PACK, KP], BF16, name="s_wide", bufs=WIDE_BUFS, align_bytes=64)
             for j in range(PACK):
                 src = s_bytes[c, g, j].bitcast(FP8)
                 dst = s_wide[c, g][:, j, :]
@@ -151,18 +181,22 @@ def tile_tomography_forward_transmission_d3_kernel(tc, F, S_bytes, S_scale, i0, 
                 elif engines[j] == "s":
                     nc.scalar.activation(out=dst, in_=src, func=ACT.Copy, scale=scale)
 
-        def s_interleave(c, g):
-            s_grouped[c, g] = new_grouped(KP)
-            src = s_wide[c, g][:].rearrange("p j (q t i) -> p t q j i", i=RUN, t=PACK)
-            dst = s_grouped[c, g][:].rearrange("p (t q i j) -> p t q j i", t=PACK, i=RUN, j=PACK)
+        def s_interleave(c, g0):
+            src = s_wide["all", c, g0][:].rearrange("p j (q t e) -> p t q j e", t=PACK, e=PACK)
+            dst = grouped["s", c, g0].rearrange("p (t q e j) -> p t q j e", t=PACK, e=PACK, j=PACK)
             nc.vector.tensor_copy(out=dst, in_=src)
 
-        def s_quant(c, g):
-            s_codes[c, g] = ring.tile([P, KP], U32, name="s_codes", bufs=C * G, align_bytes=64)
-            s_scales[c, g] = ring.tile([P, KP], U8, name="s_scales", bufs=C * G, align_bytes=64)
-            quantize(s_codes[c, g], s_scales[c, g], s_grouped[c, g])
+        def s_slice(table, c, g, t):
+            g0, n, u = s_place[c, g]
+            return table["s", c, g0][:, P * (n * t + u) : P * (n * t + u + 1)]
 
-        f_grouped, f_codes, f_scales = {}, {}, {}
+        def s_begin(c, g, engines):
+            new_wide(c, (g,))
+            widen(c, g, engines)
+
+        def s_group(c, g):
+            new_batch((("s", c, g), KP))
+            s_interleave(c, g)
 
         f_banks = {}
 
@@ -177,40 +211,42 @@ def tile_tomography_forward_transmission_d3_kernel(tc, F, S_bytes, S_scale, i0, 
                     column = (2 * (z % 2) + u) * P
                     nc.tensor.transpose(banks[-1][:, column : column + P], words[:, u : 2 * P : 2], ident[:])
 
-        def f_copy(h, g):
-            f_grouped[h, g] = new_grouped(ZH)
-            for b, bank in enumerate(f_banks[h, g]):
-                dst = f_grouped[h, g][:].bitcast(F32)[:, KP * b : KP * (b + 1)]
+        def f_copy(h, g, order):
+            for b in order:
+                dst = grouped["f", h, g].bitcast(F32)[:, KP * b : KP * (b + 1)]
                 nc.scalar.copy(
-                    out=dst.rearrange("p (z r u) -> p z r u", z=2, u=2), in_=bank[:].rearrange("p (z u r) -> p z r u", z=2, u=2)
+                    out=dst.rearrange("p (z r u) -> p z r u", z=2, u=2),
+                    in_=f_banks[h, g][b][:].rearrange("p (z u r) -> p z r u", z=2, u=2),
                 )
 
-        def f_quant(h, g):
-            f_codes[h, g] = keep.tile([P, ZH], U32, name="f_codes%d_%d" % (h, g), align_bytes=64)
-            f_scales[h, g] = keep.tile([P, ZH], U8, name="f_scales%d_%d" % (h, g), align_bytes=64)
-            quantize(f_codes[h, g], f_scales[h, g], f_grouped[h, g])
+        def f_empty(h, g):
+            new_batch((("f", h, g), ZH))
+            f_copy(h, g, (0, 1))
 
-        p_banks, h_rows, h_grouped, h_codes, h_scales = {}, {}, {}, {}, {}
+        p_banks, h_place = {}, {}
+        h_rows = {(c, 0): keep.tile([P, PACK, ZH], BF16, name="h_rows%d" % c, align_bytes=64)[:] for c in range(C)}
+        h_rows[0, 1] = keep.tile([P, PACK, ZH], BF16, name="h_rows_second", align_bytes=64)[:]
+        h_late = keep.tile([P, PACK, 2, ZH], BF16, name="h_late", align_bytes=64)
+        for c in (1, 2):
+            h_rows[c, 1] = h_late[:, :, c - 1, :]
 
         def project(c, h, slices, passes):
             for t in slices:
                 for g in passes:
                     if g == 0:
-                        p_banks[c, h, t] = new_bank(t if (c, h) == (0, 0) else PACK * (1 - h) + t)
+                        p_banks[c, h, t] = new_bank(PACK * h + t)
                     nc.tensor.matmul_mx(
                         out=p_banks[c, h, t][:],
-                        lhsT=s_codes[c, g][:, P * t : P * (t + 1)].bitcast(FP8X4),
-                        lhsT_scale=s_scales[c, g][:, P * t : P * (t + 1)],
-                        rhs=f_codes[h, g][:].bitcast(FP8X4),
-                        rhs_scale=f_scales[h, g][:],
+                        lhsT=s_slice(codes, c, g, t).bitcast(FP8X4),
+                        lhsT_scale=s_slice(scales, c, g, t),
+                        rhs=codes["f", h, g].bitcast(FP8X4),
+                        rhs_scale=scales["f", h, g],
                         start=(g == 0),
                         stop=(g == G - 1),
                     )
 
         def attenuate(c, h, slices):
             for t in slices:
-                if (c, h) not in h_rows:
-                    h_rows[c, h] = ring.tile([P, PACK, ZH], BF16, name="h_rows", bufs=PLANE_BUFS, align_bytes=64)
                 nc.scalar.activation(
                     out=h_rows[c, h][:, t, :],
                     in_=p_banks[c, h, t][:],
@@ -219,35 +255,33 @@ def tile_tomography_forward_transmission_d3_kernel(tc, F, S_bytes, S_scale, i0, 
                     scale=-1.0,
                 )
 
+        def h_part(c, z0, w):
+            for k in range(w // P):
+                h_place[c, z0 // P + k] = (("h", c, z0), P * k)
+            return (("h", c, z0), w)
+
         def h_interleave(c, z0, w, engine):
             h, z1 = divmod(z0, ZH)
-            h_grouped[c, z0] = new_grouped(w)
-            interleave(engine, h_grouped[c, z0], h_rows[c, h][:, :, z1 : z1 + w])
+            interleave(engine, grouped["h", c, z0], h_rows[c, h][:, :, z1 : z1 + w])
 
-        def h_quant(c, z0, w):
-            codes = keep.tile([P, w], U32, name="h_codes%d_%d" % (c, z0), align_bytes=64)
-            scales = keep.tile([P, w], U8, name="h_scales%d_%d" % (c, z0), align_bytes=64)
-            for k in range(w // P):
-                h_codes[c, z0 // P + k] = codes[:, P * k : P * (k + 1)]
-                h_scales[c, z0 // P + k] = scales[:, P * k : P * (k + 1)]
-            quantize(codes, scales, h_grouped[c, z0])
+        def h_late_interleave(z0, w):
+            new_batch(h_part(1, z0, w), h_part(2, z0, w))
+            src = h_late[:, :, :, z0 - ZH : z0 - ZH + w].rearrange("p j c (q i) -> p c q j i", i=RUN)
+            dst = batches["h", 1, z0][0][:].rearrange("p (c q i j) -> p c q j i", c=2, i=RUN, j=PACK)
+            nc.vector.tensor_copy(out=dst, in_=src)
 
-        d_grouped, d_codes, d_scales = {}, {}, {}
+        def h_group(c, z0, w, engine):
+            new_batch(h_part(c, z0, w))
+            h_interleave(c, z0, w, engine)
 
-        def d_sign(c):
+        def d_sign(c0, c):
             for j in range(PACK):
-                nc.vector.tensor_scalar(
-                    out=d_raw[c][:, j, :], in0=d_raw[c][:, j, :], scalar1=sgn[:, PACK * c + j : PACK * c + j + 1], scalar2=None, op0=ALU.mult
-                )
+                row = d_raw[c0][:, j, B * (c - c0) : B * (c - c0 + 1)]
+                nc.vector.tensor_scalar(out=row, in0=row, scalar1=sgn[:, PACK * c + j : PACK * c + j + 1], scalar2=None, op0=ALU.mult)
 
-        def d_interleave(c):
-            d_grouped[c] = new_grouped(B)
-            interleave("v", d_grouped[c], d_raw[c][:])
-
-        def d_quant(c):
-            d_codes[c] = keep.tile([P, B], U32, name="d_codes%d" % c, align_bytes=64)
-            d_scales[c] = keep.tile([P, B], U8, name="d_scales%d" % c, align_bytes=64)
-            quantize(d_codes[c], d_scales[c], d_grouped[c])
+        def d_group(c):
+            new_batch((("d", c), B))
+            interleave("v", grouped["d", c], d_raw[c][:])
 
         y_banks = {}
 
@@ -255,175 +289,180 @@ def tile_tomography_forward_transmission_d3_kernel(tc, F, S_bytes, S_scale, i0, 
             for c in groups:
                 if c == 0:
                     y_banks[z, b0] = new_bank(bank)
+                key, start = h_place[c, z]
                 nc.tensor.matmul_mx(
                     out=y_banks[z, b0][:, 0:w],
-                    lhsT=h_codes[c, z].bitcast(FP8X4),
-                    lhsT_scale=h_scales[c, z],
-                    rhs=d_codes[c][:, b0 : b0 + w].bitcast(FP8X4),
-                    rhs_scale=d_scales[c][:, b0 : b0 + w],
+                    lhsT=codes[key][:, start : start + P].bitcast(FP8X4),
+                    lhsT_scale=scales[key][:, start : start + P],
+                    rhs=codes["d", c][:, b0 : b0 + w].bitcast(FP8X4),
+                    rhs_scale=scales["d", c][:, b0 : b0 + w],
                     start=(c == 0),
                     stop=(c == C - 1),
                 )
 
-        def store(z, b0, w, engine):
+        def store(z, b0, w, engine, queue=nc.sync):
             y_tile = ring.tile([P, w], F32, name="y_tile", bufs=Y_BUFS)
             copy_on(engine, y_tile[:], y_banks[z, b0][:, 0:w])
-            nc.sync.dma_start(out=out[P * z : P * (z + 1), b0 : b0 + w], in_=y_tile[:])
+            queue.dma_start(out=out[P * z : P * (z + 1), b0 : b0 + w], in_=y_tile[:])
 
         nc.sync.dma_start(out=scale_first[:], in_=scale_view[:, 0:1, :])
         load_s_first(0)
-        load_i0()
         load_s_first(2)
-        load_f(0, 0)
         nc.sync.dma_start(out=scale_rest[:], in_=scale_view[:, 1:G, :])
-        for g in range(1, G):
-            load_s(g, 0, 1)
+        for g in range(G):
+            if g + 1 < G:
+                load_s(g + 1, 0, 1)
             load_f(0, g)
+            if g == 0:
+                load_i0()
         for g in range(G):
             load_s(g, 1, C)
             if g < G // 2:
                 load_f_pair(1, 2 * g)
         for c in range(C):
-            load_d(c)
-
-        nc.vector.memset(one[:], 1.0)
-        nc.scalar.activation(out=unread[:, 0:1], in_=one[:], func=ACT.Ln)
+            load_d(c, c + 1)
         make_identity(nc, ident[:])
-        widen(0, 0, "vsv-")
-        i0_parts()
-        widen(0, 0, "---s")
-        i0_factors()
-        i0_logs()
-        nc.scalar.activation(out=unread[:, 1:2], in_=one[:], func=ACT.Exp)
-        s_interleave(0, 0)
+
+        s_begin(0, 0, "vsvv")
+        s_begin(0, 1, "-sss")
+        s_group(0, 0)
+        widen(0, 1, "v---")
+        quantize(("s", 0, 0))
+        ln_step()
+        nc.scalar.activation(out=sgn, in_=i0_flat, func=ACT.Sign)
+        ln_step()
         turn(0, 0)
-        f_copy(0, 0)
-        widen(0, 1, "vvvs")
-        s_quant(0, 0)
-        i0_sum()
-        f_quant(0, 0)
-        s_interleave(0, 1)
+        f_empty(0, 0)
+        ln_step()
+        s_group(0, 1)
+        s_begin(0, 2, "vvss")
+        quantize(("f", 0, 0))
+        ln_step()
+        quantize(("s", 0, 1))
+        ln_step()
         turn(0, 1)
         project(0, 0, (0, 1), (0,))
-        widen(0, 2, "vsss")
-        f_copy(0, 1)
-        s_quant(0, 1)
-        s_interleave(0, 2)
-        f_quant(0, 1)
+        f_empty(0, 1)
+        s_group(0, 2)
+        ln_step()
+        s_begin(0, 3, "vsss")
+        ln_step()
+        quantize(("f", 0, 1))
+        ln_step()
+        quantize(("s", 0, 2))
+        ln_step()
         turn(0, 2)
         project(0, 0, (2, 3), (0,))
-        f_copy(0, 2)
-        widen(0, 3, "vsss")
-        s_quant(0, 2)
-        f_quant(0, 2)
+        f_empty(0, 2)
+        s_group(0, 3)
+        ln_step()
+        quantize(("f", 0, 2))
+        ln_step()
+        s_begin(1, 0, "vsss")
+        quantize(("s", 0, 3))
+        ln_step()
         turn(0, 3)
-        f_copy(0, 3)
+        f_empty(0, 3)
         project(0, 0, range(PACK), (1,))
-        project(0, 0, range(PACK), (2,))
-        s_interleave(0, 3)
-        widen(1, 0, "vsss")
-        f_quant(0, 3)
-        s_quant(0, 3)
-        widen(2, 0, "--s-")
+        project(0, 0, (0, 1), (2,))
+        s_begin(2, 0, "---s")
         turn(1, 0)
-        f_copy(1, 0)
-        project(0, 0, (0, 1), (3,))
-        attenuate(0, 0, (0, 1))
-        s_interleave(1, 0)
-        widen(1, 1, "vvvv")
+        project(0, 0, (2, 3), (2,))
+        f_empty(1, 0)
+        s_group(1, 0)
+        quantize(("f", 0, 3))
+        s_begin(1, 1, "vvss")
         turn(1, 1)
-        f_copy(1, 1)
-        project(0, 0, (2, 3), (3,))
-        attenuate(0, 0, (2, 3))
-        s_quant(1, 0)
-        f_quant(1, 0)
-        s_interleave(1, 1)
-        f_quant(1, 1)
+        project(0, 0, (0, 1), (3,))
+        f_empty(1, 1)
+        quantize(("s", 1, 0))
+        quantize(("f", 1, 0))
+        s_group(1, 1)
         turn(1, 2)
-        f_copy(1, 2)
-        project(0, 1, (0, 1), (0,))
+        project(0, 0, (2, 3), (3,))
+        f_empty(1, 2)
+        s_begin(1, 2, "---s")
         turn(1, 3)
-        f_copy(1, 3)
-        widen(1, 2, "vvvs")
-        f_quant(1, 2)
-        s_quant(1, 1)
-        f_quant(1, 3)
-        project(0, 1, (0, 1), (1,))
-        project(0, 1, (2, 3), (0, 1))
+        f_empty(1, 3)
+        widen(1, 2, "vvv-")
+        quantize(("f", 1, 1))
+        quantize(("s", 1, 1))
+        quantize(("f", 1, 2))
+        quantize(("f", 1, 3))
+        s_group(1, 2)
+        project(0, 1, range(PACK), (0, 1))
         project(0, 1, range(PACK), (2, 3))
-        s_interleave(1, 2)
-        widen(1, 3, "vsss")
-        widen(2, 0, "vs-s")
-        s_quant(1, 2)
-        s_interleave(1, 3)
-        attenuate(0, 1, range(PACK))
-        widen(2, 1, "vsss")
-        s_quant(1, 3)
+        s_begin(1, 3, "vvss")
+        attenuate(0, 0, range(PACK))
+        quantize(("s", 1, 2))
+        s_group(1, 3)
+        widen(2, 0, "vss-")
+        quantize(("s", 1, 3))
         project(1, 0, range(PACK), (0, 1))
         project(1, 0, range(PACK), (2, 3))
-        s_interleave(2, 0)
-        widen(2, 2, "vsss")
-        s_quant(2, 0)
-        s_interleave(2, 1)
-        widen(2, 3, "vsss")
+        s_begin(2, 1, "vsss")
+        attenuate(0, 1, range(PACK))
+        s_group(2, 0)
+        s_begin(2, 2, "vvss")
+        s_group(2, 1)
+        quantize(("s", 2, 0))
+        s_begin(2, 3, "vsss")
+        quantize(("s", 2, 1))
         attenuate(1, 0, range(PACK))
-        s_quant(2, 1)
-        s_interleave(2, 2)
-        s_interleave(2, 3)
-        s_quant(2, 2)
-        s_quant(2, 3)
-        for c in range(C):
-            d_sign(c)
-        d_interleave(0)
-        d_interleave(1)
-        d_quant(0)
-        d_interleave(2)
-        d_quant(1)
-        h_interleave(0, 0, ZH, "s")
+        d_sign(2, 2)
+        s_group(2, 2)
+        d_sign(1, 1)
+        quantize(("s", 2, 2))
+        s_group(2, 3)
+        d_sign(0, 0)
+        quantize(("s", 2, 3))
+        d_group(0)
+        d_group(1)
+        quantize(("d", 0))
+        d_group(2)
+        quantize(("d", 1))
+        h_group(0, 0, ZH, "s")
         for t in range(PACK):
             project(1, 1, (t,), range(G))
             attenuate(1, 1, (t,))
-        for t in range(PACK):
-            project(2, 0, (t,), range(G))
-            attenuate(2, 0, (t,))
-        h_interleave(0, ZH, ZQ, "s")
-        h_quant(0, 0, ZH)
-        h_interleave(1, 0, ZH, "v")
-        d_quant(2)
-        h_quant(0, ZH, ZQ)
-        h_interleave(2, 0, ZQ, "v")
-        h_quant(1, 0, ZH)
-        h_quant(2, 0, ZQ)
+        project(2, 0, range(PACK), (0, 1))
+        project(2, 0, range(PACK), (2, 3))
+        attenuate(2, 0, range(PACK))
+        h_group(0, ZH, ZQ, "s")
+        quantize(("h", 0, 0))
+        h_group(1, 0, ZQ, "v")
+        quantize(("d", 2))
+        h_group(2, 0, ZQ, "v")
+        quantize(("h", 1, 0))
+        quantize(("h", 0, ZH))
+        quantize(("h", 2, 0))
         for t in range(PACK):
             project(2, 1, (t,), range(G))
             attenuate(2, 1, (t,))
-        h_interleave(0, ZH + ZQ, ZQ, "s")
-        h_interleave(2, ZQ, ZQ, "v")
-        h_interleave(1, ZH, ZQ, "v")
-        h_quant(2, ZQ, ZQ)
-        h_quant(0, ZH + ZQ, ZQ)
-        h_interleave(2, ZH, ZQ, "v")
-        h_quant(1, ZH, ZQ)
-        h_quant(2, ZH, ZQ)
+        h_group(0, ZH + ZQ, ZQ, "s")
+        h_group(1, ZQ, ZQ, "v")
+        h_group(2, ZQ, ZQ, "v")
+        quantize(("h", 1, ZQ))
+        quantize(("h", 2, ZQ))
         last = 2 * TILES - 1
-        for z in (last - 1, last):
-            for c in (1, 2):
-                h_interleave(c, P * z, P, "v")
-            for c in (1, 2):
-                h_quant(c, P * z, P)
+        for z in range(TILES, last):
+            h_late_interleave(P * z, P)
+            quantize(("h", 0, ZH + ZQ) if z == TILES else ("h", 1, P * (z - 1)))
+        quantize(("h", 1, P * (last - 1)))
+        h_late_interleave(P * last, P)
+        quantize(("h", 1, P * last))
         for z in range(TILES + 2):
-            detect(z, (0,), 0, B, (PACK + z) % 8)
+            detect(z, (0,), 0, B, z)
         for z in range(TILES + 2):
             detect(z, (1, 2), 0, B, None)
             store(z, 0, B, "s")
             if z == TILES - 1:
-                detect(last - 1, (0,), 0, B, 2)
-                for b0, bank in ((0, 3), (BH, PACK)):
+                detect(last - 1, (0,), 0, B, last - 1)
+                for b0, bank in ((0, last), (BH, 0)):
                     detect(last, (0,), b0, BH, bank)
         detect(last - 1, (1, 2), 0, B, None)
         store(last - 1, 0, B, "s")
-        for c in (1, 2):
-            for b0 in (0, BH):
-                detect(last, (c,), b0, BH, None)
-        for b0, engine in ((0, "v"), (BH, "s")):
-            store(last, b0, BH, engine)
+        detect(last, (1, 2), 0, BH, None)
+        store(last, 0, BH, "v")
+        detect(last, (1, 2), BH, BH, None)
+        store(last, BH, BH, "s", nc.scalar)

@@ -104,6 +104,8 @@ def tile_tomography_forward_transmission_d3_kernel(tc, F, S_bytes, S_scale, i0, 
         mag, sgn, guess, half_inv, root, ratio, d, ln_i0 = [
             keep.tile([P, C * PACK], F32, name=name)[:] for name in ("mag", "sgn", "guess", "half_inv", "root", "ratio", "d", "ln_i0")
         ]
+        one = keep.tile([P, 1], F32, name="one")
+        unread = keep.tile([P, 1], F32, name="unread")
         series = [keep.tile([P, C * PACK], F32, name="series%d" % k)[:] for k in range(LOG_TERMS)]
 
         def series_step(k):
@@ -300,10 +302,10 @@ def tile_tomography_forward_transmission_d3_kernel(tc, F, S_bytes, S_scale, i0, 
                     stop=(c == C - 1),
                 )
 
-        def store(z, b0, w, engine, queue=nc.sync):
+        def store(z, b0, w, engine):
             y_tile = ring.tile([P, w], F32, name="y_tile", bufs=Y_BUFS)
             copy_on(engine, y_tile[:], y_banks[z, b0][:, 0:w])
-            queue.dma_start(out=out[P * z : P * (z + 1), b0 : b0 + w], in_=y_tile[:])
+            nc.sync.dma_start(out=out[P * z : P * (z + 1), b0 : b0 + w], in_=y_tile[:])
 
         nc.sync.dma_start(out=scale_first[:], in_=scale_view[:, 0:1, :])
         load_s_first(0)
@@ -321,6 +323,8 @@ def tile_tomography_forward_transmission_d3_kernel(tc, F, S_bytes, S_scale, i0, 
                 load_f_pair(1, 2 * g)
         for c in range(C):
             load_d(c, c + 1)
+        nc.vector.memset(one[:], 1.0)
+        nc.scalar.activation(out=unread[:], in_=one[:], func=ACT.Exp)
         make_identity(nc, ident[:])
 
         s_begin(0, 0, "vsvv")
@@ -465,4 +469,4 @@ def tile_tomography_forward_transmission_d3_kernel(tc, F, S_bytes, S_scale, i0, 
         detect(last, (1, 2), 0, BH, None)
         store(last, 0, BH, "v")
         detect(last, (1, 2), BH, BH, None)
-        store(last, BH, BH, "s", nc.scalar)
+        store(last, BH, BH, "s")

@@ -236,7 +236,7 @@ def tile_tomography_forward_transmission_d3_kernel(tc, F, S_bytes, S_scale, i0, 
             for t in slices:
                 for g in passes:
                     if g == 0:
-                        p_banks[c, h, t] = new_bank(PACK * h + t)
+                        p_banks[c, h, t] = new_bank(t if (c, h) == (0, 0) else PACK * (1 - h) + t)
                     nc.tensor.matmul_mx(
                         out=p_banks[c, h, t][:],
                         lhsT=s_slice(codes, c, g, t).bitcast(FP8X4),
@@ -315,7 +315,7 @@ def tile_tomography_forward_transmission_d3_kernel(tc, F, S_bytes, S_scale, i0, 
             if g + 1 < G:
                 load_s(g + 1, 0, 1)
             load_f(0, g)
-            if g == 0:
+            if g == 1:
                 load_i0()
         for g in range(G):
             load_s(g, 1, C)
@@ -332,27 +332,24 @@ def tile_tomography_forward_transmission_d3_kernel(tc, F, S_bytes, S_scale, i0, 
         s_group(0, 0)
         widen(0, 1, "v---")
         quantize(("s", 0, 0))
-        ln_step()
-        nc.scalar.activation(out=sgn, in_=i0_flat, func=ACT.Sign)
-        ln_step()
         turn(0, 0)
         f_empty(0, 0)
-        ln_step()
         s_group(0, 1)
         s_begin(0, 2, "vvss")
         quantize(("f", 0, 0))
-        ln_step()
         quantize(("s", 0, 1))
-        ln_step()
         turn(0, 1)
         project(0, 0, (0, 1), (0,))
         f_empty(0, 1)
+        ln_step()
+        nc.scalar.activation(out=sgn, in_=i0_flat, func=ACT.Sign)
         s_group(0, 2)
+        s_begin(0, 3, "vs--")
         ln_step()
-        s_begin(0, 3, "vsss")
+        widen(0, 3, "--s-")
         ln_step()
+        widen(0, 3, "---s")
         quantize(("f", 0, 1))
-        ln_step()
         quantize(("s", 0, 2))
         ln_step()
         turn(0, 2)
@@ -362,69 +359,77 @@ def tile_tomography_forward_transmission_d3_kernel(tc, F, S_bytes, S_scale, i0, 
         ln_step()
         quantize(("f", 0, 2))
         ln_step()
-        s_begin(1, 0, "vsss")
-        quantize(("s", 0, 3))
-        ln_step()
         turn(0, 3)
         f_empty(0, 3)
+        s_begin(1, 0, "vsss")
+        ln_step()
+        quantize(("s", 0, 3))
+        ln_step()
         project(0, 0, range(PACK), (1,))
-        project(0, 0, (0, 1), (2,))
-        s_begin(2, 0, "---s")
-        turn(1, 0)
-        project(0, 0, (2, 3), (2,))
-        f_empty(1, 0)
-        s_group(1, 0)
+        project(0, 0, range(PACK), (2,))
         quantize(("f", 0, 3))
-        s_begin(1, 1, "vvss")
-        turn(1, 1)
+        ln_step()
+        s_begin(2, 0, "--s-")
+        turn(1, 0)
+        f_empty(1, 0)
         project(0, 0, (0, 1), (3,))
+        s_group(1, 0)
+        ln_step()
+        s_begin(1, 1, "vv--")
+        ln_step()
+        widen(1, 1, "--vs")
+        ln_step()
+        turn(1, 1)
         f_empty(1, 1)
+        attenuate(0, 0, (0, 1))
+        project(0, 0, (2, 3), (3,))
         quantize(("s", 1, 0))
         quantize(("f", 1, 0))
         s_group(1, 1)
+        quantize(("f", 1, 1))
         turn(1, 2)
-        project(0, 0, (2, 3), (3,))
         f_empty(1, 2)
-        s_begin(1, 2, "---s")
+        attenuate(0, 0, (2, 3))
+        project(0, 1, (0, 1), (0,))
         turn(1, 3)
         f_empty(1, 3)
-        widen(1, 2, "vvv-")
-        quantize(("f", 1, 1))
-        quantize(("s", 1, 1))
+        s_begin(1, 2, "vvvv")
         quantize(("f", 1, 2))
+        quantize(("s", 1, 1))
         quantize(("f", 1, 3))
         s_group(1, 2)
-        project(0, 1, range(PACK), (0, 1))
-        project(0, 1, range(PACK), (2, 3))
-        s_begin(1, 3, "vvss")
-        attenuate(0, 0, range(PACK))
+        project(0, 1, (0, 1), (1,))
+        project(0, 1, (2, 3), (0, 1))
+        project(0, 1, range(PACK), (2,))
+        project(0, 1, range(PACK), (3,))
+        s_begin(1, 3, "vsss")
+        widen(2, 0, "vs-s")
         quantize(("s", 1, 2))
         s_group(1, 3)
-        widen(2, 0, "vss-")
+        s_begin(2, 1, "vsss")
+        attenuate(0, 1, range(PACK))
         quantize(("s", 1, 3))
         project(1, 0, range(PACK), (0, 1))
         project(1, 0, range(PACK), (2, 3))
-        s_begin(2, 1, "vsss")
-        attenuate(0, 1, range(PACK))
         s_group(2, 0)
-        s_begin(2, 2, "vvss")
-        s_group(2, 1)
+        s_begin(2, 2, "vsss")
         quantize(("s", 2, 0))
+        s_group(2, 1)
         s_begin(2, 3, "vsss")
-        quantize(("s", 2, 1))
         attenuate(1, 0, range(PACK))
+        quantize(("s", 2, 1))
         d_sign(2, 2)
         s_group(2, 2)
-        d_sign(1, 1)
-        quantize(("s", 2, 2))
         s_group(2, 3)
-        d_sign(0, 0)
+        quantize(("s", 2, 2))
         quantize(("s", 2, 3))
-        d_group(0)
+        d_sign(1, 1)
+        d_sign(0, 0)
         d_group(1)
-        quantize(("d", 0))
-        d_group(2)
+        d_group(0)
         quantize(("d", 1))
+        d_group(2)
+        quantize(("d", 0))
         h_group(0, 0, ZH, "s")
         for t in range(PACK):
             project(1, 1, (t,), range(G))
@@ -456,13 +461,13 @@ def tile_tomography_forward_transmission_d3_kernel(tc, F, S_bytes, S_scale, i0, 
         h_late_interleave(P * last, P)
         quantize(("h", 1, P * last))
         for z in range(TILES + 2):
-            detect(z, (0,), 0, B, z)
+            detect(z, (0,), 0, B, (PACK + z) % 8)
         for z in range(TILES + 2):
             detect(z, (1, 2), 0, B, None)
             store(z, 0, B, "s")
             if z == TILES - 1:
-                detect(last - 1, (0,), 0, B, last - 1)
-                for b0, bank in ((0, last), (BH, 0)):
+                detect(last - 1, (0,), 0, B, 2)
+                for b0, bank in ((0, 3), (BH, PACK)):
                     detect(last, (0,), b0, BH, bank)
         detect(last - 1, (1, 2), 0, B, None)
         store(last - 1, 0, B, "s")

@@ -225,6 +225,11 @@ def tile_tomography_forward_transmission_d3_kernel(tc, F, S_bytes, S_scale, i0, 
             new_batch((("f", h, g), ZH))
             f_copy(h, g, (0, 1))
 
+        def warm_up(count):
+            bank = new_bank(PACK - 1)
+            for n in range(count):
+                nc.tensor.matmul(out=bank[:], lhsT=s_wide[0, 0][:, 0, 0:P], rhs=s_wide[0, 0][:, 0, :], start=True, stop=True)
+
         p_banks, h_place = {}, {}
         h_rows = {(c, 0): keep.tile([P, PACK, ZH], BF16, name="h_rows%d" % c, align_bytes=64)[:] for c in range(C)}
         h_rows[0, 1] = keep.tile([P, PACK, ZH], BF16, name="h_rows_second", align_bytes=64)[:]
@@ -332,7 +337,9 @@ def tile_tomography_forward_transmission_d3_kernel(tc, F, S_bytes, S_scale, i0, 
         s_group(0, 0)
         widen(0, 1, "v---")
         quantize(("s", 0, 0))
+        warm_up(3)
         turn(0, 0)
+        warm_up(2)
         f_empty(0, 0)
         s_group(0, 1)
         s_begin(0, 2, "vvss")

@@ -27,12 +27,7 @@ TILES = ZH // P
 BH = B // 2
 RUN = 4
 
-F_RAW_BUFS = 3
-F_PAIR_BUFS = 2
-WIDE_BUFS = 6
-WIDE_PAIR_BUFS = 1
-GROUPED_BUFS = 6
-Y_BUFS = 6
+RING = {"f_raw": 3, "f_pair": 2, "wide": 6, "grouped_v": 3, "grouped_s": 3, "y": 6}
 
 GUESS_SHIFT = 0.043
 GUESS_SLOPE = math.log(2.0) / 2.0**23
@@ -44,114 +39,35 @@ def tile_tomography_forward_transmission_d3_kernel(tc, F, S_bytes, S_scale, i0, 
     nc = tc.nc
     with ExitStack() as ctx:
         keep = ctx.enter_context(tc.tile_pool(name="keep", bufs=1))
-        ring = ctx.enter_context(tc.tile_pool(name="ring", bufs=1))
         psum = ctx.enter_context(tc.psum_pool(name="psum", bufs=1))
         ctx.enter_context(tc.manual_schedule())
 
-        scale_first = keep.tile([P, 1, PACK], F32, name="scale_first")
-        scale_rest = keep.tile([P, G - 1, PACK], F32, name="scale_rest")
-        scale_view = S_scale.rearrange("(g p j) o -> p g (j o)", p=P, j=PACK)
-        i0_t = keep.tile([P, C, PACK * PACK], BF16, name="i0_t")
-        i0_view = i0.rearrange("(c a r) -> a c r", c=C, r=PACK * PACK)
-        s_view = S_bytes.rearrange("(g p j) n -> g p j n", p=P, j=PACK)
-        f_view = F.rearrange("(h z p) (g k) -> h g p z k", p=P, z=TILES, k=KP)
-        f_pair_view = F.rearrange("(h z p) (g k) -> h g p z k", p=P, z=TILES, k=2 * KP)
-        d_view = D.rearrange("(c a j e) b -> c e a j b", c=C, j=PACK, e=PACK)
-        s_bytes, f_raw, d_raw = {}, {}, {}
+        tiles, plans, tenants, taken = {}, {}, {}, {}
 
-        def load_i0():
-            span = PACK * (PACK - 1) + 1
-            for e in range(PACK):
-                nc.sync.dma_start(out=i0_t[e:P:PACK, :, 0:span], in_=i0_view[:, :, e : e + span])
+        def plan(value, pool, place, shape, dtype):
+            if value not in plans:
+                plans[value] = (pool, place, shape, dtype)
+                tenants.setdefault(place, []).append(value)
 
-        def load_s_first(j0):
-            tile = keep.tile([P, 2, KP], U8, name="s_first_%d" % j0)
-            for j in (j0, j0 + 1):
-                s_bytes[0, 0, j] = tile[:, j - j0, :]
-            nc.sync.dma_start(out=tile[:], in_=s_view[0][:, j0 : j0 + 2, 0:KP])
+        def plan_ring(value, ring, shape, dtype):
+            if value not in plans:
+                taken[ring] = taken.get(ring, 0) + 1
+                plan(value, keep, "%s%d" % (ring, (taken[ring] - 1) % RING[ring]), shape, dtype)
 
-        def load_s(g, c0, c1):
-            tile = keep.tile([P, PACK, KP * (c1 - c0)], U8, name="s_bytes_%d_%d" % (g, c0))
-            for c in range(c0, c1):
-                for j in range(PACK):
-                    s_bytes[c, g, j] = tile[:, j, KP * (c - c0) : KP * (c - c0 + 1)]
-            nc.sync.dma_start(out=tile[:], in_=s_view[g][:, :, KP * c0 : KP * c1])
+        def plan_kept(value, shape, dtype):
+            plan(value, keep, "_".join(str(x) for x in value), shape, dtype)
 
-        def load_f(h, g):
-            tile = ring.tile([P, TILES, KP], BF16, name="f_raw", bufs=F_RAW_BUFS)
-            f_raw[h, g] = tile
-            nc.sync.dma_start(out=tile[:], in_=f_view[h, g])
+        def plan_bank(value, bank):
+            plan(value, psum, "bank%d" % bank, [P, KP], F32)
 
-        def load_f_pair(h, g0):
-            tile = ring.tile([P, TILES, 2 * KP], BF16, name="f_pair", bufs=F_PAIR_BUFS)
-            for g in (g0, g0 + 1):
-                f_raw[h, g] = tile[:, :, KP * (g - g0) : KP * (g - g0 + 1)]
-            nc.sync.dma_start(out=tile[:], in_=f_pair_view[h, g0 // 2])
-
-        def load_d(c0, c1):
-            tile = keep.tile([P, PACK, (c1 - c0) * B], BF16, name="d_raw%d" % c0)
-            d_raw[c0] = tile
-            for c in range(c0, c1):
-                for e in range(PACK):
-                    nc.sync.dma_start(out=tile[e:P:PACK, :, B * (c - c0) : B * (c - c0 + 1)], in_=d_view[c, e])
-
-        ident = keep.tile([P, P], F32, name="ident")
-
-        def new_bank(n):
-            return psum.tile([P, KP], F32, name="bank%d" % n)
-
-        i0_flat = i0_t[:].rearrange("p c r -> p (c r)")[:, 0 : C * PACK * PACK : PACK]
-        mag, sgn, guess, half_inv, root, ratio, d, ln_i0 = [
-            keep.tile([P, C * PACK], F32, name=name)[:] for name in ("mag", "sgn", "guess", "half_inv", "root", "ratio", "d", "ln_i0")
-        ]
-        one = keep.tile([P, 1], F32, name="one")
-        unread = keep.tile([P, 1], F32, name="unread")
-        series = [keep.tile([P, C * PACK], F32, name="series%d" % k)[:] for k in range(LOG_TERMS)]
-
-        def series_step(k):
-            n = LOG_TERMS - k
-            nc.vector.scalar_tensor_tensor(out=series[k], in0=series[k - 1], scalar=(-1.0) ** (n + 1) / n, in1=d, op0=ALU.add, op1=ALU.mult)
-
-        ln_steps = [
-            lambda: nc.scalar.activation(out=mag, in_=i0_flat, func=ACT.Abs),
-            lambda: nc.scalar.activation(out=guess, in_=mag.bitcast(U32), func=ACT.Identity, scale=GUESS_SLOPE, bias=GUESS_START),
-            lambda: nc.scalar.activation(out=half_inv, in_=guess, func=ACT.Exp, scale=-0.5),
-            lambda: nc.vector.tensor_tensor(out=root, in0=mag, in1=half_inv, op=ALU.mult),
-            lambda: nc.vector.tensor_tensor(out=ratio, in0=root, in1=half_inv, op=ALU.mult),
-            lambda: nc.vector.tensor_scalar(out=d, in0=ratio, scalar1=-1.0, scalar2=None, op0=ALU.add),
-            lambda: nc.vector.tensor_scalar(out=series[0], in0=d, scalar1=(-1.0) ** (LOG_TERMS + 1) / LOG_TERMS, scalar2=None, op0=ALU.mult),
-            lambda: series_step(1),
-            lambda: series_step(2),
-            lambda: series_step(3),
-            lambda: series_step(4),
-            lambda: nc.vector.tensor_tensor(out=ln_i0, in0=series[LOG_TERMS - 1], in1=guess, op=ALU.add),
-        ]
-
-        def ln_step():
-            ln_steps.pop(0)()
-
-        grouped, batches, codes, scales = {}, {}, {}, {}
-
-        def new_batch(*parts):
-            tile = ring.tile([P, PACK * sum(w for key, w in parts)], BF16, name="grouped", bufs=GROUPED_BUFS, align_bytes=64)
-            start = 0
-            for key, w in parts:
-                grouped[key] = tile[:, PACK * start : PACK * (start + w)]
-                start = start + w
-            batches[parts[0][0]] = (tile, parts)
-
-        def quantize(first_key):
-            tile, parts = batches[first_key]
-            width = sum(w for key, w in parts)
-            name = "_".join(str(x) for x in first_key)
-            code_tile = keep.tile([P, width], U32, name="codes_" + name, align_bytes=64)
-            scale_tile = keep.tile([P, width], U8, name="scales_" + name, align_bytes=64)
-            nc.vector.quantize_mx(out=code_tile[:].bitcast(FP8X4), scales=scale_tile[:], in_=tile[:])
-            start = 0
-            for key, w in parts:
-                codes[key] = code_tile[:, start : start + w]
-                scales[key] = scale_tile[:, start : start + w]
-                start = start + w
+        def tile_of(value):
+            if value not in tiles:
+                pool, place, shape, dtype = plans[value]
+                if pool is psum:
+                    tiles[value] = pool.tile(shape, dtype, name=place)
+                else:
+                    tiles[value] = pool.tile(shape, dtype, name=place, align_bytes=64)
+            return tiles[value]
 
         def copy_on(engine, dst, src):
             if engine == "v":
@@ -159,326 +75,351 @@ def tile_tomography_forward_transmission_d3_kernel(tc, F, S_bytes, S_scale, i0, 
             else:
                 nc.scalar.copy(out=dst, in_=src)
 
-        def interleave(engine, dst, rows):
-            copy_on(engine, dst.rearrange("p (q i j) -> p q j i", i=RUN, j=PACK), rows.rearrange("p j (q i) -> p q j i", i=RUN))
+        scale_view = S_scale.rearrange("(g p j) o -> p g (j o)", p=P, j=PACK)
+        i0_view = i0.rearrange("(c a r) -> a c r", c=C, r=PACK * PACK)
+        s_view = S_bytes.rearrange("(g p j) n -> g p j n", p=P, j=PACK)
+        d_view = D.rearrange("(c a j e) b -> c e a j b", c=C, j=PACK, e=PACK)
+        row_of, scale_of, f_of = {}, {}, {}
 
-        s_wide, s_place = {}, {}
+        def load_scales(g0, g1):
+            value = ("scale", g0)
+            plan_kept(value, [P, g1 - g0, PACK], F32)
+            for g in range(g0, g1):
+                scale_of[g] = (value, g - g0)
+            return (lambda: nc.sync.dma_start(out=tile_of(value)[:], in_=scale_view[:, g0:g1, :]), [], [value])
 
-        def new_wide(c, passes):
-            n = len(passes)
-            bufs = WIDE_BUFS if n == 1 else WIDE_PAIR_BUFS
-            tile = ring.tile([P, PACK, n * KP], BF16, name="s_wide%d" % n, bufs=bufs, align_bytes=64)
-            for u, g in enumerate(passes):
-                s_wide[c, g] = tile[:, :, KP * u : KP * (u + 1)]
-                s_place[c, g] = (passes[0], n, u)
-            s_wide["all", c, passes[0]] = tile
+        def load_s(g, j0, j1, c0, c1):
+            value = ("s_bytes", g, j0, c0)
+            plan_kept(value, [P, j1 - j0, KP * (c1 - c0)], U8)
+            for c in range(c0, c1):
+                for j in range(j0, j1):
+                    row_of[c, g, j] = (value, j - j0, KP * (c - c0))
+            return (lambda: nc.sync.dma_start(out=tile_of(value)[:], in_=s_view[g][:, j0:j1, KP * c0 : KP * c1]), [], [value])
 
-        def widen(c, g, engines):
-            for j in range(PACK):
-                src = s_bytes[c, g, j].bitcast(FP8)
-                dst = s_wide[c, g][:, j, :]
-                scale = scale_first[:, 0, j : j + 1] if g == 0 else scale_rest[:, g - 1, j : j + 1]
-                if engines[j] == "v":
-                    nc.vector.tensor_scalar(out=dst, in0=src, scalar1=scale, scalar2=None, op0=ALU.mult)
-                elif engines[j] == "s":
-                    nc.scalar.activation(out=dst, in_=src, func=ACT.Copy, scale=scale)
+        def load_f(h, g0, n):
+            value = ("f_raw", h, g0)
+            plan_ring(value, "f_raw" if n == 1 else "f_pair", [P, TILES, n * KP], BF16)
+            for g in range(g0, g0 + n):
+                f_of[h, g] = (value, KP * (g - g0))
+            view = F.rearrange("(h z p) k -> h p z k", p=P, z=TILES)[h][:, :, KP * g0 : KP * (g0 + n)]
+            return (lambda: nc.sync.dma_start(out=tile_of(value)[:], in_=view), [], [value])
 
-        def s_interleave(c, g0):
-            src = s_wide["all", c, g0][:].rearrange("p j (q t e) -> p t q j e", t=PACK, e=PACK)
-            dst = grouped["s", c, g0].rearrange("p (t q e j) -> p t q j e", t=PACK, e=PACK, j=PACK)
-            nc.vector.tensor_copy(out=dst, in_=src)
+        def load_i0(e):
+            span = PACK * (PACK - 1) + 1
+            plan_kept(("i0",), [P, C, PACK * PACK], BF16)
+            return (lambda: nc.sync.dma_start(out=tile_of(("i0",))[e:P:PACK, :, 0:span], in_=i0_view[:, :, e : e + span]), [], [("i0",)])
 
-        def s_slice(table, c, g, t):
-            g0, n, u = s_place[c, g]
-            return table["s", c, g0][:, P * (n * t + u) : P * (n * t + u + 1)]
+        def load_d(c, e):
+            plan_kept(("d_raw", c), [P, PACK, B], BF16)
+            return (lambda: nc.sync.dma_start(out=tile_of(("d_raw", c))[e:P:PACK, :, :], in_=d_view[c, e]), [], [("d_raw", c)])
 
-        def s_begin(c, g, engines):
-            new_wide(c, (g,))
-            widen(c, g, engines)
+        ident = keep.tile([P, P], F32, name="ident")
 
-        def s_group(c, g):
-            new_batch((("s", c, g), KP))
-            s_interleave(c, g)
+        def small(name):
+            plan_kept((name,), [P, C * PACK], F32)
+            return tile_of((name,))[:]
 
-        f_banks = {}
+        def i0_flat():
+            return tile_of(("i0",))[:].rearrange("p c r -> p (c r)")[:, 0 : C * PACK * PACK : PACK]
 
-        def turn(h, g):
-            banks = []
-            f_banks[h, g] = banks
-            for z in range(TILES):
-                if z % 2 == 0:
-                    banks.append(new_bank(PACK + 2 * (g % 2) + z // 2))
-                words = f_raw[h, g][:, z, :].bitcast(F32)
-                for u in range(2):
-                    column = (2 * (z % 2) + u) * P
-                    nc.tensor.transpose(banks[-1][:, column : column + P], words[:, u : 2 * P : 2], ident[:])
+        def series_step(k):
+            n = LOG_TERMS - k
+            call = lambda: nc.vector.scalar_tensor_tensor(
+                out=small("series%d" % k), in0=small("series%d" % (k - 1)), scalar=(-1.0) ** (n + 1) / n, in1=small("d"), op0=ALU.add, op1=ALU.mult
+            )
+            return (call, [("series%d" % (k - 1),), ("d",)], [("series%d" % k,)])
 
-        def f_copy(h, g, order):
-            for b in order:
-                dst = grouped["f", h, g].bitcast(F32)[:, KP * b : KP * (b + 1)]
-                nc.scalar.copy(
-                    out=dst.rearrange("p (z r u) -> p z r u", z=2, u=2),
-                    in_=f_banks[h, g][b][:].rearrange("p (z u r) -> p z r u", z=2, u=2),
+        def product(name, a, b, op):
+            return (lambda: nc.vector.tensor_tensor(out=small(name), in0=small(a), in1=small(b), op=op), [(a,), (b,)], [(name,)])
+
+        def with_number(name, a, number, op):
+            return (lambda: nc.vector.tensor_scalar(out=small(name), in0=small(a), scalar1=number, scalar2=None, op0=op), [(a,)], [(name,)])
+
+        ln_scalar = [
+            (lambda: nc.scalar.activation(out=small("mag"), in_=i0_flat(), func=ACT.Abs), [("i0",)], [("mag",)]),
+            (lambda: nc.scalar.activation(out=small("sgn"), in_=i0_flat(), func=ACT.Sign), [("i0",)], [("sgn",)]),
+            (
+                lambda: nc.scalar.activation(out=small("guess"), in_=small("mag").bitcast(U32), func=ACT.Identity, scale=GUESS_SLOPE, bias=GUESS_START),
+                [("mag",)],
+                [("guess",)],
+            ),
+            (lambda: nc.scalar.activation(out=small("half_inv"), in_=small("guess"), func=ACT.Exp, scale=-0.5), [("guess",)], [("half_inv",)]),
+        ]
+        ln_vector = [
+            product("root", "mag", "half_inv", ALU.mult),
+            product("ratio", "root", "half_inv", ALU.mult),
+            with_number("d", "ratio", -1.0, ALU.add),
+            with_number("series0", "d", (-1.0) ** (LOG_TERMS + 1) / LOG_TERMS, ALU.mult),
+        ]
+        ln_vector.extend(series_step(k) for k in range(1, LOG_TERMS))
+        ln_vector.append(product("ln_i0", "series%d" % (LOG_TERMS - 1), "guess", ALU.add))
+
+        def quantize(*key):
+            width = plans[("grouped",) + key][2][1] // PACK
+            plan_kept(("codes",) + key, [P, width], U32)
+            plan_kept(("scales",) + key, [P, width], U8)
+            call = lambda: nc.vector.quantize_mx(
+                out=tile_of(("codes",) + key)[:].bitcast(FP8X4), scales=tile_of(("scales",) + key)[:], in_=tile_of(("grouped",) + key)[:]
+            )
+            return (call, [("grouped",) + key], [("codes",) + key, ("scales",) + key])
+
+        def operand(key, start, width):
+            return tile_of(("codes",) + key)[:, start : start + width].bitcast(FP8X4), tile_of(("scales",) + key)[:, start : start + width]
+
+        def mx_pass(bank_value, columns, lhs, rhs, first, last):
+            def call():
+                lhsT, lhsT_scale = operand(*lhs)
+                moving, moving_scale = operand(*rhs)
+                nc.tensor.matmul_mx(
+                    out=tile_of(bank_value)[:, 0:columns], lhsT=lhsT, lhsT_scale=lhsT_scale, rhs=moving, rhs_scale=moving_scale, start=first, stop=last
                 )
 
-        def f_empty(h, g):
-            new_batch((("f", h, g), ZH))
-            f_copy(h, g, (0, 1))
+            return (call, [("codes",) + lhs[0], ("codes",) + rhs[0]], [bank_value])
 
-        def warm_up(count):
-            bank = new_bank(PACK - 1)
-            for n in range(count):
-                nc.tensor.matmul(out=bank[:], lhsT=s_wide[0, 0][:, 0, 0:P], rhs=s_wide[0, 0][:, 0, :], start=True, stop=True)
+        def widen(engine, c, g, j):
+            plan_ring(("wide", c, g), "wide", [P, PACK, KP], BF16)
+            row, row_index, column = row_of[c, g, j]
+            scale_value, scale_index = scale_of[g]
 
-        p_banks, h_place = {}, {}
-        h_rows = {(c, 0): keep.tile([P, PACK, ZH], BF16, name="h_rows%d" % c, align_bytes=64)[:] for c in range(C)}
-        h_rows[0, 1] = keep.tile([P, PACK, ZH], BF16, name="h_rows_second", align_bytes=64)[:]
-        h_late = keep.tile([P, PACK, 2, ZH], BF16, name="h_late", align_bytes=64)
-        for c in (1, 2):
-            h_rows[c, 1] = h_late[:, :, c - 1, :]
+            def call():
+                src = tile_of(row)[:, row_index, column : column + KP].bitcast(FP8)
+                dst = tile_of(("wide", c, g))[:, j, :]
+                scale = tile_of(scale_value)[:, scale_index, j : j + 1]
+                if engine == "v":
+                    nc.vector.tensor_scalar(out=dst, in0=src, scalar1=scale, scalar2=None, op0=ALU.mult)
+                else:
+                    nc.scalar.activation(out=dst, in_=src, func=ACT.Copy, scale=scale)
 
-        def project(c, h, slices, passes):
-            for t in slices:
-                for g in passes:
-                    if g == 0:
-                        p_banks[c, h, t] = new_bank(t if (c, h) == (0, 0) else PACK * (1 - h) + t)
-                    nc.tensor.matmul_mx(
-                        out=p_banks[c, h, t][:],
-                        lhsT=s_slice(codes, c, g, t).bitcast(FP8X4),
-                        lhsT_scale=s_slice(scales, c, g, t),
-                        rhs=codes["f", h, g].bitcast(FP8X4),
-                        rhs_scale=scales["f", h, g],
-                        start=(g == 0),
-                        stop=(g == G - 1),
-                    )
+            return (call, [row, scale_value], [("wide", c, g)])
 
-        def attenuate(c, h, slices):
-            for t in slices:
+        def s_group(c, g):
+            plan_ring(("wide", c, g), "wide", [P, PACK, KP], BF16)
+            value = ("grouped", "s", c, g)
+            plan_ring(value, "grouped_v", [P, PACK * KP], BF16)
+
+            def call():
+                src = tile_of(("wide", c, g))[:].rearrange("p j (a t e) -> p t a j e", t=PACK, e=PACK)
+                dst = tile_of(value)[:].rearrange("p (t a e j) -> p t a j e", t=PACK, e=PACK, j=PACK)
+                nc.vector.tensor_copy(out=dst, in_=src)
+
+            return (call, [("wide", c, g)], [value])
+
+        def turn(h, g, b, bank):
+            value = ("turned", h, g, b)
+            plan_bank(value, bank)
+            raw, column = f_of[h, g]
+
+            def call():
+                for z in range(2):
+                    words = tile_of(raw)[:, 2 * b + z, column : column + KP].bitcast(F32)
+                    for u in range(2):
+                        start = (2 * z + u) * P
+                        nc.tensor.transpose(tile_of(value)[:, start : start + P], words[:, u : 2 * P : 2], ident[:])
+
+            return (call, [raw], [value])
+
+        def f_copy(engine, h, g, b):
+            value = ("grouped", "f", h, g)
+            plan_ring(value, "grouped_s", [P, PACK * ZH], BF16)
+
+            def call():
+                dst = tile_of(value)[:].bitcast(F32)[:, KP * b : KP * (b + 1)]
+                src = tile_of(("turned", h, g, b))[:]
+                copy_on(engine, dst.rearrange("p (z r u) -> p z r u", z=2, u=2), src.rearrange("p (z u r) -> p z r u", z=2, u=2))
+
+            return (call, [("turned", h, g, b)], [value])
+
+        def warm_up(name, count, bank, row):
+            value = ("unread", name)
+            plan_bank(value, bank)
+
+            def call():
+                rows = tile_of(("wide", 0, 0))
+                for n in range(count):
+                    nc.tensor.matmul(out=tile_of(value)[:], lhsT=rows[:, row, 0:P], rhs=rows[:, row, :], start=True, stop=True)
+
+            return (call, [("wide", 0, 0)], [value])
+
+        h_place = {}
+
+        def project(c, h, t, passes, bank=None):
+            if bank is not None:
+                plan_bank(("p", c, h, t), bank)
+            return [mx_pass(("p", c, h, t), ZH, (("s", c, g), P * t, P), (("f", h, g), 0, ZH), g == 0, g == G - 1) for g in passes]
+
+        h_tiles = {(c0, h): keep.tile([P, PACK, n, ZH], BF16, name="h_rows%d_%d" % (c0, h), align_bytes=64) for c0, n in ((0, 1), (1, 2)) for h in range(2)}
+
+        def attenuate(c, h, t):
+            def call():
                 nc.scalar.activation(
-                    out=h_rows[c, h][:, t, :],
-                    in_=p_banks[c, h, t][:],
+                    out=h_tiles[min(c, 1), h][:, t, c - min(c, 1), :],
+                    in_=tile_of(("p", c, h, t))[:],
                     func=ACT.Exp,
-                    bias=ln_i0[:, PACK * c + t : PACK * c + t + 1],
+                    bias=small("ln_i0")[:, PACK * c + t : PACK * c + t + 1],
                     scale=-1.0,
                 )
 
-        def h_part(c, z0, w):
-            for k in range(w // P):
-                h_place[c, z0 // P + k] = (("h", c, z0), P * k)
-            return (("h", c, z0), w)
+            return (call, [("p", c, h, t), ("ln_i0",)], [("h_rows", c, h)])
 
-        def h_interleave(c, z0, w, engine):
-            h, z1 = divmod(z0, ZH)
-            interleave(engine, grouped["h", c, z0], h_rows[c, h][:, :, z1 : z1 + w])
+        def h_group(engine, c0, c1, z0, n):
+            value = ("grouped", "h", c0, z0)
+            w = n * P
+            plan_ring(value, "grouped_" + engine, [P, (c1 - c0) * PACK * w], BF16)
+            for c in range(c0, c1):
+                for z in range(z0, z0 + n):
+                    h_place[c, z] = (("h", c0, z0), w * (c - c0) + P * (z - z0), P)
+            h, z1 = divmod(z0 * P, ZH)
+            first = c0 - min(c0, 1)
 
-        def h_late_interleave(z0, w):
-            new_batch(h_part(1, z0, w), h_part(2, z0, w))
-            src = h_late[:, :, :, z0 - ZH : z0 - ZH + w].rearrange("p j c (q i) -> p c q j i", i=RUN)
-            dst = batches["h", 1, z0][0][:].rearrange("p (c q i j) -> p c q j i", c=2, i=RUN, j=PACK)
-            nc.vector.tensor_copy(out=dst, in_=src)
+            def call():
+                rows = h_tiles[min(c0, 1), h][:, :, first : first + c1 - c0, z1 : z1 + w]
+                dst = tile_of(value)[:].rearrange("p (c q i j) -> p c q j i", c=c1 - c0, i=RUN, j=PACK)
+                copy_on(engine, dst, rows.rearrange("p j c (q i) -> p c q j i", i=RUN))
 
-        def h_group(c, z0, w, engine):
-            new_batch(h_part(c, z0, w))
-            h_interleave(c, z0, w, engine)
+            return (call, [("h_rows", c, h) for c in range(c0, c1)], [value])
 
-        def d_sign(c0, c):
-            for j in range(PACK):
-                row = d_raw[c0][:, j, B * (c - c0) : B * (c - c0 + 1)]
-                nc.vector.tensor_scalar(out=row, in0=row, scalar1=sgn[:, PACK * c + j : PACK * c + j + 1], scalar2=None, op0=ALU.mult)
+        def d_sign(c, j):
+            def call():
+                row = tile_of(("d_raw", c))[:, j, :]
+                nc.vector.tensor_scalar(out=row, in0=row, scalar1=small("sgn")[:, PACK * c + j : PACK * c + j + 1], scalar2=None, op0=ALU.mult)
 
-        def d_group(c):
-            new_batch((("d", c), B))
-            interleave("v", grouped["d", c], d_raw[c][:])
+            return (call, [("d_raw", c), ("sgn",)], [("d_signed", c)])
 
-        y_banks = {}
+        def d_group(engine, c):
+            value = ("grouped", "d", c)
+            plan_ring(value, "grouped_" + engine, [P, PACK * B], BF16)
 
-        def detect(z, groups, b0, w, bank):
-            for c in groups:
-                if c == 0:
-                    y_banks[z, b0] = new_bank(bank)
-                key, start = h_place[c, z]
-                nc.tensor.matmul_mx(
-                    out=y_banks[z, b0][:, 0:w],
-                    lhsT=codes[key][:, start : start + P].bitcast(FP8X4),
-                    lhsT_scale=scales[key][:, start : start + P],
-                    rhs=codes["d", c][:, b0 : b0 + w].bitcast(FP8X4),
-                    rhs_scale=scales["d", c][:, b0 : b0 + w],
-                    start=(c == 0),
-                    stop=(c == C - 1),
-                )
+            def call():
+                dst = tile_of(value)[:].rearrange("p (q i j) -> p q j i", i=RUN, j=PACK)
+                copy_on(engine, dst, tile_of(("d_raw", c))[:].rearrange("p j (q i) -> p q j i", i=RUN))
 
-        def store(z, b0, w, engine):
-            y_tile = ring.tile([P, w], F32, name="y_tile", bufs=Y_BUFS)
-            copy_on(engine, y_tile[:], y_banks[z, b0][:, 0:w])
-            nc.sync.dma_start(out=out[P * z : P * (z + 1), b0 : b0 + w], in_=y_tile[:])
+            return (call, [("d_signed", c)], [value])
 
-        nc.sync.dma_start(out=scale_first[:], in_=scale_view[:, 0:1, :])
-        load_s_first(0)
-        load_s_first(2)
-        nc.sync.dma_start(out=scale_rest[:], in_=scale_view[:, 1:G, :])
-        for g in range(G):
-            if g + 1 < G:
-                load_s(g + 1, 0, 1)
-            load_f(0, g)
-            if g == 1:
-                load_i0()
-        for g in range(G):
-            load_s(g, 1, C)
-            if g < G // 2:
-                load_f_pair(1, 2 * g)
-        for c in range(C):
-            load_d(c, c + 1)
+        def detect(z, groups, b0, w, bank=None):
+            if bank is not None:
+                plan_bank(("y_sum", z, b0), bank)
+            return [mx_pass(("y_sum", z, b0), w, h_place[c, z], (("d", c), b0, w), c == groups[0], c == groups[-1]) for c in groups]
+
+        def y_copy(engine, z, b0, w):
+            plan_ring(("y", z, b0), "y", [P, w], F32)
+            return (lambda: copy_on(engine, tile_of(("y", z, b0))[:], tile_of(("y_sum", z, b0))[:, 0:w]), [("y_sum", z, b0)], [("y", z, b0)])
+
+        def store(z, b0, w):
+            return (lambda: nc.sync.dma_start(out=out[P * z : P * (z + 1), b0 : b0 + w], in_=tile_of(("y", z, b0))[:]), [("y", z, b0)], [])
+
+        sync = [load_scales(0, 1), load_s(0, 0, 2, 0, 1), load_s(0, 2, 4, 0, 1), load_scales(1, G), load_s(1, 0, 4, 0, 1)]
+        sync += [load_f(0, 0, 1), load_s(2, 0, 4, 0, 1), load_f(0, 1, 1)] + [load_i0(e) for e in range(PACK)] + [load_s(3, 0, 4, 0, 1), load_f(0, 2, 1), load_f(0, 3, 1)]
+        sync += [load_s(0, 0, 4, 1, C), load_f(1, 0, 2), load_s(1, 0, 4, 1, C), load_f(1, 2, 2), load_s(2, 0, 4, 1, C), load_s(3, 0, 4, 1, C)]
+        sync += [load_d(c, e) for c in range(C) for e in range(PACK)]
+        for c, g in [(0, 0), (0, 1), (0, 2), (0, 3), (1, 0), (2, 0), (1, 1), (1, 2), (1, 3), (2, 1), (2, 2), (2, 3)]:
+            plan_ring(("wide", c, g), "wide", [P, PACK, KP], BF16)
+        for z in range(2 * TILES - 2):
+            plan_ring(("y", z, 0), "y", [P, B], F32)
+        for z in (2 * TILES - 2, 2 * TILES - 1):
+            for b0 in (0, BH):
+                plan_ring(("y", z, b0), "y", [P, BH], F32)
+        def rows(engine, c, g, js):
+            return [widen(engine, c, g, j) for j in js]
+
+        def empty(h, g):
+            return [f_copy("s", h, g, b) for b in range(2)]
+
+        def exps(c, h, ts=range(PACK)):
+            return [attenuate(c, h, t) for t in ts]
+
+        def weave(a, b):
+            steps = []
+            for n in range(max(len(a), len(b))):
+                steps += a[n : n + 1] + b[n : n + 1]
+            return steps
+
+        def turns(h, g):
+            return [turn(h, g, b, PACK + 2 * (g % 2) + b) for b in range(2)]
+
+        def sweep(c, h, passes, first_bank=None):
+            steps = []
+            for t in range(PACK):
+                steps += project(c, h, t, passes, None if first_bank is None else first_bank + t)
+            return steps
+
+        last = 2 * TILES - 1
+
+        scalar = rows("s", 0, 0, (1, 3)) + rows("s", 0, 1, (1, 2, 3)) + empty(0, 0) + rows("s", 0, 2, (2, 3))
+        scalar += ln_scalar[0:2] + weave(empty(0, 1), ln_scalar[2:4]) + rows("s", 0, 3, (1, 2, 3)) + empty(0, 2) + empty(0, 3)
+        scalar += rows("s", 1, 0, (1, 2, 3)) + rows("s", 2, 0, (3,)) + exps(0, 0, (0, 1)) + empty(1, 0) + exps(0, 0, (2,)) + empty(1, 1) + exps(0, 0, (3,)) + empty(1, 2) + rows("s", 1, 2, (3,)) + empty(1, 3)
+        scalar += rows("s", 1, 3, (1, 2, 3)) + rows("s", 2, 0, (1, 2)) + rows("s", 2, 1, (1, 2, 3)) + exps(0, 1, (3, 2)) + rows("s", 2, 2, (1, 2, 3)) + exps(0, 1, (0, 1)) + rows("s", 2, 3, (1, 2, 3))
+        scalar += exps(1, 0, (2, 0, 1, 3)) + exps(1, 1) + exps(2, 0, (0, 1)) + [h_group("s", 0, 1, 0, 2)] + exps(2, 0, (2, 3)) + [h_group("s", 0, 1, 2, 2)] + exps(2, 1, (0, 1, 2))
+        scalar += [h_group("s", 0, 1, 4, 1), attenuate(2, 1, 3), y_copy("s", 0, 0, B), h_group("s", 0, 1, 5, 1), y_copy("s", 1, 0, B), y_copy("s", 2, 0, B)]
+        scalar += [h_group("s", 0, 1, 6, 1), y_copy("s", 3, 0, B), y_copy("s", 4, 0, B), h_group("s", 0, 1, 7, 1), y_copy("s", 6, 0, BH), y_copy("s", last, 0, BH)]
+
+        ln = ln_vector
+        vector = rows("v", 0, 0, (0, 2)) + [s_group(0, 0), widen("v", 0, 1, 0), quantize("s", 0, 0), s_group(0, 1)]
+        vector += rows("v", 0, 2, (0, 1)) + [quantize("f", 0, 0), quantize("s", 0, 1), s_group(0, 2)]
+        vector += weave([widen("v", 0, 3, 0), quantize("f", 0, 1), quantize("s", 0, 2), s_group(0, 3), quantize("f", 0, 2), quantize("s", 0, 3), quantize("f", 0, 3), widen("v", 1, 0, 0), widen("v", 2, 0, 0)], ln)
+        vector += [s_group(1, 0), widen("v", 1, 1, 0), quantize("s", 1, 0)] + rows("v", 1, 1, (1, 2, 3)) + [quantize("f", 1, 0), s_group(1, 1), quantize("f", 1, 1)]
+        vector += rows("v", 1, 2, (0,)) + [quantize("s", 1, 1)] + rows("v", 1, 2, (1, 2)) + [quantize("f", 1, 2), s_group(1, 2), widen("v", 1, 3, 0), quantize("f", 1, 3), quantize("s", 1, 2)]
+        vector += [s_group(1, 3), widen("v", 2, 1, 0), quantize("s", 1, 3), s_group(2, 0), widen("v", 2, 2, 0), quantize("s", 2, 0), s_group(2, 1), widen("v", 2, 3, 0), quantize("s", 2, 1)]
+        vector += [s_group(2, 2), d_sign(0, 0), d_sign(0, 1), quantize("s", 2, 2), s_group(2, 3), d_sign(0, 2), d_sign(0, 3), quantize("s", 2, 3), d_group("v", 0)]
+        vector += [d_sign(1, j) for j in range(PACK)] + [quantize("d", 0), d_group("v", 1)] + [d_sign(2, j) for j in range(PACK)]
+        vector += [quantize("d", 1), d_group("v", 2), quantize("h", 0, 0), quantize("d", 2), h_group("v", 1, 3, 0, 1), h_group("v", 1, 3, 1, 1), quantize("h", 1, 0), quantize("h", 1, 1)]
+        vector += [h_group("v", 1, 3, 2, 2), quantize("h", 0, 2), quantize("h", 1, 2)]
+        vector += [h_group("v", 1, 3, TILES, 1)]
+        for z in range(TILES, last):
+            vector += [h_group("v", 1, 3, z + 1, 1), quantize("h", 0, z), quantize("h", 1, z)]
+        vector += [quantize("h", 1, last), y_copy("v", 5, 0, B), quantize("h", 0, last), y_copy("v", 6, BH, BH), y_copy("v", last, BH, BH)]
+
+        def quads(c, h, order, banks):
+            steps = []
+            for t, bank in zip(order, banks):
+                steps += project(c, h, t, range(G), bank)
+            return steps
+
+        tensor = [warm_up("first", 3, 3, 3)] + turns(0, 0) + [warm_up("second", 3, 3, 3)] + turns(0, 1) + sweep(0, 0, (0,), 0)
+        tensor += turns(0, 2) + project(0, 0, 0, (1,)) + turns(0, 3) + project(0, 0, 1, (1,)) + project(0, 0, 2, (1, 2)) + project(0, 0, 3, (1, 2))
+        tensor += project(0, 0, 0, (2, 3)) + project(0, 0, 1, (2, 3)) + turns(1, 0) + project(0, 0, 2, (3,)) + project(0, 0, 3, (3,))
+        tensor += turns(1, 1) + project(1, 0, 0, (0,), 0) + project(1, 0, 1, (0,), 1) + turns(1, 2) + project(0, 1, 0, (0, 1), 2) + turns(1, 3)
+        tensor += project(0, 1, 1, (0, 1), 3) + project(1, 0, 0, (1,)) + project(1, 0, 1, (1,)) + project(0, 1, 2, (0, 1, 2), 4) + project(0, 1, 3, range(G), 5)
+        tensor += project(0, 1, 2, (3,)) + project(0, 1, 0, (2, 3)) + project(0, 1, 1, (2, 3))
+        tensor += project(1, 0, 2, range(G), 6) + project(1, 0, 0, (2, 3)) + project(1, 0, 1, (2, 3)) + project(1, 0, 3, range(G), 7)
+        second, first = (5, 4, 2, 3), (6, 0, 1, 7)
+        tensor += quads(1, 1, range(PACK), second) + quads(2, 0, range(PACK), first) + quads(2, 1, range(PACK), second)
+        for z in range(last - 1):
+            tensor += detect(z, range(C), 0, B, (first + second)[z])
+        tensor += detect(last - 1, range(C), 0, BH, second[2]) + detect(last - 1, range(C), BH, BH, first[1])
+        tensor += detect(last, (1, 2, 0), 0, BH, second[3]) + detect(last, (1, 2, 0), BH, BH, first[0])
+        sync += [store(z, 0, B) for z in range(last - 1)] + [store(z, b0, BH) for z in (last - 1, last) for b0 in (0, BH)]
+
+        one = keep.tile([P, 1], F32, name="one")
+        unread = keep.tile([P, 1], F32, name="unread")
         nc.vector.memset(one[:], 1.0)
         nc.scalar.activation(out=unread[:], in_=one[:], func=ACT.Exp)
         make_identity(nc, ident[:])
 
-        s_begin(0, 0, "vsvv")
-        s_begin(0, 1, "-sss")
-        s_group(0, 0)
-        widen(0, 1, "v---")
-        quantize(("s", 0, 0))
-        warm_up(3)
-        turn(0, 0)
-        warm_up(2)
-        f_empty(0, 0)
-        s_group(0, 1)
-        s_begin(0, 2, "vvss")
-        quantize(("f", 0, 0))
-        quantize(("s", 0, 1))
-        turn(0, 1)
-        project(0, 0, (0, 1), (0,))
-        f_empty(0, 1)
-        ln_step()
-        nc.scalar.activation(out=sgn, in_=i0_flat, func=ACT.Sign)
-        s_group(0, 2)
-        s_begin(0, 3, "vs--")
-        ln_step()
-        widen(0, 3, "--s-")
-        ln_step()
-        widen(0, 3, "---s")
-        quantize(("f", 0, 1))
-        quantize(("s", 0, 2))
-        ln_step()
-        turn(0, 2)
-        project(0, 0, (2, 3), (0,))
-        f_empty(0, 2)
-        s_group(0, 3)
-        ln_step()
-        quantize(("f", 0, 2))
-        ln_step()
-        turn(0, 3)
-        f_empty(0, 3)
-        s_begin(1, 0, "vsss")
-        ln_step()
-        quantize(("s", 0, 3))
-        ln_step()
-        project(0, 0, range(PACK), (1,))
-        project(0, 0, range(PACK), (2,))
-        quantize(("f", 0, 3))
-        ln_step()
-        s_begin(2, 0, "--s-")
-        turn(1, 0)
-        f_empty(1, 0)
-        project(0, 0, (0, 1), (3,))
-        s_group(1, 0)
-        ln_step()
-        s_begin(1, 1, "vv--")
-        ln_step()
-        widen(1, 1, "--vs")
-        ln_step()
-        turn(1, 1)
-        f_empty(1, 1)
-        attenuate(0, 0, (0, 1))
-        project(0, 0, (2, 3), (3,))
-        quantize(("s", 1, 0))
-        quantize(("f", 1, 0))
-        s_group(1, 1)
-        quantize(("f", 1, 1))
-        turn(1, 2)
-        f_empty(1, 2)
-        attenuate(0, 0, (2, 3))
-        project(0, 1, (0, 1), (0,))
-        turn(1, 3)
-        f_empty(1, 3)
-        s_begin(1, 2, "vvvv")
-        quantize(("f", 1, 2))
-        quantize(("s", 1, 1))
-        quantize(("f", 1, 3))
-        s_group(1, 2)
-        project(0, 1, (0, 1), (1,))
-        project(0, 1, (2, 3), (0, 1))
-        project(0, 1, range(PACK), (2,))
-        project(0, 1, range(PACK), (3,))
-        s_begin(1, 3, "vsss")
-        widen(2, 0, "vs-s")
-        quantize(("s", 1, 2))
-        s_group(1, 3)
-        s_begin(2, 1, "vsss")
-        attenuate(0, 1, range(PACK))
-        quantize(("s", 1, 3))
-        project(1, 0, range(PACK), (0, 1))
-        project(1, 0, range(PACK), (2, 3))
-        s_group(2, 0)
-        s_begin(2, 2, "vsss")
-        quantize(("s", 2, 0))
-        s_group(2, 1)
-        s_begin(2, 3, "vsss")
-        attenuate(1, 0, range(PACK))
-        quantize(("s", 2, 1))
-        d_sign(2, 2)
-        s_group(2, 2)
-        s_group(2, 3)
-        quantize(("s", 2, 2))
-        quantize(("s", 2, 3))
-        d_sign(1, 1)
-        d_sign(0, 0)
-        d_group(1)
-        d_group(0)
-        quantize(("d", 1))
-        d_group(2)
-        quantize(("d", 0))
-        h_group(0, 0, ZH, "s")
-        for t in range(PACK):
-            project(1, 1, (t,), range(G))
-            attenuate(1, 1, (t,))
-        project(2, 0, range(PACK), (0, 1))
-        project(2, 0, range(PACK), (2, 3))
-        attenuate(2, 0, range(PACK))
-        h_group(0, ZH, ZQ, "s")
-        quantize(("h", 0, 0))
-        h_group(1, 0, ZQ, "v")
-        quantize(("d", 2))
-        h_group(2, 0, ZQ, "v")
-        quantize(("h", 1, 0))
-        quantize(("h", 0, ZH))
-        quantize(("h", 2, 0))
-        for t in range(PACK):
-            project(2, 1, (t,), range(G))
-            attenuate(2, 1, (t,))
-        h_group(0, ZH + ZQ, ZQ, "s")
-        h_group(1, ZQ, ZQ, "v")
-        h_group(2, ZQ, ZQ, "v")
-        quantize(("h", 1, ZQ))
-        quantize(("h", 2, ZQ))
-        last = 2 * TILES - 1
-        for z in range(TILES, last):
-            h_late_interleave(P * z, P)
-            quantize(("h", 0, ZH + ZQ) if z == TILES else ("h", 1, P * (z - 1)))
-        quantize(("h", 1, P * (last - 1)))
-        h_late_interleave(P * last, P)
-        quantize(("h", 1, P * last))
-        for z in range(TILES + 2):
-            detect(z, (0,), 0, B, (PACK + z) % 8)
-        for z in range(TILES + 2):
-            detect(z, (1, 2), 0, B, None)
-            store(z, 0, B, "s")
-            if z == TILES - 1:
-                detect(last - 1, (0,), 0, B, 2)
-                for b0, bank in ((0, 3), (BH, PACK)):
-                    detect(last, (0,), b0, BH, bank)
-        detect(last - 1, (1, 2), 0, B, None)
-        store(last - 1, 0, B, "s")
-        detect(last, (1, 2), 0, BH, None)
-        store(last, 0, BH, "v")
-        detect(last, (1, 2), BH, BH, None)
-        store(last, BH, BH, "s")
+        lists = [sync, tensor, vector, scalar]
+        unwritten, unread_by = {}, {}
+        for steps in lists:
+            for call, reads, writes in steps:
+                for value in reads:
+                    unread_by[value] = unread_by.get(value, 0) + 1
+                for value in writes:
+                    unwritten[value] = unwritten.get(value, 0) + 1
+
+        def place_is_free(value):
+            if value not in plans:
+                return True
+            queue = tenants[plans[value][1]]
+            return all(unwritten[v] == 0 and unread_by.get(v, 0) == 0 for v in queue[: queue.index(value)])
+
+        position = [0] * len(lists)
+        for turn_of_the_loop in range(sum(len(steps) for steps in lists)):
+            for n, steps in enumerate(lists):
+                if position[n] < len(steps):
+                    call, reads, writes = steps[position[n]]
+                    if all(unwritten[v] == 0 for v in reads) and all(place_is_free(v) for v in writes):
+                        call()
+                        for value in reads:
+                            unread_by[value] = unread_by[value] - 1
+                        for value in writes:
+                            unwritten[value] = unwritten[value] - 1
+                        position[n] = position[n] + 1
+        assert position == [len(steps) for steps in lists], position

@@ -27,12 +27,14 @@ TILES = ZH // P
 BH = B // 2
 RUN = 4
 
-RING = {"f_raw": 3, "f_pair": 2, "wide": 6, "grouped_v": 3, "grouped_s": 3, "y": 6}
+RING = {"f_raw": 3, "grouped": 5, "y": 10}
 
 GUESS_SHIFT = 0.043
 GUESS_SLOPE = math.log(2.0) / 2.0**23
 GUESS_START = (GUESS_SHIFT - 127.0) * math.log(2.0)
-LOG_TERMS = 5
+REACH = 0.031
+LOG_IN_D = [0.0, 1.0 - REACH**4 / 16.0, -0.5, 1.0 / 3.0 + REACH**2 / 4.0, -0.25]
+LOG_IN_R = [sum(LOG_IN_D[n] * math.factorial(n) / (math.factorial(k) * math.factorial(n - k)) * (-1.0) ** (n - k) for n in range(k, 5)) for k in range(5)]
 
 
 def tile_tomography_forward_transmission_d3_kernel(tc, F, S_bytes, S_scale, i0, D, out):
@@ -96,9 +98,12 @@ def tile_tomography_forward_transmission_d3_kernel(tc, F, S_bytes, S_scale, i0, 
                     row_of[c, g, j] = (value, j - j0, KP * (c - c0))
             return (lambda: nc.sync.dma_start(out=tile_of(value)[:], in_=s_view[g][:, j0:j1, KP * c0 : KP * c1]), [], [value])
 
-        def load_f(h, g0, n):
+        def load_f(h, g0, n, place=None):
             value = ("f_raw", h, g0)
-            plan_ring(value, "f_raw" if n == 1 else "f_pair", [P, TILES, n * KP], BF16)
+            if place is None:
+                plan_ring(value, "f_raw", [P, TILES, n * KP], BF16)
+            else:
+                plan(value, keep, place, [P, TILES, n * KP], BF16)
             for g in range(g0, g0 + n):
                 f_of[h, g] = (value, KP * (g - g0))
             view = F.rearrange("(h z p) k -> h p z k", p=P, z=TILES)[h][:, :, KP * g0 : KP * (g0 + n)]
@@ -109,9 +114,12 @@ def tile_tomography_forward_transmission_d3_kernel(tc, F, S_bytes, S_scale, i0, 
             plan_kept(("i0",), [P, C, PACK * PACK], BF16)
             return (lambda: nc.sync.dma_start(out=tile_of(("i0",))[e:P:PACK, :, 0:span], in_=i0_view[:, :, e : e + span]), [], [("i0",)])
 
+        def d_rows(c):
+            plan_kept(("d_raw", c // 2), [P, PACK, (2 - c // 2) * B], BF16)
+            return tile_of(("d_raw", c // 2))[:, :, B * (c % 2) : B * (c % 2 + 1)]
+
         def load_d(c, e):
-            plan_kept(("d_raw", c), [P, PACK, B], BF16)
-            return (lambda: nc.sync.dma_start(out=tile_of(("d_raw", c))[e:P:PACK, :, :], in_=d_view[c, e]), [], [("d_raw", c)])
+            return (lambda: nc.sync.dma_start(out=d_rows(c)[e:P:PACK, :, :], in_=d_view[c, e]), [], [("d_rows", c)])
 
         ident = keep.tile([P, P], F32, name="ident")
 
@@ -122,12 +130,9 @@ def tile_tomography_forward_transmission_d3_kernel(tc, F, S_bytes, S_scale, i0, 
         def i0_flat():
             return tile_of(("i0",))[:].rearrange("p c r -> p (c r)")[:, 0 : C * PACK * PACK : PACK]
 
-        def series_step(k):
-            n = LOG_TERMS - k
-            call = lambda: nc.vector.scalar_tensor_tensor(
-                out=small("series%d" % k), in0=small("series%d" % (k - 1)), scalar=(-1.0) ** (n + 1) / n, in1=small("d"), op0=ALU.add, op1=ALU.mult
-            )
-            return (call, [("series%d" % (k - 1),), ("d",)], [("series%d" % k,)])
+        def horner(name, before, coefficient, other, op):
+            call = lambda: nc.vector.scalar_tensor_tensor(out=small(name), in0=small(before), scalar=coefficient, in1=small(other), op0=ALU.add, op1=op)
+            return (call, [(before,), (other,)], [(name,)])
 
         def product(name, a, b, op):
             return (lambda: nc.vector.tensor_tensor(out=small(name), in0=small(a), in1=small(b), op=op), [(a,), (b,)], [(name,)])
@@ -148,11 +153,28 @@ def tile_tomography_forward_transmission_d3_kernel(tc, F, S_bytes, S_scale, i0, 
         ln_vector = [
             product("root", "mag", "half_inv", ALU.mult),
             product("ratio", "root", "half_inv", ALU.mult),
-            with_number("d", "ratio", -1.0, ALU.add),
-            with_number("series0", "d", (-1.0) ** (LOG_TERMS + 1) / LOG_TERMS, ALU.mult),
+            with_number("power4", "ratio", LOG_IN_R[4], ALU.mult),
+            horner("power3", "power4", LOG_IN_R[3], "ratio", ALU.mult),
+            horner("power2", "power3", LOG_IN_R[2], "ratio", ALU.mult),
+            horner("power1", "power2", LOG_IN_R[1], "ratio", ALU.mult),
+            horner("ln_i0", "power1", LOG_IN_R[0], "guess", ALU.add),
         ]
-        ln_vector.extend(series_step(k) for k in range(1, LOG_TERMS))
-        ln_vector.append(product("ln_i0", "series%d" % (LOG_TERMS - 1), "guess", ALU.add))
+
+        batch_of = {}
+
+        def together(*parts):
+            start = 0
+            for key, width in parts:
+                batch_of[key] = (parts[0][0], start, width)
+                start = start + width
+            plan_ring(("grouped",) + parts[0][0], "grouped", [P, PACK * start], BF16)
+
+        def grouped_value(key):
+            return ("grouped",) + batch_of[key][0]
+
+        def grouped_of(key):
+            batch, start, width = batch_of[key]
+            return tile_of(("grouped",) + batch)[:, PACK * start : PACK * (start + width)]
 
         def quantize(*key):
             width = plans[("grouped",) + key][2][1] // PACK
@@ -164,7 +186,9 @@ def tile_tomography_forward_transmission_d3_kernel(tc, F, S_bytes, S_scale, i0, 
             return (call, [("grouped",) + key], [("codes",) + key, ("scales",) + key])
 
         def operand(key, start, width):
-            return tile_of(("codes",) + key)[:, start : start + width].bitcast(FP8X4), tile_of(("scales",) + key)[:, start : start + width]
+            batch, first, whole = batch_of[key]
+            columns = slice(first + start, first + start + width)
+            return tile_of(("codes",) + batch)[:, columns].bitcast(FP8X4), tile_of(("scales",) + batch)[:, columns]
 
         def mx_pass(bank_value, columns, lhs, rhs, first, last):
             def call():
@@ -174,35 +198,42 @@ def tile_tomography_forward_transmission_d3_kernel(tc, F, S_bytes, S_scale, i0, 
                     out=tile_of(bank_value)[:, 0:columns], lhsT=lhsT, lhsT_scale=lhsT_scale, rhs=moving, rhs_scale=moving_scale, start=first, stop=last
                 )
 
-            return (call, [("codes",) + lhs[0], ("codes",) + rhs[0]], [bank_value])
+            return (call, [("codes",) + batch_of[lhs[0]][0], ("codes",) + batch_of[rhs[0]][0]], [bank_value])
 
-        def widen(engine, c, g, j):
-            plan_ring(("wide", c, g), "wide", [P, PACK, KP], BF16)
+        wide_of = {}
+
+        def plan_wide(place, *units):
+            value = ("wide",) + units[0]
+            plan(value, keep, place, [P, PACK, len(units) * KP], BF16)
+            for n, unit in enumerate(units):
+                wide_of[unit] = (value, KP * n)
+
+        def widen(engine, c, g, j, groups=1):
             row, row_index, column = row_of[c, g, j]
             scale_value, scale_index = scale_of[g]
+            wide, start = wide_of[c, g]
+            w = groups * KP
 
             def call():
-                src = tile_of(row)[:, row_index, column : column + KP].bitcast(FP8)
-                dst = tile_of(("wide", c, g))[:, j, :]
+                src = tile_of(row)[:, row_index, column : column + w].bitcast(FP8)
+                dst = tile_of(wide)[:, j, start : start + w]
                 scale = tile_of(scale_value)[:, scale_index, j : j + 1]
                 if engine == "v":
                     nc.vector.tensor_scalar(out=dst, in0=src, scalar1=scale, scalar2=None, op0=ALU.mult)
                 else:
                     nc.scalar.activation(out=dst, in_=src, func=ACT.Copy, scale=scale)
 
-            return (call, [row, scale_value], [("wide", c, g)])
+            return (call, [row, scale_value], [wide] + [("rows", c + n, g) for n in range(groups)])
 
         def s_group(c, g):
-            plan_ring(("wide", c, g), "wide", [P, PACK, KP], BF16)
-            value = ("grouped", "s", c, g)
-            plan_ring(value, "grouped_v", [P, PACK * KP], BF16)
+            wide, start = wide_of[c, g]
 
             def call():
-                src = tile_of(("wide", c, g))[:].rearrange("p j (a t e) -> p t a j e", t=PACK, e=PACK)
-                dst = tile_of(value)[:].rearrange("p (t a e j) -> p t a j e", t=PACK, e=PACK, j=PACK)
+                src = tile_of(wide)[:, :, start : start + KP].rearrange("p j (a t e) -> p t a j e", t=PACK, e=PACK)
+                dst = grouped_of(("s", c, g)).rearrange("p (t a e j) -> p t a j e", t=PACK, e=PACK, j=PACK)
                 nc.vector.tensor_copy(out=dst, in_=src)
 
-            return (call, [("wide", c, g)], [value])
+            return (call, [("rows", c, g)], [grouped_value(("s", c, g)), wide])
 
         def turn(h, g, b, bank):
             value = ("turned", h, g, b)
@@ -219,26 +250,24 @@ def tile_tomography_forward_transmission_d3_kernel(tc, F, S_bytes, S_scale, i0, 
             return (call, [raw], [value])
 
         def f_copy(engine, h, g, b):
-            value = ("grouped", "f", h, g)
-            plan_ring(value, "grouped_s", [P, PACK * ZH], BF16)
-
             def call():
-                dst = tile_of(value)[:].bitcast(F32)[:, KP * b : KP * (b + 1)]
+                dst = grouped_of(("f", h, g)).bitcast(F32)[:, KP * b : KP * (b + 1)]
                 src = tile_of(("turned", h, g, b))[:]
                 copy_on(engine, dst.rearrange("p (z r u) -> p z r u", z=2, u=2), src.rearrange("p (z u r) -> p z r u", z=2, u=2))
 
-            return (call, [("turned", h, g, b)], [value])
+            return (call, [("turned", h, g, b)], [grouped_value(("f", h, g))])
 
-        def warm_up(name, count, bank, row):
+        def warm_up(name, count, bank):
             value = ("unread", name)
             plan_bank(value, bank)
+            wide, start = wide_of[0, 0]
 
             def call():
-                rows = tile_of(("wide", 0, 0))
+                row = tile_of(wide)[:, 1, 0:KP]
                 for n in range(count):
-                    nc.tensor.matmul(out=tile_of(value)[:], lhsT=rows[:, row, 0:P], rhs=rows[:, row, :], start=True, stop=True)
+                    nc.tensor.matmul(out=tile_of(value)[:], lhsT=row[:, 0:P], rhs=row, start=True, stop=True)
 
-            return (call, [("wide", 0, 0)], [value])
+            return (call, [("rows", 0, 0)], [value, wide])
 
         h_place = {}
 
@@ -262,9 +291,7 @@ def tile_tomography_forward_transmission_d3_kernel(tc, F, S_bytes, S_scale, i0, 
             return (call, [("p", c, h, t), ("ln_i0",)], [("h_rows", c, h)])
 
         def h_group(engine, c0, c1, z0, n):
-            value = ("grouped", "h", c0, z0)
             w = n * P
-            plan_ring(value, "grouped_" + engine, [P, (c1 - c0) * PACK * w], BF16)
             for c in range(c0, c1):
                 for z in range(z0, z0 + n):
                     h_place[c, z] = (("h", c0, z0), w * (c - c0) + P * (z - z0), P)
@@ -273,27 +300,26 @@ def tile_tomography_forward_transmission_d3_kernel(tc, F, S_bytes, S_scale, i0, 
 
             def call():
                 rows = h_tiles[min(c0, 1), h][:, :, first : first + c1 - c0, z1 : z1 + w]
-                dst = tile_of(value)[:].rearrange("p (c q i j) -> p c q j i", c=c1 - c0, i=RUN, j=PACK)
+                dst = grouped_of(("h", c0, z0)).rearrange("p (c q i j) -> p c q j i", c=c1 - c0, i=RUN, j=PACK)
                 copy_on(engine, dst, rows.rearrange("p j c (q i) -> p c q j i", i=RUN))
 
-            return (call, [("h_rows", c, h) for c in range(c0, c1)], [value])
+            return (call, [("h_rows", c, h) for c in range(c0, c1)], [grouped_value(("h", c0, z0))])
 
         def d_sign(c, j):
             def call():
-                row = tile_of(("d_raw", c))[:, j, :]
+                row = d_rows(c)[:, j, :]
                 nc.vector.tensor_scalar(out=row, in0=row, scalar1=small("sgn")[:, PACK * c + j : PACK * c + j + 1], scalar2=None, op0=ALU.mult)
 
-            return (call, [("d_raw", c), ("sgn",)], [("d_signed", c)])
+            return (call, [("d_rows", c), ("sgn",)], [("d_signed", c // 2)])
 
-        def d_group(engine, c):
-            value = ("grouped", "d", c)
-            plan_ring(value, "grouped_" + engine, [P, PACK * B], BF16)
+        def d_group(c):
+            value = grouped_value(("d", c))
 
             def call():
                 dst = tile_of(value)[:].rearrange("p (q i j) -> p q j i", i=RUN, j=PACK)
-                copy_on(engine, dst, tile_of(("d_raw", c))[:].rearrange("p j (q i) -> p q j i", i=RUN))
+                nc.vector.tensor_copy(out=dst, in_=tile_of(("d_raw", c // 2))[:].rearrange("p j (q i) -> p q j i", i=RUN))
 
-            return (call, [("d_signed", c)], [value])
+            return (call, [("d_signed", c // 2)], [value])
 
         def detect(z, groups, b0, w, bank=None):
             if bank is not None:
@@ -309,15 +335,17 @@ def tile_tomography_forward_transmission_d3_kernel(tc, F, S_bytes, S_scale, i0, 
 
         sync = [load_scales(0, 1), load_s(0, 0, 2, 0, 1), load_s(0, 2, 4, 0, 1), load_scales(1, G), load_s(1, 0, 4, 0, 1)]
         sync += [load_f(0, 0, 1), load_s(2, 0, 4, 0, 1), load_f(0, 1, 1)] + [load_i0(e) for e in range(PACK)] + [load_s(3, 0, 4, 0, 1), load_f(0, 2, 1), load_f(0, 3, 1)]
-        sync += [load_s(0, 0, 4, 1, C), load_f(1, 0, 2), load_s(1, 0, 4, 1, C), load_f(1, 2, 2), load_s(2, 0, 4, 1, C), load_s(3, 0, 4, 1, C)]
+        sync += [load_s(0, 0, 4, 1, C), load_f(1, 0, 2, "late0"), load_s(1, 0, 4, 1, C), load_f(1, 2, 2, "late1"), load_s(2, 0, 4, 1, C), load_s(3, 0, 4, 1, C)]
         sync += [load_d(c, e) for c in range(C) for e in range(PACK)]
-        for c, g in [(0, 0), (0, 1), (0, 2), (0, 3), (1, 0), (2, 0), (1, 1), (1, 2), (1, 3), (2, 1), (2, 2), (2, 3)]:
-            plan_ring(("wide", c, g), "wide", [P, PACK, KP], BF16)
+        units = [(0, 0), (0, 1), (0, 2), (0, 3), (1, 0), (2, 0), (1, 1), (1, 2), (1, 3), (2, 1), (2, 2), (2, 3)]
+        for unit, place in zip(units, ["wide0", "wide1", "wide2"] * 2 + ["wide0", "wide1", "late0", "wide0", "late1", "wide1"]):
+            plan_wide(place, unit)
         for z in range(2 * TILES - 2):
             plan_ring(("y", z, 0), "y", [P, B], F32)
         for z in (2 * TILES - 2, 2 * TILES - 1):
             for b0 in (0, BH):
                 plan_ring(("y", z, b0), "y", [P, BH], F32)
+
         def rows(engine, c, g, js):
             return [widen(engine, c, g, j) for j in js]
 
@@ -336,57 +364,56 @@ def tile_tomography_forward_transmission_d3_kernel(tc, F, S_bytes, S_scale, i0, 
         def turns(h, g):
             return [turn(h, g, b, PACK + 2 * (g % 2) + b) for b in range(2)]
 
-        def sweep(c, h, passes, first_bank=None):
+        def sweep(c, h, passes, first_bank=None, slices=range(PACK)):
             steps = []
-            for t in range(PACK):
+            for t in slices:
                 steps += project(c, h, t, passes, None if first_bank is None else first_bank + t)
             return steps
 
         last = 2 * TILES - 1
 
-        scalar = rows("s", 0, 0, (1, 3)) + rows("s", 0, 1, (1, 2, 3)) + empty(0, 0) + rows("s", 0, 2, (2, 3))
-        scalar += ln_scalar[0:2] + weave(empty(0, 1), ln_scalar[2:4]) + rows("s", 0, 3, (1, 2, 3)) + empty(0, 2) + empty(0, 3)
-        scalar += rows("s", 1, 0, (1, 2, 3)) + rows("s", 2, 0, (3,)) + exps(0, 0, (0, 1)) + empty(1, 0) + exps(0, 0, (2,)) + empty(1, 1) + exps(0, 0, (3,)) + empty(1, 2) + rows("s", 1, 2, (3,)) + empty(1, 3)
-        scalar += rows("s", 1, 3, (1, 2, 3)) + rows("s", 2, 0, (1, 2)) + rows("s", 2, 1, (1, 2, 3)) + exps(0, 1, (3, 2)) + rows("s", 2, 2, (1, 2, 3)) + exps(0, 1, (0, 1)) + rows("s", 2, 3, (1, 2, 3))
-        scalar += exps(1, 0, (2, 0, 1, 3)) + exps(1, 1) + exps(2, 0, (0, 1)) + [h_group("s", 0, 1, 0, 2)] + exps(2, 0, (2, 3)) + [h_group("s", 0, 1, 2, 2)] + exps(2, 1, (0, 1, 2))
-        scalar += [h_group("s", 0, 1, 4, 1), attenuate(2, 1, 3), y_copy("s", 0, 0, B), h_group("s", 0, 1, 5, 1), y_copy("s", 1, 0, B), y_copy("s", 2, 0, B)]
-        scalar += [h_group("s", 0, 1, 6, 1), y_copy("s", 3, 0, B), y_copy("s", 4, 0, B), h_group("s", 0, 1, 7, 1), y_copy("s", 6, 0, BH), y_copy("s", last, 0, BH)]
+        for key in [("s", 0, 0), ("f", 0, 0), ("s", 0, 1), ("f", 0, 1), ("s", 0, 2), ("f", 0, 2), ("s", 0, 3), ("f", 0, 3), ("s", 1, 0)]:
+            together((key, KP))
+        together((("s", 1, 1), KP))
+        together((("f", 1, 0), ZH), (("f", 1, 1), ZH))
+        together((("f", 1, 2), ZH), (("f", 1, 3), ZH))
+        for c, g in ((1, 2), (2, 0), (2, 2)):
+            together((("s", c, g), KP), (("s", c, g + 1), KP))
+        together((("d", 0), B), (("d", 1), B))
+        together((("d", 2), B))
+        for z in range(2 * TILES):
+            together((("h", 0, z), P), (("h", 1, z), 2 * P))
+
+        scalar = rows("s", 0, 0, (1,)) + rows("s", 0, 1, (1, 2, 3)) + empty(0, 0) + rows("s", 0, 2, (2, 3))
+        scalar += ln_scalar[0:2] + weave(empty(0, 1), ln_scalar[2:4]) + rows("s", 0, 3, (1, 2, 3)) + empty(0, 2) + rows("s", 1, 0, (1,)) + empty(0, 3)
+        scalar += rows("s", 1, 0, (2,)) + rows("s", 1, 0, (3,)) + rows("s", 2, 0, (2, 3)) + empty(1, 0) + exps(0, 0, (0, 1)) + empty(1, 1) + exps(0, 0, (2,)) + empty(1, 2) + exps(0, 0, (3,)) + empty(1, 3) + rows("s", 1, 2, (3,))
+        scalar += rows("s", 1, 3, (1, 2, 3)) + rows("s", 2, 0, (1,)) + rows("s", 2, 1, (1, 2, 3)) + exps(0, 1, (3, 0)) + rows("s", 2, 2, (1, 2, 3)) + exps(0, 1, (1, 2)) + rows("s", 2, 3, (1, 2, 3))
+        scalar += exps(1, 0) + exps(1, 1, (3, 0, 1, 2)) + exps(2, 0, (0, 1)) + [h_group("s", 0, 1, 0, 1)] + exps(2, 0, (2, 3)) + weave([h_group("s", 0, 1, z, 1) for z in (1, 2, 3)], exps(2, 1, (0, 1, 2)))
+        scalar += [h_group("s", 0, 1, 4, 1), attenuate(2, 1, 3), y_copy("s", 0, 0, B), h_group("s", 0, 1, 5, 1), y_copy("s", 1, 0, B), h_group("s", 0, 1, 6, 1), y_copy("s", 2, 0, B)]
+        scalar += [h_group("s", 0, 1, 7, 1), y_copy("s", 3, 0, B), y_copy("s", 4, 0, B), y_copy("s", 5, 0, B), y_copy("s", 6, 0, BH), y_copy("s", last, 0, BH)]
 
         ln = ln_vector
-        vector = rows("v", 0, 0, (0, 2)) + [s_group(0, 0), widen("v", 0, 1, 0), quantize("s", 0, 0), s_group(0, 1)]
+        vector = rows("v", 0, 0, (0, 2, 3)) + [s_group(0, 0), widen("v", 0, 1, 0), quantize("s", 0, 0), s_group(0, 1)]
         vector += rows("v", 0, 2, (0, 1)) + [quantize("f", 0, 0), quantize("s", 0, 1), s_group(0, 2)]
-        vector += weave([widen("v", 0, 3, 0), quantize("f", 0, 1), quantize("s", 0, 2), s_group(0, 3), quantize("f", 0, 2), quantize("s", 0, 3), quantize("f", 0, 3), widen("v", 1, 0, 0), widen("v", 2, 0, 0)], ln)
-        vector += [s_group(1, 0), widen("v", 1, 1, 0), quantize("s", 1, 0)] + rows("v", 1, 1, (1, 2, 3)) + [quantize("f", 1, 0), s_group(1, 1), quantize("f", 1, 1)]
-        vector += rows("v", 1, 2, (0,)) + [quantize("s", 1, 1)] + rows("v", 1, 2, (1, 2)) + [quantize("f", 1, 2), s_group(1, 2), widen("v", 1, 3, 0), quantize("f", 1, 3), quantize("s", 1, 2)]
-        vector += [s_group(1, 3), widen("v", 2, 1, 0), quantize("s", 1, 3), s_group(2, 0), widen("v", 2, 2, 0), quantize("s", 2, 0), s_group(2, 1), widen("v", 2, 3, 0), quantize("s", 2, 1)]
-        vector += [s_group(2, 2), d_sign(0, 0), d_sign(0, 1), quantize("s", 2, 2), s_group(2, 3), d_sign(0, 2), d_sign(0, 3), quantize("s", 2, 3), d_group("v", 0)]
-        vector += [d_sign(1, j) for j in range(PACK)] + [quantize("d", 0), d_group("v", 1)] + [d_sign(2, j) for j in range(PACK)]
-        vector += [quantize("d", 1), d_group("v", 2), quantize("h", 0, 0), quantize("d", 2), h_group("v", 1, 3, 0, 1), h_group("v", 1, 3, 1, 1), quantize("h", 1, 0), quantize("h", 1, 1)]
-        vector += [h_group("v", 1, 3, 2, 2), quantize("h", 0, 2), quantize("h", 1, 2)]
-        vector += [h_group("v", 1, 3, TILES, 1)]
-        for z in range(TILES, last):
-            vector += [h_group("v", 1, 3, z + 1, 1), quantize("h", 0, z), quantize("h", 1, z)]
-        vector += [quantize("h", 1, last), y_copy("v", 5, 0, B), quantize("h", 0, last), y_copy("v", 6, BH, BH), y_copy("v", last, BH, BH)]
+        vector += weave([widen("v", 0, 3, 0), quantize("f", 0, 1), quantize("s", 0, 2), s_group(0, 3), quantize("f", 0, 2), quantize("s", 0, 3), widen("v", 1, 0, 0), quantize("f", 0, 3), widen("v", 2, 0, 0)], ln)
+        vector += [s_group(1, 0)] + rows("v", 1, 1, range(PACK)) + [quantize("s", 1, 0), s_group(1, 1), quantize("f", 1, 0), quantize("s", 1, 1)]
+        vector += rows("v", 1, 2, (0, 1, 2)) + [widen("v", 1, 3, 0), widen("v", 2, 1, 0), quantize("f", 1, 2), s_group(1, 2), s_group(1, 3), widen("v", 2, 2, 0), quantize("s", 1, 2)]
+        vector += [s_group(2, 0), s_group(2, 1), widen("v", 2, 3, 0), quantize("s", 2, 0), s_group(2, 2)] + [d_sign(0, j) for j in range(PACK)]
+        vector += [s_group(2, 3), d_sign(1, 0), d_sign(1, 1), quantize("s", 2, 2), d_sign(1, 2), d_sign(1, 3)] + [d_sign(2, j) for j in (0, 1)] + [d_group(0)]
+        vector += [d_sign(2, j) for j in (2, 3)] + [quantize("d", 0), d_group(2), h_group("v", 1, 3, 0, 1), quantize("d", 2)]
+        for z in range(last):
+            vector += [h_group("v", 1, 3, z + 1, 1), quantize("h", 0, z)]
+        vector += [quantize("h", 0, last), y_copy("v", 6, BH, BH), y_copy("v", last, BH, BH)]
 
-        def quads(c, h, order, banks):
-            steps = []
-            for t, bank in zip(order, banks):
-                steps += project(c, h, t, range(G), bank)
-            return steps
-
-        tensor = [warm_up("first", 3, 3, 3)] + turns(0, 0) + [warm_up("second", 3, 3, 3)] + turns(0, 1) + sweep(0, 0, (0,), 0)
-        tensor += turns(0, 2) + project(0, 0, 0, (1,)) + turns(0, 3) + project(0, 0, 1, (1,)) + project(0, 0, 2, (1, 2)) + project(0, 0, 3, (1, 2))
-        tensor += project(0, 0, 0, (2, 3)) + project(0, 0, 1, (2, 3)) + turns(1, 0) + project(0, 0, 2, (3,)) + project(0, 0, 3, (3,))
-        tensor += turns(1, 1) + project(1, 0, 0, (0,), 0) + project(1, 0, 1, (0,), 1) + turns(1, 2) + project(0, 1, 0, (0, 1), 2) + turns(1, 3)
-        tensor += project(0, 1, 1, (0, 1), 3) + project(1, 0, 0, (1,)) + project(1, 0, 1, (1,)) + project(0, 1, 2, (0, 1, 2), 4) + project(0, 1, 3, range(G), 5)
-        tensor += project(0, 1, 2, (3,)) + project(0, 1, 0, (2, 3)) + project(0, 1, 1, (2, 3))
-        tensor += project(1, 0, 2, range(G), 6) + project(1, 0, 0, (2, 3)) + project(1, 0, 1, (2, 3)) + project(1, 0, 3, range(G), 7)
-        second, first = (5, 4, 2, 3), (6, 0, 1, 7)
-        tensor += quads(1, 1, range(PACK), second) + quads(2, 0, range(PACK), first) + quads(2, 1, range(PACK), second)
+        tensor = [warm_up("first", 3, 3)] + turns(0, 0) + [warm_up("second", 3, 3)] + turns(0, 1) + sweep(0, 0, (0,), 0)
+        tensor += turns(0, 2) + sweep(0, 0, (1,), None, (0, 1)) + turns(0, 3) + sweep(0, 0, (1, 2), None, (2, 3)) + sweep(0, 0, (2,), None, (0, 1))
+        tensor += turns(1, 0) + sweep(0, 0, (3,), None, (0, 1)) + turns(1, 1) + sweep(0, 0, (3,), None, (2, 3))
+        tensor += turns(1, 2) + sweep(1, 0, (0,), 0, (0, 1)) + turns(1, 3) + sweep(1, 0, (0, 1), 0, (2, 3)) + sweep(1, 0, (1,), None, (0, 1))
+        tensor += sweep(0, 1, (0, 1), PACK, (0, 1, 2)) + sweep(0, 1, range(G), PACK, (3,)) + sweep(0, 1, (2, 3), None, (0, 1, 2)) + sweep(1, 0, (2, 3))
+        tensor += sweep(1, 1, range(G), PACK, (3, 0, 1, 2)) + sweep(2, 0, (0, 1), 0, (0, 1)) + sweep(2, 0, (2, 3), None, (0, 1)) + sweep(2, 0, range(G), 0, (2, 3)) + sweep(2, 1, range(G), PACK)
         for z in range(last - 1):
-            tensor += detect(z, range(C), 0, B, (first + second)[z])
-        tensor += detect(last - 1, range(C), 0, BH, second[2]) + detect(last - 1, range(C), BH, BH, first[1])
-        tensor += detect(last, (1, 2, 0), 0, BH, second[3]) + detect(last, (1, 2, 0), BH, BH, first[0])
+            tensor += detect(z, range(C), 0, B, z)
+        tensor += detect(last - 1, range(C), 0, BH, 6) + detect(last - 1, range(C), BH, BH, 7) + detect(last, range(C), 0, BH, 0) + detect(last, range(C), BH, BH, 1)
         sync += [store(z, 0, B) for z in range(last - 1)] + [store(z, b0, BH) for z in (last - 1, last) for b0 in (0, BH)]
 
         one = keep.tile([P, 1], F32, name="one")

@@ -229,8 +229,8 @@ def tile_tomography_forward_transmission_d3_kernel(tc, F, S_bytes, S_scale, i0, 
             wide, start = wide_of[c, g]
 
             def call():
-                src = tile_of(wide)[:, :, start : start + KP].rearrange("p j (a t e) -> p t a j e", t=PACK, e=PACK)
-                dst = grouped_of(("s", c, g)).rearrange("p (t a e j) -> p t a j e", t=PACK, e=PACK, j=PACK)
+                src = tile_of(wide)[:, :, start : start + KP].rearrange("p j (a t e) -> p a t j e", t=PACK, e=PACK)
+                dst = grouped_of(("s", c, g)).rearrange("p (t a e j) -> p a t j e", t=PACK, e=PACK, j=PACK)
                 nc.vector.tensor_copy(out=dst, in_=src)
 
             return (call, [("rows", c, g)], [grouped_value(("s", c, g)), wide])
@@ -324,7 +324,7 @@ def tile_tomography_forward_transmission_d3_kernel(tc, F, S_bytes, S_scale, i0, 
         def detect(z, groups, b0, w, bank=None):
             if bank is not None:
                 plan_bank(("y_sum", z, b0), bank)
-            return [mx_pass(("y_sum", z, b0), w, h_place[c, z], (("d", c), b0, w), c == groups[0], c == groups[-1]) for c in groups]
+            return [mx_pass(("y_sum", z, b0), w, h_place[c, z], (("d", c), b0, w), c == 0, c == C - 1) for c in groups]
 
         def y_copy(engine, z, b0, w):
             plan_ring(("y", z, b0), "y", [P, w], F32)
@@ -379,8 +379,8 @@ def tile_tomography_forward_transmission_d3_kernel(tc, F, S_bytes, S_scale, i0, 
         together((("f", 1, 2), ZH), (("f", 1, 3), ZH))
         for c, g in ((1, 2), (2, 0), (2, 2)):
             together((("s", c, g), KP), (("s", c, g + 1), KP))
-        together((("d", 0), B), (("d", 1), B))
         together((("d", 2), B))
+        together((("d", 0), B), (("d", 1), B))
         for z in range(2 * TILES):
             together((("h", 0, z), P), (("h", 1, z), 2 * P))
 
@@ -398,15 +398,15 @@ def tile_tomography_forward_transmission_d3_kernel(tc, F, S_bytes, S_scale, i0, 
         vector += weave([widen("v", 0, 3, 0), quantize("f", 0, 1), quantize("s", 0, 2), s_group(0, 3), quantize("f", 0, 2), quantize("s", 0, 3), widen("v", 1, 0, 0), quantize("f", 0, 3), widen("v", 2, 0, 0)], ln)
         vector += [s_group(1, 0)] + rows("v", 1, 1, range(PACK)) + [quantize("s", 1, 0), s_group(1, 1), quantize("f", 1, 0), quantize("s", 1, 1)]
         vector += rows("v", 1, 2, (0, 1, 2)) + [widen("v", 1, 3, 0), widen("v", 2, 1, 0), quantize("f", 1, 2), s_group(1, 2), s_group(1, 3), widen("v", 2, 2, 0), quantize("s", 1, 2)]
-        vector += [s_group(2, 0), s_group(2, 1), widen("v", 2, 3, 0), quantize("s", 2, 0), s_group(2, 2)] + [d_sign(0, j) for j in range(PACK)]
-        vector += [s_group(2, 3), d_sign(1, 0), d_sign(1, 1), quantize("s", 2, 2), d_sign(1, 2), d_sign(1, 3)] + [d_sign(2, j) for j in (0, 1)] + [d_group(0)]
-        vector += [d_sign(2, j) for j in (2, 3)] + [quantize("d", 0), d_group(2), h_group("v", 1, 3, 0, 1), quantize("d", 2)]
-        for z in range(last):
+        vector += [s_group(2, 0), s_group(2, 1), widen("v", 2, 3, 0), quantize("s", 2, 0), s_group(2, 2)] + [d_sign(2, j) for j in range(PACK)]
+        vector += [s_group(2, 3), d_sign(0, 0), d_sign(0, 1), quantize("s", 2, 2), d_group(2), d_sign(0, 2), d_sign(0, 3)] + [d_sign(1, j) for j in range(PACK)]
+        vector += [quantize("d", 2), d_group(0), h_group("v", 1, 3, 0, 1), quantize("d", 0)]
+        for z in range(last - 1):
             vector += [h_group("v", 1, 3, z + 1, 1), quantize("h", 0, z)]
-        vector += [quantize("h", 0, last), y_copy("v", 6, BH, BH), y_copy("v", last, BH, BH)]
+        vector += [quantize("h", 0, last - 1), h_group("v", 1, 3, last, 1), quantize("h", 0, last), y_copy("v", 6, BH, BH), y_copy("v", last, BH, BH)]
 
         tensor = [warm_up("first", 3, 3)] + turns(0, 0) + [warm_up("second", 3, 3)] + turns(0, 1) + sweep(0, 0, (0,), 0)
-        tensor += turns(0, 2) + sweep(0, 0, (1,), None, (0, 1)) + turns(0, 3) + sweep(0, 0, (1, 2), None, (2, 3)) + sweep(0, 0, (2,), None, (0, 1))
+        tensor += turns(0, 2) + sweep(0, 0, (1,), None, (0, 1)) + turns(0, 3) + sweep(0, 0, (1,), None, (2, 3)) + sweep(0, 0, (2,), None, (3, 2, 0, 1))
         tensor += turns(1, 0) + sweep(0, 0, (3,), None, (0, 1)) + turns(1, 1) + sweep(0, 0, (3,), None, (2, 3))
         tensor += turns(1, 2) + sweep(1, 0, (0,), 0, (0, 1)) + turns(1, 3) + sweep(1, 0, (0, 1), 0, (2, 3)) + sweep(1, 0, (1,), None, (0, 1))
         tensor += sweep(0, 1, (0, 1), PACK, (0, 1, 2)) + sweep(0, 1, range(G), PACK, (3,)) + sweep(0, 1, (2, 3), None, (0, 1, 2)) + sweep(1, 0, (2, 3))

@@ -25,7 +25,7 @@ ZH = Z // 2
 ZQ = ZH // 2
 TILES = ZH // P
 BH = B // 2
-RUN = 4
+RUN = 8
 
 RING = {"f_raw": 3, "grouped": 5, "y": 10}
 

@@ -335,7 +335,7 @@ def tile_tomography_forward_transmission_d3_kernel(tc, F, S_bytes, S_scale, i0, 
 
         sync = [load_scales(0, 1), load_s(0, 0, 2, 0, 1), load_s(0, 2, 4, 0, 1), load_scales(1, G), load_s(1, 0, 4, 0, 1)]
         sync += [load_f(0, 0, 1), load_s(2, 0, 4, 0, 1), load_f(0, 1, 1)] + [load_i0(e) for e in range(PACK)] + [load_s(3, 0, 4, 0, 1), load_f(0, 2, 1), load_f(0, 3, 1)]
-        sync += [load_s(0, 0, 4, 1, C), load_f(1, 0, 2, "late0"), load_s(1, 0, 4, 1, C), load_f(1, 2, 2, "late1"), load_s(2, 0, 4, 1, C), load_s(3, 0, 4, 1, C)]
+        sync += [load_s(0, 0, 4, 1, 3), load_f(1, 0, 2, "late0"), load_s(1, 0, 4, 1, 2), load_f(1, 2, 2, "late1"), load_s(2, 0, 4, 1, 2), load_s(3, 0, 4, 1, 2), load_s(1, 0, 4, 2, 3), load_s(2, 0, 4, 2, 3), load_s(3, 0, 4, 2, 3)]
         sync += [load_d(c, e) for c in range(C) for e in range(PACK)]
         units = [(0, 0), (0, 1), (0, 2), (0, 3), (1, 0), (2, 0), (1, 1), (1, 2), (1, 3), (2, 1), (2, 2), (2, 3)]
         for unit, place in zip(units, ["wide0", "wide1", "wide2"] * 2 + ["wide0", "wide1", "late0", "wide0", "late1", "wide1"]):

import math
from contextlib import ExitStack

import concourse.mybir as mybir
from concourse.masks import make_identity

Z, V, R, B = 1024, 2048, 1536, 512
FLOPS = 2 * Z * V * R + 2 * Z * R * B

F32 = mybir.dt.float32
BF16 = mybir.dt.bfloat16
U32 = mybir.dt.uint32
U8 = mybir.dt.uint8
FP8 = mybir.dt.float8_e4m3fn
FP8X4 = mybir.dt.float8_e4m3fn_x4
ALU = mybir.AluOpType
ACT = mybir.ActivationFunctionType

P = 128
PACK = 4
KP = P * PACK
G = V // KP
C = R // KP
ZH = Z // 2
ZQ = ZH // 2
TILES = ZH // P
BH = B // 2
RUN = 8

RING = {"f_raw": 3, "grouped": 5, "y": 10}

GUESS_SHIFT = 0.043
GUESS_SLOPE = math.log(2.0) / 2.0**23
GUESS_START = (GUESS_SHIFT - 127.0) * math.log(2.0)
REACH = 0.031
LOG_IN_D = [0.0, 1.0 - REACH**4 / 16.0, -0.5, 1.0 / 3.0 + REACH**2 / 4.0, -0.25]
LOG_IN_R = [sum(LOG_IN_D[n] * math.factorial(n) / (math.factorial(k) * math.factorial(n - k)) * (-1.0) ** (n - k) for n in range(k, 5)) for k in range(5)]


def tile_tomography_forward_transmission_d3_kernel(tc, F, S_bytes, S_scale, i0, D, out):
    nc = tc.nc
    with ExitStack() as ctx:
        keep = ctx.enter_context(tc.tile_pool(name="keep", bufs=1))
        psum = ctx.enter_context(tc.psum_pool(name="psum", bufs=1))
        ctx.enter_context(tc.manual_schedule())

        tiles, plans, tenants, taken = {}, {}, {}, {}

        def plan(value, pool, place, shape, dtype):
            if value not in plans:
                plans[value] = (pool, place, shape, dtype)
                tenants.setdefault(place, []).append(value)

        def plan_ring(value, ring, shape, dtype):
            if value not in plans:
                taken[ring] = taken.get(ring, 0) + 1
                plan(value, keep, "%s%d" % (ring, (taken[ring] - 1) % RING[ring]), shape, dtype)

        def plan_kept(value, shape, dtype):
            plan(value, keep, "_".join(str(x) for x in value), shape, dtype)

        def plan_bank(value, bank):
            plan(value, psum, "bank%d" % bank, [P, KP], F32)

        def tile_of(value):
            if value not in tiles:
                pool, place, shape, dtype = plans[value]
                if pool is psum:
                    tiles[value] = pool.tile(shape, dtype, name=place)
                else:
                    tiles[value] = pool.tile(shape, dtype, name=place, align_bytes=64)
            return tiles[value]

        def copy_on(engine, dst, src):
            if engine == "v":
                nc.vector.tensor_copy(out=dst, in_=src)
            else:
                nc.scalar.copy(out=dst, in_=src)

        scale_view = S_scale.rearrange("(g p j) o -> p g (j o)", p=P, j=PACK)
        i0_view = i0.rearrange("(c a r) -> a c r", c=C, r=PACK * PACK)
        s_view = S_bytes.rearrange("(g p j) n -> g p j n", p=P, j=PACK)
        d_view = D.rearrange("(c a j e) b -> c e a j b", c=C, j=PACK, e=PACK)
        row_of, scale_of, f_of = {}, {}, {}

        def load_scales(g0, g1):
            value = ("scale", g0)
            plan_kept(value, [P, g1 - g0, PACK], F32)
            for g in range(g0, g1):
                scale_of[g] = (value, g - g0)
            return (lambda: nc.sync.dma_start(out=tile_of(value)[:], in_=scale_view[:, g0:g1, :]), [], [value])

        def load_s(g, j0, j1, c0, c1):
            value = ("s_bytes", g, j0, c0)
            plan_kept(value, [P, j1 - j0, KP * (c1 - c0)], U8)
            for c in range(c0, c1):
                for j in range(j0, j1):
                    row_of[c, g, j] = (value, j - j0, KP * (c - c0))
            return (lambda: nc.sync.dma_start(out=tile_of(value)[:], in_=s_view[g][:, j0:j1, KP * c0 : KP * c1]), [], [value])

        def load_f(h, g0, n, place=None):
            value = ("f_raw", h, g0)
            if place is None:
                plan_ring(value, "f_raw", [P, TILES, n * KP], BF16)
            else:
                plan(value, keep, place, [P, TILES, n * KP], BF16)
            for g in range(g0, g0 + n):
                f_of[h, g] = (value, KP * (g - g0))
            view = F.rearrange("(h z p) k -> h p z k", p=P, z=TILES)[h][:, :, KP * g0 : KP * (g0 + n)]
            return (lambda: nc.sync.dma_start(out=tile_of(value)[:], in_=view), [], [value])

        def load_i0(e):
            span = PACK * (PACK - 1) + 1
            plan_kept(("i0",), [P, C, PACK * PACK], BF16)
            return (lambda: nc.sync.dma_start(out=tile_of(("i0",))[e:P:PACK, :, 0:span], in_=i0_view[:, :, e : e + span]), [], [("i0",)])

        def d_rows(c):
            plan_kept(("d_raw", c // 2), [P, PACK, (2 - c // 2) * B], BF16)
            return tile_of(("d_raw", c // 2))[:, :, B * (c % 2) : B * (c % 2 + 1)]

        def load_d(c, e):
            return (lambda: nc.sync.dma_start(out=d_rows(c)[e:P:PACK, :, :], in_=d_view[c, e]), [], [("d_rows", c)])

        ident = keep.tile([P, P], F32, name="ident")

        def small(name):
            plan_kept((name,), [P, C * PACK], F32)
            return tile_of((name,))[:]

        def i0_flat():
            return tile_of(("i0",))[:].rearrange("p c r -> p (c r)")[:, 0 : C * PACK * PACK : PACK]

        def horner(name, before, coefficient, other, op):
            call = lambda: nc.vector.scalar_tensor_tensor(out=small(name), in0=small(before), scalar=coefficient, in1=small(other), op0=ALU.add, op1=op)
            return (call, [(before,), (other,)], [(name,)])

        def product(name, a, b, op):
            return (lambda: nc.vector.tensor_tensor(out=small(name), in0=small(a), in1=small(b), op=op), [(a,), (b,)], [(name,)])

        def with_number(name, a, number, op):
            return (lambda: nc.vector.tensor_scalar(out=small(name), in0=small(a), scalar1=number, scalar2=None, op0=op), [(a,)], [(name,)])

        ln_scalar = [
            (lambda: nc.scalar.activation(out=small("mag"), in_=i0_flat(), func=ACT.Abs), [("i0",)], [("mag",)]),
            (lambda: nc.scalar.activation(out=small("sgn"), in_=i0_flat(), func=ACT.Sign), [("i0",)], [("sgn",)]),
            (
                lambda: nc.scalar.activation(out=small("guess"), in_=small("mag").bitcast(U32), func=ACT.Identity, scale=GUESS_SLOPE, bias=GUESS_START),
                [("mag",)],
                [("guess",)],
            ),
            (lambda: nc.scalar.activation(out=small("half_inv"), in_=small("guess"), func=ACT.Exp, scale=-0.5), [("guess",)], [("half_inv",)]),
        ]
        ln_vector = [
            product("root", "mag", "half_inv", ALU.mult),
            product("ratio", "root", "half_inv", ALU.mult),
            with_number("power4", "ratio", LOG_IN_R[4], ALU.mult),
            horner("power3", "power4", LOG_IN_R[3], "ratio", ALU.mult),
            horner("power2", "power3", LOG_IN_R[2], "ratio", ALU.mult),
            horner("power1", "power2", LOG_IN_R[1], "ratio", ALU.mult),
            horner("ln_i0", "power1", LOG_IN_R[0], "guess", ALU.add),
        ]

        batch_of = {}

        def together(*parts):
            start = 0
            for key, width in parts:
                batch_of[key] = (parts[0][0], start, width)
                start = start + width
            plan_ring(("grouped",) + parts[0][0], "grouped", [P, PACK * start], BF16)

        def grouped_value(key):
            return ("grouped",) + batch_of[key][0]

        def grouped_of(key):
            batch, start, width = batch_of[key]
            return tile_of(("grouped",) + batch)[:, PACK * start : PACK * (start + width)]

        def quantize(*key):
            width = plans[("grouped",) + key][2][1] // PACK
            plan_kept(("codes",) + key, [P, width], U32)
            plan_kept(("scales",) + key, [P, width], U8)
            call = lambda: nc.vector.quantize_mx(
                out=tile_of(("codes",) + key)[:].bitcast(FP8X4), scales=tile_of(("scales",) + key)[:], in_=tile_of(("grouped",) + key)[:]
            )
            return (call, [("grouped",) + key], [("codes",) + key, ("scales",) + key])

        def operand(key, start, width):
            batch, first, whole = batch_of[key]
            columns = slice(first + start, first + start + width)
            return tile_of(("codes",) + batch)[:, columns].bitcast(FP8X4), tile_of(("scales",) + batch)[:, columns]

        def mx_pass(bank_value, columns, lhs, rhs, first, last):
            def call():
                lhsT, lhsT_scale = operand(*lhs)
                moving, moving_scale = operand(*rhs)
                nc.tensor.matmul_mx(
                    out=tile_of(bank_value)[:, 0:columns], lhsT=lhsT, lhsT_scale=lhsT_scale, rhs=moving, rhs_scale=moving_scale, start=first, stop=last
                )

            return (call, [("codes",) + batch_of[lhs[0]][0], ("codes",) + batch_of[rhs[0]][0]], [bank_value])

        wide_of = {}

        def plan_wide(place, *units):
            value = ("wide",) + units[0]
            plan(value, keep, place, [P, PACK, len(units) * KP], BF16)
            for n, unit in enumerate(units):
                wide_of[unit] = (value, KP * n)

        def widen(engine, c, g, j, groups=1):
            row, row_index, column = row_of[c, g, j]
            scale_value, scale_index = scale_of[g]
            wide, start = wide_of[c, g]
            w = groups * KP

            def call():
                src = tile_of(row)[:, row_index, column : column + w].bitcast(FP8)
                dst = tile_of(wide)[:, j, start : start + w]
                scale = tile_of(scale_value)[:, scale_index, j : j + 1]
                if engine == "v":
                    nc.vector.tensor_scalar(out=dst, in0=src, scalar1=scale, scalar2=None, op0=ALU.mult)
                else:
                    nc.scalar.activation(out=dst, in_=src, func=ACT.Copy, scale=scale)

            return (call, [row, scale_value], [wide] + [("rows", c + n, g) for n in range(groups)])

        def s_group(c, g):
            wide, start = wide_of[c, g]

            def call():
                src = tile_of(wide)[:, :, start : start + KP].rearrange("p j (a t e) -> p a t j e", t=PACK, e=PACK)
                dst = grouped_of(("s", c, g)).rearrange("p (t a e j) -> p a t j e", t=PACK, e=PACK, j=PACK)
                nc.vector.tensor_copy(out=dst, in_=src)

            return (call, [("rows", c, g)], [grouped_value(("s", c, g)), wide])

        def turn(h, g, b, bank):
            value = ("turned", h, g, b)
            plan_bank(value, bank)
            raw, column = f_of[h, g]

            def call():
                for z in range(2):
                    words = tile_of(raw)[:, 2 * b + z, column : column + KP].bitcast(F32)
                    for u in range(2):
                        start = (2 * z + u) * P
                        nc.tensor.transpose(tile_of(value)[:, start : start + P], words[:, u : 2 * P : 2], ident[:])

            return (call, [raw], [value])

        def f_copy(engine, h, g, b):
            def call():
                dst = grouped_of(("f", h, g)).bitcast(F32)[:, KP * b : KP * (b + 1)]
                src = tile_of(("turned", h, g, b))[:]
                copy_on(engine, dst.rearrange("p (z r u) -> p z r u", z=2, u=2), src.rearrange("p (z u r) -> p z r u", z=2, u=2))

            return (call, [("turned", h, g, b)], [grouped_value(("f", h, g))])

        def warm_up(name, count, bank):
            value = ("unread", name)
            plan_bank(value, bank)
            wide, start = wide_of[0, 0]

            def call():
                row = tile_of(wide)[:, 1, 0:KP]
                for n in range(count):
                    nc.tensor.matmul(out=tile_of(value)[:], lhsT=row[:, 0:P], rhs=row, start=True, stop=True)

            return (call, [("rows", 0, 0)], [value, wide])

        h_place = {}

        def project(c, h, t, passes, bank=None):
            if bank is not None:
                plan_bank(("p", c, h, t), bank)
            return [mx_pass(("p", c, h, t), ZH, (("s", c, g), P * t, P), (("f", h, g), 0, ZH), g == 0, g == G - 1) for g in passes]

        h_tiles = {(c0, h): keep.tile([P, PACK, n, ZH], BF16, name="h_rows%d_%d" % (c0, h), align_bytes=64) for c0, n in ((0, 1), (1, 2)) for h in range(2)}

        def attenuate(c, h, t):
            def call():
                nc.scalar.activation(
                    out=h_tiles[min(c, 1), h][:, t, c - min(c, 1), :],
                    in_=tile_of(("p", c, h, t))[:],
                    func=ACT.Exp,
                    bias=small("ln_i0")[:, PACK * c + t : PACK * c + t + 1],
                    scale=-1.0,
                )

            return (call, [("p", c, h, t), ("ln_i0",)], [("h_rows", c, h)])

        def h_group(engine, c0, c1, z0, n):
            w = n * P
            for c in range(c0, c1):
                for z in range(z0, z0 + n):
                    h_place[c, z] = (("h", c0, z0), w * (c - c0) + P * (z - z0), P)
            h, z1 = divmod(z0 * P, ZH)
            first = c0 - min(c0, 1)

            def call():
                rows = h_tiles[min(c0, 1), h][:, :, first : first + c1 - c0, z1 : z1 + w]
                dst = grouped_of(("h", c0, z0)).rearrange("p (c q i j) -> p c q j i", c=c1 - c0, i=RUN, j=PACK)
                copy_on(engine, dst, rows.rearrange("p j c (q i) -> p c q j i", i=RUN))

            return (call, [("h_rows", c, h) for c in range(c0, c1)], [grouped_value(("h", c0, z0))])

        def d_sign(c, j):
            def call():
                row = d_rows(c)[:, j, :]
                nc.vector.tensor_scalar(out=row, in0=row, scalar1=small("sgn")[:, PACK * c + j : PACK * c + j + 1], scalar2=None, op0=ALU.mult)

            return (call, [("d_rows", c), ("sgn",)], [("d_signed", c // 2)])

        def d_group(c):
            value = grouped_value(("d", c))

            def call():
                dst = tile_of(value)[:].rearrange("p (q i j) -> p q j i", i=RUN, j=PACK)
                nc.vector.tensor_copy(out=dst, in_=tile_of(("d_raw", c // 2))[:].rearrange("p j (q i) -> p q j i", i=RUN))

            return (call, [("d_signed", c // 2)], [value])

        def detect(z, groups, b0, w, bank=None):
            if bank is not None:
                plan_bank(("y_sum", z, b0), bank)
            return [mx_pass(("y_sum", z, b0), w, h_place[c, z], (("d", c), b0, w), c == 0, c == C - 1) for c in groups]

        def y_copy(engine, z, b0, w):
            plan_ring(("y", z, b0), "y", [P, w], F32)
            return (lambda: copy_on(engine, tile_of(("y", z, b0))[:], tile_of(("y_sum", z, b0))[:, 0:w]), [("y_sum", z, b0)], [("y", z, b0)])

        def store(z, b0, w):
            return (lambda: nc.sync.dma_start(out=out[P * z : P * (z + 1), b0 : b0 + w], in_=tile_of(("y", z, b0))[:]), [("y", z, b0)], [])

        sync = [load_scales(0, 1), load_s(0, 0, 2, 0, 1), load_s(0, 2, 4, 0, 1), load_scales(1, G), load_s(1, 0, 4, 0, 1)]
        sync += [load_f(0, 0, 1), load_s(2, 0, 4, 0, 1), load_f(0, 1, 1)] + [load_i0(e) for e in range(PACK)] + [load_s(3, 0, 4, 0, 1), load_f(0, 2, 1), load_f(0, 3, 1)]
        sync += [load_s(0, 0, 4, 1, 3), load_f(1, 0, 2, "late0"), load_s(1, 0, 4, 1, 2), load_f(1, 2, 2, "late1"), load_s(2, 0, 4, 1, 2), load_s(3, 0, 4, 1, 2), load_s(1, 0, 4, 2, 3), load_s(2, 0, 4, 2, 3), load_s(3, 0, 4, 2, 3)]
        sync += [load_d(c, e) for c in range(C) for e in range(PACK)]
        units = [(0, 0), (0, 1), (0, 2), (0, 3), (1, 0), (2, 0), (1, 1), (1, 2), (1, 3), (2, 1), (2, 2), (2, 3)]
        for unit, place in zip(units, ["wide0", "wide1", "wide2"] * 2 + ["wide0", "wide1", "late0", "wide0", "late1", "wide1"]):
            plan_wide(place, unit)
        for z in range(2 * TILES - 2):
            plan_ring(("y", z, 0), "y", [P, B], F32)
        for z in (2 * TILES - 2, 2 * TILES - 1):
            for b0 in (0, BH):
                plan_ring(("y", z, b0), "y", [P, BH], F32)

        def rows(engine, c, g, js):
            return [widen(engine, c, g, j) for j in js]

        def empty(h, g):
            return [f_copy("s", h, g, b) for b in range(2)]

        def exps(c, h, ts=range(PACK)):
            return [attenuate(c, h, t) for t in ts]

        def weave(a, b):
            steps = []
            for n in range(max(len(a), len(b))):
                steps += a[n : n + 1] + b[n : n + 1]
            return steps

        def turns(h, g):
            return [turn(h, g, b, PACK + 2 * (g % 2) + b) for b in range(2)]

        def sweep(c, h, passes, first_bank=None, slices=range(PACK)):
            steps = []
            for t in slices:
                steps += project(c, h, t, passes, None if first_bank is None else first_bank + t)
            return steps

        last = 2 * TILES - 1

        for key in [("s", 0, 0), ("f", 0, 0), ("s", 0, 1), ("f", 0, 1), ("s", 0, 2), ("f", 0, 2), ("s", 0, 3), ("f", 0, 3), ("s", 1, 0)]:
            together((key, KP))
        together((("s", 1, 1), KP))
        together((("f", 1, 0), ZH), (("f", 1, 1), ZH))
        together((("f", 1, 2), ZH), (("f", 1, 3), ZH))
        for c, g in ((1, 2), (2, 0), (2, 2)):
            together((("s", c, g), KP), (("s", c, g + 1), KP))
        together((("d", 2), B))
        together((("d", 0), B), (("d", 1), B))
        for z in range(2 * TILES):
            together((("h", 0, z), P), (("h", 1, z), 2 * P))

        scalar = rows("s", 0, 0, (1,)) + rows("s", 0, 1, (1, 2, 3)) + empty(0, 0) + rows("s", 0, 2, (2, 3))
        scalar += ln_scalar[0:2] + weave(empty(0, 1), ln_scalar[2:4]) + rows("s", 0, 3, (1, 2, 3)) + empty(0, 2) + rows("s", 1, 0, (1,)) + empty(0, 3)
        scalar += rows("s", 1, 0, (2,)) + rows("s", 1, 0, (3,)) + rows("s", 2, 0, (2, 3)) + empty(1, 0) + exps(0, 0, (0, 1)) + empty(1, 1) + exps(0, 0, (2,)) + empty(1, 2) + exps(0, 0, (3,)) + empty(1, 3) + rows("s", 1, 2, (3,))
        scalar += rows("s", 1, 3, (1, 2, 3)) + rows("s", 2, 0, (1,)) + rows("s", 2, 1, (1, 2, 3)) + exps(0, 1, (3, 0)) + rows("s", 2, 2, (1, 2, 3)) + exps(0, 1, (1, 2)) + rows("s", 2, 3, (1, 2, 3))
        scalar += exps(1, 0) + exps(1, 1, (3, 0, 1, 2)) + exps(2, 0, (0, 1)) + [h_group("s", 0, 1, 0, 1)] + exps(2, 0, (2, 3)) + weave([h_group("s", 0, 1, z, 1) for z in (1, 2, 3)], exps(2, 1, (0, 1, 2)))
        scalar += [h_group("s", 0, 1, 4, 1), attenuate(2, 1, 3), y_copy("s", 0, 0, B), h_group("s", 0, 1, 5, 1), y_copy("s", 1, 0, B), h_group("s", 0, 1, 6, 1), y_copy("s", 2, 0, B)]
        scalar += [h_group("s", 0, 1, 7, 1), y_copy("s", 3, 0, B), y_copy("s", 4, 0, B), y_copy("s", 5, 0, B), y_copy("s", 6, 0, BH), y_copy("s", last, 0, BH)]

        ln = ln_vector
        vector = rows("v", 0, 0, (0, 2, 3)) + [s_group(0, 0), widen("v", 0, 1, 0), quantize("s", 0, 0), s_group(0, 1)]
        vector += rows("v", 0, 2, (0, 1)) + [quantize("f", 0, 0), quantize("s", 0, 1), s_group(0, 2)]
        vector += weave([widen("v", 0, 3, 0), quantize("f", 0, 1), quantize("s", 0, 2), s_group(0, 3), quantize("f", 0, 2), quantize("s", 0, 3), widen("v", 1, 0, 0), quantize("f", 0, 3), widen("v", 2, 0, 0)], ln)
        vector += [s_group(1, 0)] + rows("v", 1, 1, range(PACK)) + [quantize("s", 1, 0), s_group(1, 1), quantize("f", 1, 0), quantize("s", 1, 1)]
        vector += rows("v", 1, 2, (0, 1, 2)) + [widen("v", 1, 3, 0), widen("v", 2, 1, 0), quantize("f", 1, 2), s_group(1, 2), s_group(1, 3), widen("v", 2, 2, 0), quantize("s", 1, 2)]
        vector += [s_group(2, 0), s_group(2, 1), widen("v", 2, 3, 0), quantize("s", 2, 0), s_group(2, 2)] + [d_sign(2, j) for j in range(PACK)]
        vector += [s_group(2, 3), d_sign(0, 0), d_sign(0, 1), quantize("s", 2, 2), d_group(2), d_sign(0, 2), d_sign(0, 3)] + [d_sign(1, j) for j in range(PACK)]
        vector += [quantize("d", 2), d_group(0), h_group("v", 1, 3, 0, 1), quantize("d", 0)]
        for z in range(last - 1):
            vector += [h_group("v", 1, 3, z + 1, 1), quantize("h", 0, z)]
        vector += [quantize("h", 0, last - 1), h_group("v", 1, 3, last, 1), quantize("h", 0, last), y_copy("v", 6, BH, BH), y_copy("v", last, BH, BH)]

        tensor = [warm_up("first", 3, 3)] + turns(0, 0) + [warm_up("second", 3, 3)] + turns(0, 1) + sweep(0, 0, (0,), 0)
        tensor += turns(0, 2) + sweep(0, 0, (1,), None, (0, 1)) + turns(0, 3) + sweep(0, 0, (1,), None, (2, 3)) + sweep(0, 0, (2,), None, (3, 2, 0, 1))
        tensor += turns(1, 0) + sweep(0, 0, (3,), None, (0, 1)) + turns(1, 1) + sweep(0, 0, (3,), None, (2, 3))
        tensor += turns(1, 2) + sweep(1, 0, (0,), 0, (0, 1)) + turns(1, 3) + sweep(1, 0, (0, 1), 0, (2, 3)) + sweep(1, 0, (1,), None, (0, 1))
        tensor += sweep(0, 1, (0, 1), PACK, (0, 1, 2)) + sweep(0, 1, range(G), PACK, (3,)) + sweep(0, 1, (2, 3), None, (0, 1, 2)) + sweep(1, 0, (2, 3))
        tensor += sweep(1, 1, range(G), PACK, (3, 0, 1, 2)) + sweep(2, 0, (0, 1), 0, (0, 1)) + sweep(2, 0, (2, 3), None, (0, 1)) + sweep(2, 0, range(G), 0, (2, 3)) + sweep(2, 1, range(G), PACK)
        for z in range(last - 1):
            tensor += detect(z, range(C), 0, B, z)
        tensor += detect(last - 1, range(C), 0, BH, 6) + detect(last - 1, range(C), BH, BH, 7) + detect(last, range(C), 0, BH, 0) + detect(last, range(C), BH, BH, 1)
        sync += [store(z, 0, B) for z in range(last - 1)] + [store(z, b0, BH) for z in (last - 1, last) for b0 in (0, BH)]

        one = keep.tile([P, 1], F32, name="one")
        unread = keep.tile([P, 1], F32, name="unread")
        nc.vector.memset(one[:], 1.0)
        nc.scalar.activation(out=unread[:], in_=one[:], func=ACT.Exp)
        make_identity(nc, ident[:])

        lists = [sync, tensor, vector, scalar]
        unwritten, unread_by = {}, {}
        for steps in lists:
            for call, reads, writes in steps:
                for value in reads:
                    unread_by[value] = unread_by.get(value, 0) + 1
                for value in writes:
                    unwritten[value] = unwritten.get(value, 0) + 1

        def place_is_free(value):
            if value not in plans:
                return True
            queue = tenants[plans[value][1]]
            return all(unwritten[v] == 0 and unread_by.get(v, 0) == 0 for v in queue[: queue.index(value)])

        position = [0] * len(lists)
        for turn_of_the_loop in range(sum(len(steps) for steps in lists)):
            for n, steps in enumerate(lists):
                if position[n] < len(steps):
                    call, reads, writes = steps[position[n]]
                    if all(unwritten[v] == 0 for v in reads) and all(place_is_free(v) for v in writes):
                        call()
                        for value in reads:
                            unread_by[value] = unread_by[value] - 1
                        for value in writes:
                            unwritten[value] = unwritten[value] - 1
                        position[n] = position[n] + 1
        assert position == [len(steps) for steps in lists], position
